import numpy as np
import ml_dtypes


def mxq(x, axis, fmt="e4m3"):
    dtype, down = {"e4m3": (ml_dtypes.float8_e4m3fn, 7), "e5m2": (ml_dtypes.float8_e5m2, 14)}[fmt]
    v = np.moveaxis(np.asarray(x, np.float32).astype(ml_dtypes.bfloat16).astype(np.float64), axis, -1)
    blocks = v.reshape(v.shape[:-1] + (-1, 32))
    amax = np.abs(blocks).max(-1, keepdims=True)
    byte = np.maximum(np.where(amax > 0, np.frexp(amax)[1] - 1 + 127, 0) - down, 1)
    scale = np.exp2(byte - 127.0)
    codes = (blocks / scale).astype(np.float32).astype(dtype).astype(np.float64)
    return np.moveaxis((codes * scale).reshape(v.shape), -1, axis)


WIDE = False


def mx_kscale(k):
    if not WIDE:
        return np.ones(k)
    levels = np.array([10, -10, 5, -5, 0])
    if k % 512:
        return np.exp2(np.random.permutation(np.resize(levels, k // 32))).repeat(32)
    a = np.empty((k // 512, 16))
    for p in range(k // 512):
        a[p, :8] = np.random.permutation(np.resize(levels, 8))
        for g in range(8):
            far = levels[np.abs(levels - a[p, g]) >= 10]
            a[p, g + 8] = far[np.random.randint(len(far))]
    return np.exp2(a.ravel()).repeat(32)


BF16 = ml_dtypes.bfloat16


def bf(x):
    return np.asarray(x, np.float32).astype(BF16)


def f64(x):
    return np.asarray(x).astype(np.float64)


E2M1 = np.array([0.0, 0.5, 1.0, 1.5, 2.0, 3.0, 4.0, 6.0, -0.0, -0.5, -1.0, -1.5, -2.0, -3.0, -4.0, -6.0])


def pack_weight(w, fmt):
    k, n = w.shape
    w = f64(bf(w)).reshape(k // 32, 32, n)
    amax = np.abs(w).max(1)
    if fmt == "e4m3":
        byte = np.frexp(amax)[1] - 1 + 127 - 7
    else:
        mant, ex = np.frexp(amax / 6.0)
        byte = np.where(mant > 0.5, ex, ex - 1) + 127
    byte = np.clip(np.where(amax > 0, byte, 1), 1, 254)
    scaled = (w * np.exp2(127.0 - byte)[:, None, :]).reshape(k, n).astype(np.float32)
    by_word = np.ascontiguousarray(scaled.reshape(k // 512, 128, 4, n).transpose(0, 1, 3, 2))
    if fmt == "e4m3":
        words = by_word.astype(ml_dtypes.float8_e4m3fn).view(np.uint8)
    else:
        c = by_word.astype(ml_dtypes.float4_e2m1fn).view(np.uint8) & 0xF
        words = c[..., 0::2] | (c[..., 1::2] << 4)
    return np.ascontiguousarray(words), np.ascontiguousarray(byte.astype(np.uint8).reshape(k // 512, 16, n))


def unpack_weight(words, scales, fmt):
    g, p, n, _ = words.shape
    if fmt == "e4m3":
        vals = np.ascontiguousarray(words).view(ml_dtypes.float8_e4m3fn).astype(np.float64)
    else:
        nib = np.empty((g, p, n, 4), np.uint8)
        nib[..., 0::2] = words & 0xF
        nib[..., 1::2] = words >> 4
        vals = E2M1[nib]
    vals = vals * np.repeat(np.exp2(scales.astype(np.float64) - 127.0), 8, axis=1)[..., None]
    return vals.transpose(0, 1, 3, 2).reshape(g * 512, n)
def pack4(w):
    words, scales = pack_weight(w, "e2m1")
    return words.reshape(words.shape[0], 128, -1), scales


def unpack4(words, scales):
    return unpack_weight(words.reshape(words.shape[0], 128, -1, 2), scales, "e2m1")


T, A, N, R, Q = 2048, 1536, 1024, 512, 256


def draw0():
    s = mx_kscale(A)
    t = mx_kscale(N)
    u = mx_kscale(T)
    sens = np.random.standard_normal((N, R)) / np.sqrt(N) / t[:, None]
    sens_words, sens_scales = pack4(sens)
    return {"flow": bf(np.random.standard_normal((T, A)) * s),
            "impact": bf(np.random.standard_normal((A, N)) / np.sqrt(A) / s[:, None]),
            "vol": bf((1 + 0.2 * np.random.standard_normal(N)) * t),
            "depth": bf((1 + 0.2 * np.random.standard_normal(T)) * u),
            "sched": bf(np.random.standard_normal((Q, T)) / np.sqrt(T) / u),
            "sens_words": sens_words,
            "sens_scales": sens_scales}


def core(flow, impact, vol, depth, sched, sens_words, sens_scales):
    z = mxq(f64(flow), 1, "e4m3") @ mxq(f64(impact), 0, "e4m3")
    h = np.tanh(z)
    moves = h * f64(vol)
    hedge = mxq(moves, 1, "e4m3") @ unpack4(sens_words, sens_scales)
    weighted = h * f64(depth)[:, None]
    cost = mxq(f64(sched), 1, "e4m3") @ mxq(weighted, 0, "e4m3")
    return hedge, cost


def e4m3fn_bytes(y):
    return np.clip(np.asarray(y, np.float64), -448.0, 448.0).astype(np.float32).astype(ml_dtypes.float8_e4m3fn).view(np.uint8)


def e4m3fn_values(b):
    return np.asarray(b, np.uint8).view(ml_dtypes.float8_e4m3fn).astype(np.float64)


def setup_inputs():
    d = draw0()
    x0 = np.asarray(d['flow']).astype(np.float64)
    s = (np.max(np.abs(x0), axis=(0,), keepdims=True) / 448.0).astype(np.float32)
    out = {}
    for k, v in d.items():
        if k == 'flow':
            out['flow_bytes'] = e4m3fn_bytes(x0 / s.astype(np.float64))
            out['flow_scale'] = s
        else:
            out[k] = v
    return out


def reference(flow_bytes, flow_scale, impact, vol, depth, sched, sens_words, sens_scales):
    return core(e4m3fn_values(flow_bytes) * flow_scale.astype(np.float64), impact, vol, depth, sched, sens_words, sens_scales)

@@ -1,0 +1,497 @@
+from contextlib import ExitStack
+
+import concourse.mybir as mybir
+from concourse.masks import make_identity
+
+T, A, N, R, Q = 2048, 1536, 1024, 512, 256
+
+F32 = mybir.dt.float32
+BF16 = mybir.dt.bfloat16
+U8 = mybir.dt.uint8
+U32 = mybir.dt.uint32
+I32 = mybir.dt.int32
+FP8 = mybir.dt.float8_e4m3fn
+FP8X4 = mybir.dt.float8_e4m3fn_x4
+FP4X4 = mybir.dt.float4_e2m1fn_x4
+MULT = mybir.AluOpType.mult
+TANH = mybir.ActivationFunctionType.Tanh
+COPY = mybir.ActivationFunctionType.Copy
+
+FLOPS = 2 * T * A * N + 2 * T * N * R + 2 * Q * T * N
+
+P = 128
+PACK = 4
+K_PASS = P * PACK
+A_PASSES = A // K_PASS
+N_PASSES = N // K_PASS
+T_PASSES = T // K_PASS
+TILES = T // P
+BANK = 512
+W_LEAD = 4
+CH = 256
+CHUNKS = N // CH
+
+
+def tile_cross_impact_hedge_s8_kernel(
+    tc, flow_bytes, flow_scale, impact, vol, depth, sched, sens_words, sens_scales, hedge, cost
+):
+    nc = tc.nc
+    with ExitStack() as ctx:
+        keep = ctx.enter_context(tc.tile_pool(name="keep", bufs=1))
+        work = ctx.enter_context(tc.tile_pool(name="work", bufs=3))
+        psum = ctx.enter_context(tc.psum_pool(name="psum", bufs=2))
+        ctx.enter_context(tc.manual_schedule())
+
+        warm = keep.tile([P, 1], F32, name="warm")
+        nc.vector.memset(warm[:], 0.0)
+        nc.scalar.activation(out=warm[:], in_=warm[:], func=TANH)
+        scale_rows = keep.tile([P, 3 * P], F32, name="scale_rows")
+        nc.vector.memset(scale_rows[:], 0.0)
+        w_scales = keep.tile([P, N_PASSES, R], U8, name="w_scales", align_bytes=64)
+        nc.vector.memset(w_scales[:].bitcast(I32), 0)
+        ident = keep.tile([P, P], F32, name="ident")
+        make_identity(nc, ident[:])
+
+        flow_view = flow_bytes.rearrange("(g p j) a -> g p j a", p=P, j=PACK)
+        flow_sb = []
+        for g in range(T_PASSES):
+            for half in range(2):
+                t_f = keep.tile([P, 2, A], U8, name=f"flow_{g}_{half}", align_bytes=64)
+                flow_sb.append(t_f)
+
+        def load_flow(pair):
+            g, half = divmod(pair, 2)
+            nc.sync.dma_start(out=flow_sb[pair][:], in_=flow_view[g, :, 2 * half : 2 * half + 2, :])
+
+        imp_view = impact.rearrange("(c p t) n -> c p t n", p=P, t=PACK)
+        imp_raw = {}
+        for c in range(A_PASSES):
+            for half in range(N_PASSES):
+                t_i = keep.tile([P, PACK, BANK], BF16, name=f"imp_raw_{c}_{half}", align_bytes=64)
+                imp_raw[c, half] = t_i
+
+        def load_impact(c, half):
+            nc.sync.dma_start(out=imp_raw[c, half][:], in_=imp_view[c, :, :, half * BANK : (half + 1) * BANK])
+
+        scale_sb = keep.tile([P, A], F32, name="scale_sb", align_bytes=64)
+        vol_b = keep.tile([P, N_PASSES, PACK], BF16, name="vol_b")
+        depth_b = keep.tile([P, T_PASSES, PACK], BF16, name="depth_b")
+        w_words = keep.tile([P, N_PASSES, 2 * R], U8, name="w_words", align_bytes=64)
+        sched_sb = []
+        for qt in range(2):
+            t_s = keep.tile([P, T], BF16, name=f"sched_{qt}", align_bytes=64)
+            sched_sb.append(t_s)
+
+        nc.sync.dma_start(out=scale_rows[0:4, :], in_=flow_scale.rearrange("o (r k) -> (o r) k", r=4))
+        load_impact(0, 0)
+        load_impact(1, 0)
+        load_flow(0)
+        load_impact(2, 0)
+        load_impact(0, 1)
+        load_impact(1, 1)
+        load_impact(2, 1)
+        load_flow(1)
+        load_flow(2)
+        nc.sync.dma_start(out=vol_b[:], in_=vol.rearrange("(g p j) -> p g j", p=P, j=PACK))
+        nc.sync.dma_start(out=depth_b[:], in_=depth.rearrange("(g p j) -> p g j", p=P, j=PACK))
+        for q4 in range(4):
+            nc.sync.dma_start(
+                out=w_scales[32 * q4 : 32 * q4 + 4, :, :].bitcast(I32),
+                in_=sens_scales[:, 4 * q4 : 4 * q4 + 4, :].rearrange("g r n -> r g n").bitcast(I32),
+            )
+        nc.sync.dma_start(out=w_words[:].bitcast(I32), in_=sens_words.rearrange("g p b -> p g b").bitcast(I32))
+        load_flow(3)
+        load_flow(4)
+        for qt in range(2):
+            nc.sync.dma_start(out=sched_sb[qt][:], in_=sched[qt * P : (qt + 1) * P, :])
+        load_flow(5)
+        load_flow(6)
+        load_flow(7)
+
+        vol_f = keep.tile([P, N_PASSES, PACK], F32, name="vol_f")
+        depth_f = keep.tile([P, T_PASSES, PACK], F32, name="depth_f")
+
+        imp_codes = keep.tile([P, A_PASSES, N], U32, name="imp_codes", align_bytes=64)
+        imp_scales = keep.tile([P, A_PASSES, N], U8, name="imp_scales", align_bytes=64)
+        wt_codes = keep.tile([P, T_PASSES, N], U32, name="wt_codes", align_bytes=64)
+        wt_scales = keep.tile([P, T_PASSES, N], U8, name="wt_scales", align_bytes=64)
+        sch_codes = keep.tile([P, 2, T_PASSES, P], U32, name="sch_codes", align_bytes=64)
+        sch_scales = keep.tile([P, 2, T_PASSES, P], U8, name="sch_scales", align_bytes=64)
+        tiles = {}
+
+        def impact_interleave(c, half, engine):
+            grouped = work.tile([P, BANK, PACK], BF16, name=f"imp_grp_{c}_{half}", tag="imp_grp", bufs=3, align_bytes=64)
+            tiles["ig", c, half] = grouped
+            dst = grouped[:].rearrange("p (n i) t -> p n t i", i=4)
+            src = imp_raw[c, half][:].rearrange("p t (n i) -> p n t i", i=4)
+            if engine == "A":
+                nc.scalar.copy(out=dst, in_=src)
+            else:
+                nc.vector.tensor_copy(out=dst, in_=src)
+
+        def impact_quantize(c, half):
+            cols = slice(half * BANK, (half + 1) * BANK)
+            nc.vector.quantize_mx(
+                out=imp_codes[:, c, cols].bitcast(FP8X4),
+                scales=imp_scales[:, c, cols],
+                in_=tiles.pop(("ig", c, half))[:].rearrange("p n t -> p (n t)"),
+            )
+
+        def spread_scale():
+            bank = psum.tile([P, 3, P], F32, name="scale_cols", tag="ht", bufs=2)
+            for b in range(3):
+                nc.tensor.transpose(bank[:, b, :], scale_rows[:, b * P : (b + 1) * P], ident[:])
+            scale_cols = keep.tile([P, 4, 3], F32, name="scale_cols_sb")
+            nc.scalar.copy(out=scale_cols[:], in_=bank[:, :, 0:4].rearrange("p b r -> p r b"))
+            for c in range(A_PASSES):
+                bank = psum.tile([P, PACK, P], F32, name=f"scale_bank_{c}", tag="z", bufs=2)
+                for s in range(PACK):
+                    k = PACK * c + s
+                    nc.tensor.transpose(
+                        bank[:, s, :], scale_cols[:, k // 3, k % 3 : k % 3 + 1].to_broadcast([P, P]), ident[:]
+                    )
+                nc.scalar.copy(
+                    out=scale_sb[:, c * K_PASS : (c + 1) * K_PASS], in_=bank[:].rearrange("p s k -> p (s k)")
+                )
+
+        def widen(i):
+            wide = work.tile([P, A], BF16, name=f"wide_{i}", tag="wide", bufs=5, align_bytes=64)
+            tiles["wide", i] = wide
+            nc.vector.tensor_tensor(
+                out=wide[:], in0=flow_sb[i // 2][:, i % 2, :].bitcast(FP8), in1=scale_sb[:], op=MULT
+            )
+
+        def flow_transpose(i):
+            words = tiles.pop(("wide", i))[:].bitcast(F32)
+            for part, passes in ((0, (0, 1)), (1, (2,))):
+                bank = psum.tile([P, PACK, P], F32, name=f"xt_{i}_{part}", tag="xt", bufs=3)
+                tiles["xt", i, part] = bank
+                slot = 0
+                for c in passes:
+                    for u in range(2):
+                        nc.tensor.transpose(
+                            bank[:, slot, :], words[:, 256 * c + u : 256 * (c + 1) : 2], ident[:]
+                        )
+                        slot += 1
+
+        def flow_exit(i):
+            grouped = work.tile([P, A_PASSES, P, PACK], BF16, name=f"fg_{i}", tag="fg", bufs=3, align_bytes=64)
+            tiles["fg", i] = grouped
+            words = grouped[:].rearrange("p c r t -> p (c r t)").bitcast(F32)
+            words = words.rearrange("p (c r u) -> p c r u", c=A_PASSES, u=2)
+            xt0 = tiles.pop(("xt", i, 0))
+            xt1 = tiles.pop(("xt", i, 1))
+            nc.scalar.copy(out=words[:, 0:2, :, :], in_=xt0[:].rearrange("p (c u) r -> p c r u", u=2))
+            nc.scalar.copy(out=words[:, 2, :, :], in_=xt1[:, 0:2, :].rearrange("p u r -> p r u"))
+
+        def flow_quantize(i):
+            codes = work.tile([P, A_PASSES, P], U32, name=f"fc_{i}", tag="fc", bufs=4, align_bytes=64)
+            scales = work.tile([P, A_PASSES, P], U8, name=f"fs_{i}", tag="fs", bufs=4, align_bytes=64)
+            tiles["fc", i] = (codes, scales)
+            grouped = tiles.pop(("fg", i))
+            for lo, hi in ((0, 2), (2, 3)):
+                nc.vector.quantize_mx(
+                    out=codes[:, lo:hi, :].rearrange("p c r -> p (c r)").bitcast(FP8X4),
+                    scales=scales[:, lo:hi, :].rearrange("p c r -> p (c r)"),
+                    in_=grouped[:, lo:hi, :, :].rearrange("p c r t -> p (c r t)"),
+                )
+
+        def impact_matmul(i, half):
+            codes, scales = tiles["fc", i]
+            z = psum.tile([P, BANK], F32, name=f"z_{i}_{half}", tag="z", bufs=2)
+            tiles["z", i, half] = z
+            cols = slice(half * BANK, (half + 1) * BANK)
+            for c in range(A_PASSES):
+                nc.tensor.matmul_mx(
+                    out=z[:],
+                    lhsT=codes[:, c, :].bitcast(FP8X4),
+                    lhsT_scale=scales[:, c, :],
+                    rhs=imp_codes[:, c, cols].bitcast(FP8X4),
+                    rhs_scale=imp_scales[:, c, cols],
+                    start=(c == 0),
+                    stop=(c == A_PASSES - 1),
+                )
+
+        def saturate(i, half):
+            if half == 0:
+                h = work.tile([P, N], F32, name=f"h_{i}", tag="h", bufs=4, align_bytes=64)
+                tiles["h", i] = h
+            nc.scalar.activation(
+                out=tiles["h", i][:, half * BANK : (half + 1) * BANK].rearrange("p (j m) -> p j m", j=PACK),
+                in_=tiles.pop(("z", i, half))[:].rearrange("p (m j) -> p j m", j=PACK),
+                func=TANH,
+            )
+
+        def weigh(i, engine, lo=0, hi=N):
+            g, j = divmod(i, PACK)
+            if j == 0:
+                planes = work.tile([P, PACK, N], BF16, name=f"wp_{g}", tag="wp", bufs=3, align_bytes=64)
+                tiles["wp", g] = planes
+            planes = tiles["wp", g]
+            if engine == "A":
+                nc.scalar.activation(
+                    out=planes[:, j, lo:hi], in_=tiles["h", i][:, lo:hi], func=COPY, scale=depth_f[:, g, j : j + 1]
+                )
+            else:
+                nc.vector.tensor_scalar(
+                    out=planes[:, j, lo:hi], in0=tiles["h", i][:, lo:hi], scalar1=depth_f[:, g, j : j + 1], scalar2=None, op0=MULT
+                )
+
+        def weighted_interleave(g, ch, engine):
+            grouped = work.tile([P, CH, PACK], BF16, name=f"wg_{g}_{ch}", tag="wg", bufs=4, align_bytes=64)
+            tiles["wg", g, ch] = grouped
+            src = tiles["wp", g][:, :, ch * CH : (ch + 1) * CH].rearrange("p j (n i) -> p n j i", i=4)
+            dst = grouped[:].rearrange("p (n i) j -> p n j i", i=4)
+            if engine == "A":
+                nc.scalar.copy(out=dst, in_=src)
+            else:
+                nc.vector.tensor_copy(out=dst, in_=src)
+
+        def weighted_quantize(g, ch):
+            cols = slice(ch * CH, (ch + 1) * CH)
+            nc.vector.quantize_mx(
+                out=wt_codes[:, g, cols].bitcast(FP8X4),
+                scales=wt_scales[:, g, cols],
+                in_=tiles.pop(("wg", g, ch))[:].rearrange("p n t -> p (n t)"),
+            )
+
+        def moves_transpose(i, half):
+            bank = psum.tile([P, PACK, P], F32, name=f"ht_{i}_{half}", tag="z" if i == TILES - 1 else "ht", bufs=2)
+            tiles["ht", i, half] = bank
+            h = tiles["h", i]
+            for j in range(PACK):
+                c0 = half * BANK + j * P
+                nc.tensor.transpose(bank[:, j, :], h[:, c0 : c0 + P], ident[:])
+
+        def moves_scale(i, half):
+            if half == 0:
+                grouped = work.tile([P, N_PASSES, P, PACK], BF16, name=f"mg_{i}", tag="mg", bufs=3, align_bytes=64)
+                tiles["mg", i] = grouped
+            grouped = tiles["mg", i]
+            nc.vector.tensor_tensor(
+                out=grouped[:, half, :, :],
+                in0=tiles.pop(("ht", i, half))[:].rearrange("p j t -> p t j"),
+                in1=vol_f[:, half, :].unsqueeze(1).to_broadcast([P, P, PACK]),
+                op=MULT,
+            )
+
+        def moves_quantize(i):
+            codes = work.tile([P, N_PASSES, P], U32, name=f"mc_{i}", tag="mc", bufs=4, align_bytes=64)
+            scales = work.tile([P, N_PASSES, P], U8, name=f"ms_{i}", tag="ms", bufs=4, align_bytes=64)
+            tiles["mc", i] = (codes, scales)
+            nc.vector.quantize_mx(
+                out=codes[:].rearrange("p g t -> p (g t)").bitcast(FP8X4),
+                scales=scales[:].rearrange("p g t -> p (g t)"),
+                in_=tiles.pop(("mg", i))[:].rearrange("p g t j -> p (g t j)"),
+            )
+
+        def hedge_matmul(i):
+            codes, scales = tiles.pop(("mc", i))
+            side = i in (TILES - 3, TILES - 1)
+            bank = psum.tile([P, R], F32, name=f"hg_{i}", tag="ht" if side else "hg", bufs=2 if side else 1)
+            tiles["hg", i] = bank
+            for g in range(N_PASSES):
+                nc.tensor.matmul_mx(
+                    out=bank[:],
+                    lhsT=codes[:, g, :].bitcast(FP8X4),
+                    lhsT_scale=scales[:, g, :],
+                    rhs=w_words[:, g, :].bitcast(FP4X4),
+                    rhs_scale=w_scales[:, g, :],
+                    start=(g == 0),
+                    stop=(g == N_PASSES - 1),
+                )
+
+        hedge_view = hedge.rearrange("(g p j) r -> g j p r", p=P, j=PACK)
+
+        def hedge_exit(i, engine):
+            g, j = divmod(i, PACK)
+            res = work.tile([P, R], F32, name=f"hr_{i}", tag="hr", bufs=3, align_bytes=64)
+            bank = tiles.pop(("hg", i))
+            if engine == "A":
+                nc.scalar.copy(out=res[:], in_=bank[:])
+            else:
+                nc.vector.tensor_copy(out=res[:], in_=bank[:])
+            nc.sync.dma_start(out=hedge_view[g, j], in_=res[:])
+
+        def sched_transpose(b):
+            qt, gp = divmod(b, 2)
+            words = sched_sb[qt][:].bitcast(F32)
+            bank = psum.tile([P, PACK, P], F32, name=f"st_{b}", tag="xt", bufs=3)
+            tiles["st", b] = bank
+            for s in range(2):
+                g = 2 * gp + s
+                for u in range(2):
+                    nc.tensor.transpose(bank[:, 2 * s + u, :], words[:, 256 * g + u : 256 * (g + 1) : 2], ident[:])
+
+        def sched_exit(b):
+            grouped = work.tile([P, 2, P, PACK], BF16, name=f"sg_{b}", tag="sg", bufs=2, align_bytes=64)
+            tiles["sg", b] = grouped
+            words = grouped[:].rearrange("p s q t -> p (s q t)").bitcast(F32)
+            nc.scalar.copy(
+                out=words.rearrange("p (s q u) -> p s q u", s=2, u=2),
+                in_=tiles.pop(("st", b))[:].rearrange("p (s u) q -> p s q u", u=2),
+            )
+
+        def sched_quantize(b):
+            qt, gp = divmod(b, 2)
+            nc.vector.quantize_mx(
+                out=sch_codes[:, qt, 2 * gp : 2 * gp + 2, :].rearrange("p s q -> p (s q)").bitcast(FP8X4),
+                scales=sch_scales[:, qt, 2 * gp : 2 * gp + 2, :].rearrange("p s q -> p (s q)"),
+                in_=tiles.pop(("sg", b))[:].rearrange("p s q t -> p (s q t)"),
+            )
+
+        def cost_matmul(qt, half, g):
+            if g == 0:
+                bank = psum.tile(
+                    [P, BANK],
+                    F32,
+                    name=f"cost_{qt}_{half}",
+                    tag="ht" if (qt, half) == (1, 1) else "xt",
+                    bufs=2 if (qt, half) == (1, 1) else 3,
+                )
+                tiles["cb", qt, half] = bank
+            cols = slice(half * BANK, (half + 1) * BANK)
+            nc.tensor.matmul_mx(
+                out=tiles["cb", qt, half][:],
+                lhsT=sch_codes[:, qt, g, :].bitcast(FP8X4),
+                lhsT_scale=sch_scales[:, qt, g, :],
+                rhs=wt_codes[:, g, cols].bitcast(FP8X4),
+                rhs_scale=wt_scales[:, g, cols],
+                start=(g == 0),
+                stop=(g == T_PASSES - 1),
+            )
+
+        def cost_exit(qt, half, engine):
+            res = work.tile([P, BANK], F32, name=f"cr_{qt}_{half}", tag="cr", bufs=4, align_bytes=64)
+            dst = res[:].rearrange("p (m j) -> p m j", j=PACK)
+            src = tiles.pop(("cb", qt, half))[:].rearrange("p (j m) -> p m j", j=PACK)
+            if engine == "A":
+                nc.scalar.copy(out=dst, in_=src)
+            else:
+                nc.vector.tensor_copy(out=dst, in_=src)
+            nc.sync.dma_start(out=cost[qt * P : (qt + 1) * P, half * BANK : (half + 1) * BANK], in_=res[:])
+
+        spread_scale()
+        impact_interleave(0, 0, "D")
+        impact_interleave(1, 0, "D")
+        impact_interleave(2, 0, "A")
+        impact_quantize(0, 0)
+        widen(0)
+        flow_transpose(0)
+        flow_exit(0)
+        impact_interleave(0, 1, "A")
+        impact_quantize(1, 0)
+        widen(1)
+        impact_quantize(2, 0)
+        flow_transpose(1)
+        flow_quantize(0)
+        flow_exit(1)
+        impact_interleave(1, 1, "A")
+        widen(2)
+        impact_matmul(0, 0)
+        saturate(0, 0)
+        flow_quantize(1)
+        impact_quantize(0, 1)
+        impact_matmul(1, 0)
+        flow_transpose(2)
+        flow_exit(2)
+        saturate(1, 0)
+        widen(3)
+        impact_interleave(2, 1, "D")
+        impact_quantize(1, 1)
+        nc.vector.tensor_copy(out=vol_f[:], in_=vol_b[:])
+        nc.vector.tensor_copy(out=depth_f[:], in_=depth_b[:])
+        impact_quantize(2, 1)
+        flow_transpose(3)
+        flow_exit(3)
+        impact_matmul(0, 1)
+        widen(4)
+        flow_quantize(2)
+
+        early = [(0, 0, 0), (1, 0, 0), (0, 1, 0), (0, 0, 1), (1, 0, 1), (0, 1, 1), (0, 0, 2), (1, 0, 2), (0, 1, 2)]
+
+        def cost_early(count):
+            for c in range(count):
+                cost_matmul(*early.pop(0))
+
+        on_scalar = (0, 3, 6,)
+        chunk_step = (5, 6, 7, 8, 9, 10, 11, 12, 13, 14, 14, 15)
+        for s in range(1, TILES):
+            chunks = [k for k in range(len(chunk_step)) if chunk_step[k] == s]
+            if 0 <= s - 3 < TILES:
+                moves_quantize(s - 3)
+            for half in range(N_PASSES):
+                if (s - 1, half) not in ((0, 0), (1, 0)):
+                    saturate(s - 1, half)
+            if 4 <= s + 2 < TILES:
+                flow_transpose(s + 2)
+                flow_exit(s + 2)
+            if 3 <= s + 1 < TILES:
+                flow_quantize(s + 1)
+            weigh(s - 1, "A")
+            if 9 <= s < 9 + 4:
+                sched_transpose(s - 9)
+                sched_exit(s - 9)
+            if s >= TILES - 2:
+                cost_early(2 if s == TILES - 2 else 2)
+            for half in range(N_PASSES):
+                if s >= 2 and (s - 2, half) not in ():
+                    moves_transpose(s - 2, half)
+                    moves_scale(s - 2, half)
+            for k in chunks:
+                weighted_interleave(k // CHUNKS, k % CHUNKS, "A" if k in on_scalar else "D")
+            if 9 <= s < 9 + 4:
+                sched_quantize(s - 9)
+            if s >= 4:
+                hedge_matmul(s - 4)
+                hedge_exit(s - 4, "A")
+            if 5 <= s + 4 < TILES:
+                widen(s + 4)
+            for k in chunks:
+                weighted_quantize(k // CHUNKS, k % CHUNKS)
+            for half in range(N_PASSES):
+                if (s, half) not in ((1, 0),):
+                    impact_matmul(s, half)
+
+        last = TILES - 1
+        g = T_PASSES - 1
+        saturate(last, 0)
+        weigh(last, "D", 0, BANK)
+        saturate(last, 1)
+        moves_quantize(last - 2)
+        for i in (last - 1, last):
+            for half in range(N_PASSES):
+                moves_transpose(i, half)
+        weighted_interleave(g, 1, "A")
+        moves_scale(last - 1, 0)
+        weigh(last, "D", BANK, N)
+        moves_scale(last - 1, 1)
+        hedge_matmul(last - 3)
+        hedge_exit(last - 3, "A")
+        weighted_interleave(g, 0, "D")
+        moves_scale(last, 0)
+        moves_quantize(last - 1)
+        hedge_matmul(last - 2)
+        weighted_interleave(g, 3, "A")
+        hedge_exit(last - 2, "A")
+        cost_early(len(early))
+        weighted_quantize(g, 0)
+        moves_scale(last, 1)
+        weighted_quantize(g, 1)
+        weighted_interleave(g, 2, "D")
+        hedge_matmul(last - 1)
+        hedge_exit(last - 1, "A")
+        for g2 in range(T_PASSES - 1):
+            cost_matmul(1, 1, g2)
+        for qt in range(2):
+            cost_matmul(qt, 0, g)
+            cost_exit(qt, 0, "A")
+        moves_quantize(last)
+        weighted_quantize(g, 2)
+        weighted_quantize(g, 3)
+        hedge_matmul(last)
+        for qt in range(2):
+            cost_matmul(qt, 1, g)
+        hedge_exit(last, "A")
+        cost_exit(0, 1, "D")
+        cost_exit(1, 1, "D")

@@ -14,6 +14,7 @@ FP8 = mybir.dt.float8_e4m3fn
 FP8X4 = mybir.dt.float8_e4m3fn_x4
 FP4X4 = mybir.dt.float4_e2m1fn_x4
 MULT = mybir.AluOpType.mult
+ADD = mybir.AluOpType.add
 TANH = mybir.ActivationFunctionType.Tanh
 COPY = mybir.ActivationFunctionType.Copy
 
@@ -26,10 +27,10 @@ A_PASSES = A // K_PASS
 N_PASSES = N // K_PASS
 T_PASSES = T // K_PASS
 TILES = T // P
+PAIRS = TILES // 2
+STEPS = PAIRS * N_PASSES
 BANK = 512
-W_LEAD = 4
 CH = 256
-CHUNKS = N // CH
 
 
 def tile_cross_impact_hedge_s8_kernel(
@@ -42,11 +43,6 @@ def tile_cross_impact_hedge_s8_kernel(
         psum = ctx.enter_context(tc.psum_pool(name="psum", bufs=2))
         ctx.enter_context(tc.manual_schedule())
 
-        warm = keep.tile([P, 1], F32, name="warm")
-        nc.vector.memset(warm[:], 0.0)
-        nc.scalar.activation(out=warm[:], in_=warm[:], func=TANH)
-        scale_rows = keep.tile([P, 3 * P], F32, name="scale_rows")
-        nc.vector.memset(scale_rows[:], 0.0)
         w_scales = keep.tile([P, N_PASSES, R], U8, name="w_scales", align_bytes=64)
         nc.vector.memset(w_scales[:].bitcast(I32), 0)
         ident = keep.tile([P, P], F32, name="ident")
@@ -54,14 +50,13 @@ def tile_cross_impact_hedge_s8_kernel(
 
         flow_view = flow_bytes.rearrange("(g p j) a -> g p j a", p=P, j=PACK)
         flow_sb = []
-        for g in range(T_PASSES):
-            for half in range(2):
-                t_f = keep.tile([P, 2, A], U8, name=f"flow_{g}_{half}", align_bytes=64)
-                flow_sb.append(t_f)
+        for q in range(PAIRS):
+            t_f = keep.tile([P, 2, A], U8, name=f"flow_{q}", align_bytes=64)
+            flow_sb.append(t_f)
 
-        def load_flow(pair):
-            g, half = divmod(pair, 2)
-            nc.sync.dma_start(out=flow_sb[pair][:], in_=flow_view[g, :, 2 * half : 2 * half + 2, :])
+        def load_flow(q):
+            g, r = divmod(q, 2)
+            nc.sync.dma_start(out=flow_sb[q][:], in_=flow_view[g, :, 2 * r : 2 * r + 2, :])
 
         imp_view = impact.rearrange("(c p t) n -> c p t n", p=P, t=PACK)
         imp_raw = {}
@@ -73,43 +68,37 @@ def tile_cross_impact_hedge_s8_kernel(
         def load_impact(c, half):
             nc.sync.dma_start(out=imp_raw[c, half][:], in_=imp_view[c, :, :, half * BANK : (half + 1) * BANK])
 
-        scale_sb = keep.tile([P, A], F32, name="scale_sb", align_bytes=64)
-        vol_b = keep.tile([P, N_PASSES, PACK], BF16, name="vol_b")
-        depth_b = keep.tile([P, T_PASSES, PACK], BF16, name="depth_b")
+        scale_sb = keep.tile([P, A_PASSES, PACK], F32, name="scale_sb", align_bytes=64)
+        vol_sb = keep.tile([P, N_PASSES, PACK], BF16, name="vol_sb", align_bytes=64)
+        depth_bf = keep.tile([P, T_PASSES, PACK], BF16, name="depth_bf", align_bytes=64)
+        depth_sb = keep.tile([P, T_PASSES, PACK], F32, name="depth_sb", align_bytes=64)
+        planes = keep.tile([P, PACK, BANK], BF16, name="planes", align_bytes=64)
         w_words = keep.tile([P, N_PASSES, 2 * R], U8, name="w_words", align_bytes=64)
         sched_sb = []
         for qt in range(2):
             t_s = keep.tile([P, T], BF16, name=f"sched_{qt}", align_bytes=64)
             sched_sb.append(t_s)
 
-        nc.sync.dma_start(out=scale_rows[0:4, :], in_=flow_scale.rearrange("o (r k) -> (o r) k", r=4))
-        load_impact(0, 0)
-        load_impact(1, 0)
-        load_flow(0)
-        load_impact(2, 0)
-        load_impact(0, 1)
-        load_impact(1, 1)
-        load_impact(2, 1)
-        load_flow(1)
-        load_flow(2)
-        nc.sync.dma_start(out=vol_b[:], in_=vol.rearrange("(g p j) -> p g j", p=P, j=PACK))
-        nc.sync.dma_start(out=depth_b[:], in_=depth.rearrange("(g p j) -> p g j", p=P, j=PACK))
-        for q4 in range(4):
-            nc.sync.dma_start(
-                out=w_scales[32 * q4 : 32 * q4 + 4, :, :].bitcast(I32),
-                in_=sens_scales[:, 4 * q4 : 4 * q4 + 4, :].rearrange("g r n -> r g n").bitcast(I32),
-            )
-        nc.sync.dma_start(out=w_words[:].bitcast(I32), in_=sens_words.rearrange("g p b -> p g b").bitcast(I32))
-        load_flow(3)
-        load_flow(4)
-        for qt in range(2):
-            nc.sync.dma_start(out=sched_sb[qt][:], in_=sched[qt * P : (qt + 1) * P, :])
-        load_flow(5)
-        load_flow(6)
-        load_flow(7)
+        def load_scale():
+            nc.scalar.dma_start(out=scale_sb[:], in_=flow_scale.rearrange("o (c p t) -> p (o c) t", p=P, t=PACK))
 
-        vol_f = keep.tile([P, N_PASSES, PACK], F32, name="vol_f")
-        depth_f = keep.tile([P, T_PASSES, PACK], F32, name="depth_f")
+        def load_depth():
+            nc.scalar.dma_start(out=depth_bf[:], in_=depth.rearrange("(g p j) -> p g j", p=P, j=PACK))
+            nc.scalar.activation(out=depth_sb[:], in_=depth_bf[:], func=COPY)
+
+        def load_vol():
+            nc.sync.dma_start(out=vol_sb[:], in_=vol.rearrange("(g p j) -> p g j", p=P, j=PACK))
+
+        def load_sens():
+            for q4 in range(4):
+                nc.sync.dma_start(
+                    out=w_scales[32 * q4 : 32 * q4 + 4, :, :].bitcast(I32),
+                    in_=sens_scales[:, 4 * q4 : 4 * q4 + 4, :].rearrange("g r n -> r g n").bitcast(I32),
+                )
+            nc.sync.dma_start(out=w_words[:].bitcast(I32), in_=sens_words.rearrange("g p b -> p g b").bitcast(I32))
+
+        def load_sched(qt):
+            nc.sync.dma_start(out=sched_sb[qt][:], in_=sched[qt * P : (qt + 1) * P, :])
 
         imp_codes = keep.tile([P, A_PASSES, N], U32, name="imp_codes", align_bytes=64)
         imp_scales = keep.tile([P, A_PASSES, N], U8, name="imp_scales", align_bytes=64)
@@ -119,93 +108,84 @@ def tile_cross_impact_hedge_s8_kernel(
         sch_scales = keep.tile([P, 2, T_PASSES, P], U8, name="sch_scales", align_bytes=64)
         tiles = {}
 
-        def impact_interleave(c, half, engine):
-            grouped = work.tile([P, BANK, PACK], BF16, name=f"imp_grp_{c}_{half}", tag="imp_grp", bufs=3, align_bytes=64)
-            tiles["ig", c, half] = grouped
+        def impact_interleave(c, ch, engine):
+            half, lo = divmod(ch * CH, BANK)
+            grouped = work.tile([P, CH, PACK], BF16, name=f"ig_{c}_{ch}", tag="ig", bufs=6, align_bytes=64)
+            tiles["ig", c, ch] = grouped
+            raw = imp_raw[c, half][:, :, lo : lo + CH]
             dst = grouped[:].rearrange("p (n i) t -> p n t i", i=4)
-            src = imp_raw[c, half][:].rearrange("p t (n i) -> p n t i", i=4)
-            if engine == "A":
+            src = raw.rearrange("p t (n i) -> p n t i", i=4)
+            if engine == "S":
                 nc.scalar.copy(out=dst, in_=src)
-            else:
+            elif engine == "V":
                 nc.vector.tensor_copy(out=dst, in_=src)
+            else:
+                nc.gpsimd.tensor_scalar(
+                    out=grouped[:], in0=raw.rearrange("p t n -> p n t"), scalar1=1.0, scalar2=0.0, op0=MULT, op1=ADD
+                )
 
-        def impact_quantize(c, half):
-            cols = slice(half * BANK, (half + 1) * BANK)
+        def impact_quantize(c, ch):
+            cols = slice(ch * CH, (ch + 1) * CH)
             nc.vector.quantize_mx(
                 out=imp_codes[:, c, cols].bitcast(FP8X4),
                 scales=imp_scales[:, c, cols],
-                in_=tiles.pop(("ig", c, half))[:].rearrange("p n t -> p (n t)"),
+                in_=tiles.pop(("ig", c, ch))[:].rearrange("p n t -> p (n t)"),
             )
 
-        def spread_scale():
-            bank = psum.tile([P, 3, P], F32, name="scale_cols", tag="ht", bufs=2)
-            for b in range(3):
-                nc.tensor.transpose(bank[:, b, :], scale_rows[:, b * P : (b + 1) * P], ident[:])
-            scale_cols = keep.tile([P, 4, 3], F32, name="scale_cols_sb")
-            nc.scalar.copy(out=scale_cols[:], in_=bank[:, :, 0:4].rearrange("p b r -> p r b"))
-            for c in range(A_PASSES):
-                bank = psum.tile([P, PACK, P], F32, name=f"scale_bank_{c}", tag="z", bufs=2)
-                for s in range(PACK):
-                    k = PACK * c + s
-                    nc.tensor.transpose(
-                        bank[:, s, :], scale_cols[:, k // 3, k % 3 : k % 3 + 1].to_broadcast([P, P]), ident[:]
-                    )
-                nc.scalar.copy(
-                    out=scale_sb[:, c * K_PASS : (c + 1) * K_PASS], in_=bank[:].rearrange("p s k -> p (s k)")
-                )
-
-        def widen(i):
+        def widen(i, engine="S"):
             wide = work.tile([P, A], BF16, name=f"wide_{i}", tag="wide", bufs=5, align_bytes=64)
             tiles["wide", i] = wide
+            src = flow_sb[i // 2][:, i % 2, :].bitcast(FP8)
+            if engine == "S":
+                nc.scalar.copy(out=wide[:], in_=src)
+            else:
+                nc.vector.tensor_copy(out=wide[:], in_=src)
+
+        def flow_transpose(q, c):
+            bank = psum.tile([P, 2, 2, P], F32, name=f"xt_{q}_{c}", tag="xt", bufs=3)
+            tiles["xt", q, c] = bank
+            for r in range(2):
+                words = tiles["wide", 2 * q + r][:].bitcast(F32)
+                for u in range(2):
+                    nc.tensor.transpose(bank[:, u, r, :], words[:, 256 * c + u : 256 * (c + 1) : 2], ident[:])
+
+        def flow_scale_out(q, c, lo=0, hi=2):
+            if lo == 0:
+                grouped = work.tile([P, 2 * P, PACK], BF16, name=f"fg_{q}_{c}", tag="fg", bufs=4, align_bytes=64)
+                tiles["fg", q, c] = grouped
+            halves = tiles["xt", q, c][:].rearrange("p u r m -> p (u r m)").bitcast(BF16)
+            rows = slice(lo * P, hi * P)
             nc.vector.tensor_tensor(
-                out=wide[:], in0=flow_sb[i // 2][:, i % 2, :].bitcast(FP8), in1=scale_sb[:], op=MULT
+                out=tiles["fg", q, c][:, rows, :].rearrange("p m (u e) -> p m u e", u=2),
+                in0=halves.rearrange("p (u m e) -> p m u e", u=2, e=2)[:, rows, :, :],
+                in1=scale_sb[:, c, :]
+                .rearrange("p (u e) -> p u e", u=2)
+                .unsqueeze(1)
+                .to_broadcast([P, (hi - lo) * P, 2, 2]),
+                op=MULT,
             )
 
-        def flow_transpose(i):
-            words = tiles.pop(("wide", i))[:].bitcast(F32)
-            for part, passes in ((0, (0, 1)), (1, (2,))):
-                bank = psum.tile([P, PACK, P], F32, name=f"xt_{i}_{part}", tag="xt", bufs=3)
-                tiles["xt", i, part] = bank
-                slot = 0
-                for c in passes:
-                    for u in range(2):
-                        nc.tensor.transpose(
-                            bank[:, slot, :], words[:, 256 * c + u : 256 * (c + 1) : 2], ident[:]
-                        )
-                        slot += 1
-
-        def flow_exit(i):
-            grouped = work.tile([P, A_PASSES, P, PACK], BF16, name=f"fg_{i}", tag="fg", bufs=3, align_bytes=64)
-            tiles["fg", i] = grouped
-            words = grouped[:].rearrange("p c r t -> p (c r t)").bitcast(F32)
-            words = words.rearrange("p (c r u) -> p c r u", c=A_PASSES, u=2)
-            xt0 = tiles.pop(("xt", i, 0))
-            xt1 = tiles.pop(("xt", i, 1))
-            nc.scalar.copy(out=words[:, 0:2, :, :], in_=xt0[:].rearrange("p (c u) r -> p c r u", u=2))
-            nc.scalar.copy(out=words[:, 2, :, :], in_=xt1[:, 0:2, :].rearrange("p u r -> p r u"))
-
-        def flow_quantize(i):
-            codes = work.tile([P, A_PASSES, P], U32, name=f"fc_{i}", tag="fc", bufs=4, align_bytes=64)
-            scales = work.tile([P, A_PASSES, P], U8, name=f"fs_{i}", tag="fs", bufs=4, align_bytes=64)
-            tiles["fc", i] = (codes, scales)
-            grouped = tiles.pop(("fg", i))
-            for lo, hi in ((0, 2), (2, 3)):
-                nc.vector.quantize_mx(
-                    out=codes[:, lo:hi, :].rearrange("p c r -> p (c r)").bitcast(FP8X4),
-                    scales=scales[:, lo:hi, :].rearrange("p c r -> p (c r)"),
-                    in_=grouped[:, lo:hi, :, :].rearrange("p c r t -> p (c r t)"),
-                )
+        def flow_quantize(q, c):
+            codes = work.tile([P, 2 * P], U32, name=f"fc_{q}_{c}", tag="fc", bufs=9, align_bytes=64)
+            scales = work.tile([P, 2 * P], U8, name=f"fs_{q}_{c}", tag="fs", bufs=9, align_bytes=64)
+            tiles["fc", q, c] = (codes, scales)
+            nc.vector.quantize_mx(
+                out=codes[:].bitcast(FP8X4),
+                scales=scales[:],
+                in_=tiles.pop(("fg", q, c))[:].rearrange("p m t -> p (m t)"),
+            )
 
         def impact_matmul(i, half):
-            codes, scales = tiles["fc", i]
+            q, r = divmod(i, 2)
             z = psum.tile([P, BANK], F32, name=f"z_{i}_{half}", tag="z", bufs=2)
             tiles["z", i, half] = z
             cols = slice(half * BANK, (half + 1) * BANK)
             for c in range(A_PASSES):
+                codes, scales = tiles["fc", q, c]
                 nc.tensor.matmul_mx(
                     out=z[:],
-                    lhsT=codes[:, c, :].bitcast(FP8X4),
-                    lhsT_scale=scales[:, c, :],
+                    lhsT=codes[:, r * P : (r + 1) * P].bitcast(FP8X4),
+                    lhsT_scale=scales[:, r * P : (r + 1) * P],
                     rhs=imp_codes[:, c, cols].bitcast(FP8X4),
                     rhs_scale=imp_scales[:, c, cols],
                     start=(c == 0),
@@ -213,36 +193,55 @@ def tile_cross_impact_hedge_s8_kernel(
                 )
 
         def saturate(i, half):
-            if half == 0:
-                h = work.tile([P, N], F32, name=f"h_{i}", tag="h", bufs=4, align_bytes=64)
-                tiles["h", i] = h
+            g, j = divmod(i, PACK)
+            if j == 0:
+                h = work.tile([P, PACK, BANK], F32, name=f"h_{g}_{half}", tag="h", bufs=4, align_bytes=64)
+                tiles["h", g, half] = h
             nc.scalar.activation(
-                out=tiles["h", i][:, half * BANK : (half + 1) * BANK].rearrange("p (j m) -> p j m", j=PACK),
-                in_=tiles.pop(("z", i, half))[:].rearrange("p (m j) -> p j m", j=PACK),
+                out=tiles["h", g, half][:, j, :].rearrange("p (t m) -> p t m", t=PACK),
+                in_=tiles.pop(("z", i, half))[:].rearrange("p (m t) -> p t m", t=PACK),
                 func=TANH,
             )
 
-        def weigh(i, engine, lo=0, hi=N):
-            g, j = divmod(i, PACK)
-            if j == 0:
-                planes = work.tile([P, PACK, N], BF16, name=f"wp_{g}", tag="wp", bufs=3, align_bytes=64)
-                tiles["wp", g] = planes
-            planes = tiles["wp", g]
-            if engine == "A":
-                nc.scalar.activation(
-                    out=planes[:, j, lo:hi], in_=tiles["h", i][:, lo:hi], func=COPY, scale=depth_f[:, g, j : j + 1]
+        def weigh(g, ch, engine):
+            half, lo = divmod(ch * CH, BANK)
+            grouped = work.tile(
+                [P, CH, PACK], BF16, name=f"wg_{g}_{ch}", tag="wg" + engine, bufs=1 if engine == "G" else 2, align_bytes=64
+            )
+            tiles["wg", g, ch] = grouped
+            src = tiles["h", g, half][:, :, lo : lo + CH]
+            if engine == "G":
+                nc.gpsimd.tensor_tensor(
+                    out=grouped[:],
+                    in0=src.rearrange("p j n -> p n j"),
+                    in1=depth_sb[:, g, :].unsqueeze(1).to_broadcast([P, CH, PACK]),
+                    op=MULT,
                 )
             else:
-                nc.vector.tensor_scalar(
-                    out=planes[:, j, lo:hi], in0=tiles["h", i][:, lo:hi], scalar1=depth_f[:, g, j : j + 1], scalar2=None, op0=MULT
+                nc.vector.tensor_tensor(
+                    out=grouped[:].rearrange("p (n i) j -> p n j i", i=4),
+                    in0=src.rearrange("p j (n i) -> p n j i", i=4),
+                    in1=depth_sb[:, g, :].unsqueeze(1).unsqueeze(3).to_broadcast([P, CH // 4, PACK, 4]),
+                    op=MULT,
                 )
 
-        def weighted_interleave(g, ch, engine):
-            grouped = work.tile([P, CH, PACK], BF16, name=f"wg_{g}_{ch}", tag="wg", bufs=4, align_bytes=64)
-            tiles["wg", g, ch] = grouped
-            src = tiles["wp", g][:, :, ch * CH : (ch + 1) * CH].rearrange("p j (n i) -> p n j i", i=4)
-            dst = grouped[:].rearrange("p (n i) j -> p n j i", i=4)
-            if engine == "A":
+        def weigh_plane(j, engine):
+            g = T_PASSES - 1
+            src = tiles["h", g, 1][:, j, :]
+            if engine == "S":
+                nc.scalar.activation(out=planes[:, j, :], in_=src, func=COPY, scale=depth_sb[:, g, j : j + 1])
+            else:
+                nc.vector.tensor_scalar(
+                    out=planes[:, j, :], in0=src, scalar1=depth_sb[:, g, j : j + 1], scalar2=None, op0=MULT
+                )
+
+        def planes_interleave(ch, engine):
+            grouped = work.tile([P, CH, PACK], BF16, name=f"wg_last_{ch}", tag="ig", bufs=6, align_bytes=64)
+            tiles["wg", T_PASSES - 1, ch] = grouped
+            lo = ch * CH - BANK
+            dst = grouped[:].rearrange("p (n i) t -> p n t i", i=4)
+            src = planes[:, :, lo : lo + CH].rearrange("p t (n i) -> p n t i", i=4)
+            if engine == "S":
                 nc.scalar.copy(out=dst, in_=src)
             else:
                 nc.vector.tensor_copy(out=dst, in_=src)
@@ -255,59 +254,60 @@ def tile_cross_impact_hedge_s8_kernel(
                 in_=tiles.pop(("wg", g, ch))[:].rearrange("p n t -> p (n t)"),
             )
 
-        def moves_transpose(i, half):
-            bank = psum.tile([P, PACK, P], F32, name=f"ht_{i}_{half}", tag="z" if i == TILES - 1 else "ht", bufs=2)
+        def moves_transpose(i, half, tag="ht"):
+            g, j = divmod(i, PACK)
+            bank = psum.tile([P, PACK, P], F32, name=f"ht_{i}_{half}", tag=tag, bufs=2)
             tiles["ht", i, half] = bank
-            h = tiles["h", i]
-            for j in range(PACK):
-                c0 = half * BANK + j * P
-                nc.tensor.transpose(bank[:, j, :], h[:, c0 : c0 + P], ident[:])
+            for t in range(PACK):
+                nc.tensor.transpose(bank[:, t, :], tiles["h", g, half][:, j, t * P : (t + 1) * P], ident[:])
 
         def moves_scale(i, half):
-            if half == 0:
-                grouped = work.tile([P, N_PASSES, P, PACK], BF16, name=f"mg_{i}", tag="mg", bufs=3, align_bytes=64)
-                tiles["mg", i] = grouped
-            grouped = tiles["mg", i]
+            q, r = divmod(i, 2)
+            if r == 0:
+                grouped = work.tile([P, 2, P, PACK], BF16, name=f"mg_{q}_{half}", tag="mg", bufs=3, align_bytes=64)
+                tiles["mg", q, half] = grouped
             nc.vector.tensor_tensor(
-                out=grouped[:, half, :, :],
-                in0=tiles.pop(("ht", i, half))[:].rearrange("p j t -> p t j"),
-                in1=vol_f[:, half, :].unsqueeze(1).to_broadcast([P, P, PACK]),
+                out=tiles["mg", q, half][:, r, :, :],
+                in0=tiles.pop(("ht", i, half))[:].rearrange("p t m -> p m t"),
+                in1=vol_sb[:, half, :].unsqueeze(1).to_broadcast([P, P, PACK]),
                 op=MULT,
             )
 
-        def moves_quantize(i):
-            codes = work.tile([P, N_PASSES, P], U32, name=f"mc_{i}", tag="mc", bufs=4, align_bytes=64)
-            scales = work.tile([P, N_PASSES, P], U8, name=f"ms_{i}", tag="ms", bufs=4, align_bytes=64)
-            tiles["mc", i] = (codes, scales)
+        def moves_quantize(q, half):
+            codes = work.tile([P, 2 * P], U32, name=f"mc_{q}_{half}", tag="mc", bufs=5, align_bytes=64)
+            scales = work.tile([P, 2 * P], U8, name=f"ms_{q}_{half}", tag="ms", bufs=5, align_bytes=64)
+            tiles["mc", q, half] = (codes, scales)
             nc.vector.quantize_mx(
-                out=codes[:].rearrange("p g t -> p (g t)").bitcast(FP8X4),
-                scales=scales[:].rearrange("p g t -> p (g t)"),
-                in_=tiles.pop(("mg", i))[:].rearrange("p g t j -> p (g t j)"),
+                out=codes[:].bitcast(FP8X4),
+                scales=scales[:],
+                in_=tiles.pop(("mg", q, half))[:].rearrange("p r m t -> p (r m t)"),
             )
 
-        def hedge_matmul(i):
-            codes, scales = tiles.pop(("mc", i))
-            side = i in (TILES - 3, TILES - 1)
-            bank = psum.tile([P, R], F32, name=f"hg_{i}", tag="ht" if side else "hg", bufs=2 if side else 1)
-            tiles["hg", i] = bank
-            for g in range(N_PASSES):
+        def hedge_matmul(i, tag="hg", halves=(0, 1)):
+            q, r = divmod(i, 2)
+            if halves[0] == 0:
+                bank = psum.tile([P, R], F32, name=f"hg_{i}", tag=tag, bufs=1 if tag == "hg" else 2)
+                tiles["hg", i] = bank
+            bank = tiles["hg", i]
+            for half in halves:
+                codes, scales = tiles["mc", q, half]
                 nc.tensor.matmul_mx(
                     out=bank[:],
-                    lhsT=codes[:, g, :].bitcast(FP8X4),
-                    lhsT_scale=scales[:, g, :],
-                    rhs=w_words[:, g, :].bitcast(FP4X4),
-                    rhs_scale=w_scales[:, g, :],
-                    start=(g == 0),
-                    stop=(g == N_PASSES - 1),
+                    lhsT=codes[:, r * P : (r + 1) * P].bitcast(FP8X4),
+                    lhsT_scale=scales[:, r * P : (r + 1) * P],
+                    rhs=w_words[:, half, :].bitcast(FP4X4),
+                    rhs_scale=w_scales[:, half, :],
+                    start=(half == 0),
+                    stop=(half == N_PASSES - 1),
                 )
 
         hedge_view = hedge.rearrange("(g p j) r -> g j p r", p=P, j=PACK)
 
-        def hedge_exit(i, engine):
+        def hedge_exit(i, engine="S"):
             g, j = divmod(i, PACK)
             res = work.tile([P, R], F32, name=f"hr_{i}", tag="hr", bufs=3, align_bytes=64)
             bank = tiles.pop(("hg", i))
-            if engine == "A":
+            if engine == "S":
                 nc.scalar.copy(out=res[:], in_=bank[:])
             else:
                 nc.vector.tensor_copy(out=res[:], in_=bank[:])
@@ -316,12 +316,12 @@ def tile_cross_impact_hedge_s8_kernel(
         def sched_transpose(b):
             qt, gp = divmod(b, 2)
             words = sched_sb[qt][:].bitcast(F32)
-            bank = psum.tile([P, PACK, P], F32, name=f"st_{b}", tag="xt", bufs=3)
+            bank = psum.tile([P, 2, 2, P], F32, name=f"st_{b}", tag="xt", bufs=3)
             tiles["st", b] = bank
             for s in range(2):
                 g = 2 * gp + s
                 for u in range(2):
-                    nc.tensor.transpose(bank[:, 2 * s + u, :], words[:, 256 * g + u : 256 * (g + 1) : 2], ident[:])
+                    nc.tensor.transpose(bank[:, s, u, :], words[:, 256 * g + u : 256 * (g + 1) : 2], ident[:])
 
         def sched_exit(b):
             grouped = work.tile([P, 2, P, PACK], BF16, name=f"sg_{b}", tag="sg", bufs=2, align_bytes=64)
@@ -329,7 +329,7 @@ def tile_cross_impact_hedge_s8_kernel(
             words = grouped[:].rearrange("p s q t -> p (s q t)").bitcast(F32)
             nc.scalar.copy(
                 out=words.rearrange("p (s q u) -> p s q u", s=2, u=2),
-                in_=tiles.pop(("st", b))[:].rearrange("p (s u) q -> p s q u", u=2),
+                in_=tiles.pop(("st", b))[:].rearrange("p s u q -> p s q u"),
             )
 
         def sched_quantize(b):
@@ -342,13 +342,8 @@ def tile_cross_impact_hedge_s8_kernel(
 
         def cost_matmul(qt, half, g):
             if g == 0:
-                bank = psum.tile(
-                    [P, BANK],
-                    F32,
-                    name=f"cost_{qt}_{half}",
-                    tag="ht" if (qt, half) == (1, 1) else "xt",
-                    bufs=2 if (qt, half) == (1, 1) else 3,
-                )
+                last = (qt, half) == (1, 1)
+                bank = psum.tile([P, BANK], F32, name=f"cost_{qt}_{half}", tag="z" if last else "xt", bufs=2 if last else 3)
                 tiles["cb", qt, half] = bank
             cols = slice(half * BANK, (half + 1) * BANK)
             nc.tensor.matmul_mx(
@@ -363,135 +358,169 @@ def tile_cross_impact_hedge_s8_kernel(
 
         def cost_exit(qt, half, engine):
             res = work.tile([P, BANK], F32, name=f"cr_{qt}_{half}", tag="cr", bufs=4, align_bytes=64)
-            dst = res[:].rearrange("p (m j) -> p m j", j=PACK)
-            src = tiles.pop(("cb", qt, half))[:].rearrange("p (j m) -> p m j", j=PACK)
-            if engine == "A":
+            dst = res[:].rearrange("p (m t) -> p m t", t=PACK)
+            src = tiles.pop(("cb", qt, half))[:].rearrange("p (t m) -> p m t", t=PACK)
+            if engine == "S":
                 nc.scalar.copy(out=dst, in_=src)
             else:
                 nc.vector.tensor_copy(out=dst, in_=src)
             nc.sync.dma_start(out=cost[qt * P : (qt + 1) * P, half * BANK : (half + 1) * BANK], in_=res[:])
 
-        spread_scale()
-        impact_interleave(0, 0, "D")
-        impact_interleave(1, 0, "D")
-        impact_interleave(2, 0, "A")
-        impact_quantize(0, 0)
-        widen(0)
-        flow_transpose(0)
-        flow_exit(0)
-        impact_interleave(0, 1, "A")
-        impact_quantize(1, 0)
-        widen(1)
-        impact_quantize(2, 0)
-        flow_transpose(1)
-        flow_quantize(0)
-        flow_exit(1)
-        impact_interleave(1, 1, "A")
+        load_scale()
+        load_depth()
+        load_flow(0)
+        load_impact(0, 0)
+        load_impact(1, 0)
+        load_impact(2, 0)
+        load_flow(1)
+        load_impact(0, 1)
+        load_impact(1, 1)
+        load_impact(2, 1)
+        load_flow(2)
+        load_vol()
+        load_sens()
+        load_flow(3)
+        load_flow(4)
+        load_sched(0)
+        load_sched(1)
+        for q in range(5, PAIRS):
+            load_flow(q)
+
+        widen(0, "V")
+        widen(1, "S")
+        for c in range(A_PASSES):
+            flow_transpose(0, c)
+        impact_interleave(0, 0, "S")
+        impact_interleave(0, 1, "V")
+        impact_interleave(1, 0, "S")
+        impact_interleave(1, 1, "G")
+        impact_interleave(2, 0, "S")
+        impact_interleave(2, 1, "G")
         widen(2)
-        impact_matmul(0, 0)
-        saturate(0, 0)
-        flow_quantize(1)
-        impact_quantize(0, 1)
-        impact_matmul(1, 0)
-        flow_transpose(2)
-        flow_exit(2)
-        saturate(1, 0)
         widen(3)
-        impact_interleave(2, 1, "D")
-        impact_quantize(1, 1)
-        nc.vector.tensor_copy(out=vol_f[:], in_=vol_b[:])
-        nc.vector.tensor_copy(out=depth_f[:], in_=depth_b[:])
-        impact_quantize(2, 1)
-        flow_transpose(3)
-        flow_exit(3)
-        impact_matmul(0, 1)
+        for c in range(A_PASSES):
+            flow_scale_out(0, c)
+        for c in range(A_PASSES):
+            flow_transpose(1, c)
+        for c in range(A_PASSES):
+            impact_quantize(c, 0)
+            impact_quantize(c, 1)
+            flow_quantize(0, c)
+        impact_interleave(0, 2, "S")
+        impact_interleave(0, 3, "G")
+        impact_interleave(1, 2, "S")
+        impact_interleave(1, 3, "G")
+        impact_interleave(2, 2, "S")
+        for c in range(A_PASSES):
+            flow_scale_out(1, c)
+        for r in range(2):
+            impact_matmul(r, 0)
+        impact_interleave(2, 3, "S")
+        for r in range(2):
+            saturate(r, 0)
         widen(4)
-        flow_quantize(2)
+        widen(5)
+        for c in range(A_PASSES):
+            impact_quantize(c, 2)
+            impact_quantize(c, 3)
+        for c in range(A_PASSES):
+            flow_quantize(1, c)
+        for r in range(2):
+            moves_transpose(r, 0)
+        for r in range(2):
+            impact_matmul(r, 1)
+            saturate(r, 1)
+        for r in range(2):
+            moves_scale(r, 0)
+        moves_quantize(0, 0)
 
-        early = [(0, 0, 0), (1, 0, 0), (0, 1, 0), (0, 0, 1), (1, 0, 1), (0, 1, 1), (0, 0, 2), (1, 0, 2), (0, 1, 2)]
-
-        def cost_early(count):
-            for c in range(count):
-                cost_matmul(*early.pop(0))
-
-        on_scalar = (0, 3, 6,)
-        chunk_step = (5, 6, 7, 8, 9, 10, 11, 12, 13, 14, 14, 15)
-        for s in range(1, TILES):
-            chunks = [k for k in range(len(chunk_step)) if chunk_step[k] == s]
-            if 0 <= s - 3 < TILES:
-                moves_quantize(s - 3)
-            for half in range(N_PASSES):
-                if (s - 1, half) not in ((0, 0), (1, 0)):
-                    saturate(s - 1, half)
-            if 4 <= s + 2 < TILES:
-                flow_transpose(s + 2)
-                flow_exit(s + 2)
-            if 3 <= s + 1 < TILES:
-                flow_quantize(s + 1)
-            weigh(s - 1, "A")
-            if 9 <= s < 9 + 4:
-                sched_transpose(s - 9)
-                sched_exit(s - 9)
-            if s >= TILES - 2:
-                cost_early(2 if s == TILES - 2 else 2)
-            for half in range(N_PASSES):
-                if s >= 2 and (s - 2, half) not in ():
-                    moves_transpose(s - 2, half)
-                    moves_scale(s - 2, half)
-            for k in chunks:
-                weighted_interleave(k // CHUNKS, k % CHUNKS, "A" if k in on_scalar else "D")
-            if 9 <= s < 9 + 4:
-                sched_quantize(s - 9)
+        last = T_PASSES - 1
+        for s in range(2, STEPS):
+            q, half = divmod(s, 2)
+            units = [(q + 1, c) for c in ((0, 1) if half == 0 else (2,))] if q + 1 < PAIRS else []
+            bank = (s - 7) // 2 if half == 1 and 7 <= s <= 13 else None
+            before = divmod(s - 1, 2) if s >= 1 else None
+            chunk = divmod(s - 3, PACK) if s >= 3 else None
+            if chunk and s < STEPS - 1:
+                weigh(*chunk, "G")
+            if s == STEPS - 1:
+                weigh(last, 0, "V")
+                weigh(last, 1, "V")
+                weigh_plane(0, "S")
+                weigh_plane(1, "S")
+            for unit in units:
+                flow_transpose(*unit)
+            if bank is not None:
+                sched_transpose(bank)
+            if before:
+                for r in range(2):
+                    moves_transpose(2 * before[0] + r, before[1])
             if s >= 4:
-                hedge_matmul(s - 4)
-                hedge_exit(s - 4, "A")
-            if 5 <= s + 4 < TILES:
+                hedge_exit(s - 4)
+            if s + 4 < TILES:
                 widen(s + 4)
-            for k in chunks:
-                weighted_quantize(k // CHUNKS, k % CHUNKS)
-            for half in range(N_PASSES):
-                if (s, half) not in ((1, 0),):
-                    impact_matmul(s, half)
+            if bank is not None:
+                sched_exit(bank)
+            if units and half == 0:
+                flow_scale_out(q + 1, 0)
+                flow_scale_out(q + 1, 1, 0, 1)
+            if units and half == 1:
+                flow_scale_out(q + 1, 1, 1, 2)
+                flow_scale_out(q + 1, 2)
+            if before:
+                for r in range(2):
+                    moves_scale(2 * before[0] + r, before[1])
+            if s == 0:
+                for c in range(A_PASSES):
+                    impact_quantize(c, 2)
+                    impact_quantize(c, 3)
+            if units:
+                for c in (0,) if half == 0 else (1, 2):
+                    flow_quantize(q + 1, c)
+            if bank is not None:
+                sched_quantize(bank)
+            if before:
+                moves_quantize(*before)
+            if chunk:
+                weighted_quantize(*chunk)
+            for r in range(2):
+                impact_matmul(2 * q + r, half)
+                saturate(2 * q + r, half)
+            if s >= 3:
+                hedge_matmul(s - 3)
+            if s == STEPS - 2:
+                for g in range(last):
+                    cost_matmul(0, 0, g)
 
-        last = TILES - 1
-        g = T_PASSES - 1
-        saturate(last, 0)
-        weigh(last, "D", 0, BANK)
-        saturate(last, 1)
-        moves_quantize(last - 2)
-        for i in (last - 1, last):
-            for half in range(N_PASSES):
-                moves_transpose(i, half)
-        weighted_interleave(g, 1, "A")
-        moves_scale(last - 1, 0)
-        weigh(last, "D", BANK, N)
-        moves_scale(last - 1, 1)
-        hedge_matmul(last - 3)
-        hedge_exit(last - 3, "A")
-        weighted_interleave(g, 0, "D")
-        moves_scale(last, 0)
-        moves_quantize(last - 1)
-        hedge_matmul(last - 2)
-        weighted_interleave(g, 3, "A")
-        hedge_exit(last - 2, "A")
-        cost_early(len(early))
-        weighted_quantize(g, 0)
-        moves_scale(last, 1)
-        weighted_quantize(g, 1)
-        weighted_interleave(g, 2, "D")
-        hedge_matmul(last - 1)
-        hedge_exit(last - 1, "A")
-        for g2 in range(T_PASSES - 1):
-            cost_matmul(1, 1, g2)
-        for qt in range(2):
-            cost_matmul(qt, 0, g)
-            cost_exit(qt, 0, "A")
-        moves_quantize(last)
-        weighted_quantize(g, 2)
-        weighted_quantize(g, 3)
-        hedge_matmul(last)
-        for qt in range(2):
-            cost_matmul(qt, 1, g)
-        hedge_exit(last, "A")
-        cost_exit(0, 1, "D")
-        cost_exit(1, 1, "D")
+        weighted_quantize(last, 1)
+        weigh_plane(2, "V")
+        weigh_plane(3, "V")
+        moves_transpose(TILES - 2, 1)
+        moves_transpose(TILES - 1, 1)
+        hedge_exit(TILES - 4)
+        planes_interleave(3, "S")
+        moves_scale(TILES - 2, 1)
+        moves_scale(TILES - 1, 1)
+        planes_interleave(2, "V")
+        moves_quantize(PAIRS - 1, 1)
+        weighted_quantize(last, 2)
+        weighted_quantize(last, 3)
+        cost_matmul(0, 0, last)
+        hedge_matmul(TILES - 3)
+        for g in range(T_PASSES):
+            cost_matmul(1, 0, g)
+        cost_exit(0, 0, "S")
+        hedge_exit(TILES - 3)
+        for g in range(last):
+            cost_matmul(0, 1, g)
+        for g in range(last):
+            cost_matmul(1, 1, g)
+        cost_exit(1, 0, "V")
+        hedge_matmul(TILES - 2, "ht")
+        cost_matmul(0, 1, last)
+        hedge_matmul(TILES - 1, "ht")
+        cost_matmul(1, 1, last)
+        hedge_exit(TILES - 2, "S")
+        cost_exit(0, 1, "V")
+        hedge_exit(TILES - 1, "S")
+        cost_exit(1, 1, "V")

@@ -133,7 +133,7 @@ def tile_cross_impact_hedge_s8_kernel(
             )
 
         def widen(i, engine="S"):
-            wide = work.tile([P, A], BF16, name=f"wide_{i}", tag="wide", bufs=5, align_bytes=64)
+            wide = work.tile([P, A], BF16, name=f"wide_{i}", tag="wide", bufs=4, align_bytes=64)
             tiles["wide", i] = wide
             src = flow_sb[i // 2][:, i % 2, :].bitcast(FP8)
             if engine == "S":
@@ -141,13 +141,23 @@ def tile_cross_impact_hedge_s8_kernel(
             else:
                 nc.vector.tensor_copy(out=wide[:], in_=src)
 
+        def regroup(i):
+            sorted_words = work.tile([P, A_PASSES, 2, P], F32, name=f"words_{i}", tag="words", bufs=4, align_bytes=64)
+            tiles["words", i] = sorted_words
+            words = tiles["wide", i][:].bitcast(F32)
+            nc.scalar.copy(out=sorted_words[:], in_=words.rearrange("p (c m u) -> p c u m", c=A_PASSES, u=2))
+
         def flow_transpose(q, c):
             bank = psum.tile([P, 2, 2, P], F32, name=f"xt_{q}_{c}", tag="xt", bufs=3)
             tiles["xt", q, c] = bank
             for r in range(2):
-                words = tiles["wide", 2 * q + r][:].bitcast(F32)
+                i = 2 * q + r
                 for u in range(2):
-                    nc.tensor.transpose(bank[:, u, r, :], words[:, 256 * c + u : 256 * (c + 1) : 2], ident[:])
+                    if ("words", i) in tiles:
+                        src = tiles["words", i][:, c, u, :]
+                    else:
+                        src = tiles["wide", i][:].bitcast(F32)[:, 256 * c + u : 256 * (c + 1) : 2]
+                    nc.tensor.transpose(bank[:, u, r, :], src, ident[:])
 
         def flow_scale_out(q, c, lo=0, hi=2):
             if lo == 0:
@@ -433,6 +443,7 @@ def tile_cross_impact_hedge_s8_kernel(
         for r in range(2):
             moves_scale(r, 0)
         moves_quantize(0, 0)
+        widen(6)
 
         last = T_PASSES - 1
         for s in range(2, STEPS):
@@ -458,7 +469,9 @@ def tile_cross_impact_hedge_s8_kernel(
             if s >= 4:
                 hedge_exit(s - 4)
             if s + 4 < TILES:
-                widen(s + 4)
+                regroup(s + 4)
+            if s + 5 < TILES:
+                widen(s + 5)
             if bank is not None:
                 sched_exit(bank)
             if units and half == 0:
@@ -505,22 +518,21 @@ def tile_cross_impact_hedge_s8_kernel(
         moves_quantize(PAIRS - 1, 1)
         weighted_quantize(last, 2)
         weighted_quantize(last, 3)
-        cost_matmul(0, 0, last)
         hedge_matmul(TILES - 3)
+        cost_matmul(0, 0, last)
         for g in range(T_PASSES):
             cost_matmul(1, 0, g)
-        cost_exit(0, 0, "S")
         hedge_exit(TILES - 3)
+        cost_exit(0, 0, "S")
         for g in range(last):
             cost_matmul(0, 1, g)
-        for g in range(last):
+        hedge_matmul(TILES - 2, "ht")
+        hedge_matmul(TILES - 1, "ht")
+        cost_matmul(0, 1, last)
+        for g in range(T_PASSES):
             cost_matmul(1, 1, g)
         cost_exit(1, 0, "V")
-        hedge_matmul(TILES - 2, "ht")
-        cost_matmul(0, 1, last)
-        hedge_matmul(TILES - 1, "ht")
-        cost_matmul(1, 1, last)
         hedge_exit(TILES - 2, "S")
-        cost_exit(0, 1, "V")
-        hedge_exit(TILES - 1, "S")
+        hedge_exit(TILES - 1, "V")
+        cost_exit(0, 1, "S")
         cost_exit(1, 1, "V")

@@ -62,7 +62,7 @@ def tile_cross_impact_hedge_s8_kernel(
         imp_raw = {}
         for c in range(A_PASSES):
             for half in range(N_PASSES):
-                t_i = keep.tile([P, PACK, BANK], BF16, name=f"imp_raw_{c}_{half}", align_bytes=64)
+                t_i = work.tile([P, PACK, BANK], BF16, name=f"imp_raw_{c}_{half}", tag="raw", bufs=6, align_bytes=64)
                 imp_raw[c, half] = t_i
 
         def load_impact(c, half):
@@ -72,7 +72,6 @@ def tile_cross_impact_hedge_s8_kernel(
         vol_sb = keep.tile([P, N_PASSES, PACK], BF16, name="vol_sb", align_bytes=64)
         depth_bf = keep.tile([P, T_PASSES, PACK], BF16, name="depth_bf", align_bytes=64)
         depth_sb = keep.tile([P, T_PASSES, PACK], F32, name="depth_sb", align_bytes=64)
-        planes = keep.tile([P, PACK, BANK], BF16, name="planes", align_bytes=64)
         w_words = keep.tile([P, N_PASSES, 2 * R], U8, name="w_words", align_bytes=64)
         sched_sb = []
         for qt in range(2):
@@ -213,44 +212,35 @@ def tile_cross_impact_hedge_s8_kernel(
                 func=TANH,
             )
 
-        def weigh(g, ch, engine):
+        def weigh(g, ch):
             half, lo = divmod(ch * CH, BANK)
-            grouped = work.tile(
-                [P, CH, PACK], BF16, name=f"wg_{g}_{ch}", tag="wg" + engine, bufs=1 if engine == "G" else 2, align_bytes=64
-            )
+            grouped = work.tile([P, CH, PACK], BF16, name=f"wg_{g}_{ch}", tag="wg", bufs=1, align_bytes=64)
             tiles["wg", g, ch] = grouped
-            src = tiles["h", g, half][:, :, lo : lo + CH]
-            if engine == "G":
-                nc.gpsimd.tensor_tensor(
-                    out=grouped[:],
-                    in0=src.rearrange("p j n -> p n j"),
-                    in1=depth_sb[:, g, :].unsqueeze(1).to_broadcast([P, CH, PACK]),
-                    op=MULT,
-                )
-            else:
-                nc.vector.tensor_tensor(
-                    out=grouped[:].rearrange("p (n i) j -> p n j i", i=4),
-                    in0=src.rearrange("p j (n i) -> p n j i", i=4),
-                    in1=depth_sb[:, g, :].unsqueeze(1).unsqueeze(3).to_broadcast([P, CH // 4, PACK, 4]),
-                    op=MULT,
-                )
+            nc.gpsimd.tensor_tensor(
+                out=grouped[:],
+                in0=tiles["h", g, half][:, :, lo : lo + CH].rearrange("p j n -> p n j"),
+                in1=depth_sb[:, g, :].unsqueeze(1).to_broadcast([P, CH, PACK]),
+                op=MULT,
+            )
 
-        def weigh_plane(j, engine):
+        def weigh_plane(half, j, engine):
             g = T_PASSES - 1
-            src = tiles["h", g, 1][:, j, :]
+            if j == 0:
+                planes = work.tile([P, PACK, BANK], BF16, name=f"planes_{half}", tag="raw", bufs=6, align_bytes=64)
+                tiles["planes", half] = planes
+            dst = tiles["planes", half][:, j, :]
+            src = tiles["h", g, half][:, j, :]
             if engine == "S":
-                nc.scalar.activation(out=planes[:, j, :], in_=src, func=COPY, scale=depth_sb[:, g, j : j + 1])
+                nc.scalar.activation(out=dst, in_=src, func=COPY, scale=depth_sb[:, g, j : j + 1])
             else:
-                nc.vector.tensor_scalar(
-                    out=planes[:, j, :], in0=src, scalar1=depth_sb[:, g, j : j + 1], scalar2=None, op0=MULT
-                )
+                nc.vector.tensor_scalar(out=dst, in0=src, scalar1=depth_sb[:, g, j : j + 1], scalar2=None, op0=MULT)
 
         def planes_interleave(ch, engine):
             grouped = work.tile([P, CH, PACK], BF16, name=f"wg_last_{ch}", tag="ig", bufs=6, align_bytes=64)
             tiles["wg", T_PASSES - 1, ch] = grouped
-            lo = ch * CH - BANK
+            half, lo = divmod(ch * CH, BANK)
             dst = grouped[:].rearrange("p (n i) t -> p n t i", i=4)
-            src = planes[:, :, lo : lo + CH].rearrange("p t (n i) -> p n t i", i=4)
+            src = tiles["planes", half][:, :, lo : lo + CH].rearrange("p t (n i) -> p n t i", i=4)
             if engine == "S":
                 nc.scalar.copy(out=dst, in_=src)
             else:
@@ -450,52 +440,47 @@ def tile_cross_impact_hedge_s8_kernel(
             q, half = divmod(s, 2)
             units = [(q + 1, c) for c in ((0, 1) if half == 0 else (2,))] if q + 1 < PAIRS else []
             bank = (s - 7) // 2 if half == 1 and 7 <= s <= 13 else None
-            before = divmod(s - 1, 2) if s >= 1 else None
-            chunk = divmod(s - 3, PACK) if s >= 3 else None
-            if chunk and s < STEPS - 1:
-                weigh(*chunk, "G")
-            if s == STEPS - 1:
-                weigh(last, 0, "V")
-                weigh(last, 1, "V")
-                weigh_plane(0, "S")
-                weigh_plane(1, "S")
+            before = divmod(s - 1, 2)
+            chunk = divmod(s - 3, PACK) if 3 <= s < STEPS - 1 else None
+            if chunk:
+                weigh(*chunk)
+            if units and half == 1:
+                flow_scale_out(q + 1, 1, 1, 2)
             for unit in units:
                 flow_transpose(*unit)
             if bank is not None:
                 sched_transpose(bank)
-            if before:
-                for r in range(2):
-                    moves_transpose(2 * before[0] + r, before[1])
+            for r in range(2):
+                moves_transpose(2 * before[0] + r, before[1])
             if s >= 4:
                 hedge_exit(s - 4)
             if s + 4 < TILES:
                 regroup(s + 4)
             if s + 5 < TILES:
                 widen(s + 5)
+            if before[0] >= PAIRS - 2:
+                for r in range(2):
+                    weigh_plane(before[1], 2 * (before[0] % 2) + r, "S")
             if bank is not None:
                 sched_exit(bank)
             if units and half == 0:
                 flow_scale_out(q + 1, 0)
                 flow_scale_out(q + 1, 1, 0, 1)
             if units and half == 1:
-                flow_scale_out(q + 1, 1, 1, 2)
                 flow_scale_out(q + 1, 2)
-            if before:
-                for r in range(2):
-                    moves_scale(2 * before[0] + r, before[1])
-            if s == 0:
-                for c in range(A_PASSES):
-                    impact_quantize(c, 2)
-                    impact_quantize(c, 3)
+            for r in range(2):
+                moves_scale(2 * before[0] + r, before[1])
+            if s == STEPS - 1:
+                planes_interleave(0, "V")
+                planes_interleave(1, "V")
             if units:
                 for c in (0,) if half == 0 else (1, 2):
                     flow_quantize(q + 1, c)
             if bank is not None:
                 sched_quantize(bank)
-            if before:
-                moves_quantize(*before)
             if chunk:
                 weighted_quantize(*chunk)
+            moves_quantize(*before)
             for r in range(2):
                 impact_matmul(2 * q + r, half)
                 saturate(2 * q + r, half)
@@ -505,9 +490,10 @@ def tile_cross_impact_hedge_s8_kernel(
                 for g in range(last):
                     cost_matmul(0, 0, g)
 
+        weighted_quantize(last, 0)
         weighted_quantize(last, 1)
-        weigh_plane(2, "V")
-        weigh_plane(3, "V")
+        weigh_plane(1, 2, "V")
+        weigh_plane(1, 3, "V")
         moves_transpose(TILES - 2, 1)
         moves_transpose(TILES - 1, 1)
         hedge_exit(TILES - 4)

@@ -223,24 +223,23 @@ def tile_cross_impact_hedge_s8_kernel(
                 op=MULT,
             )
 
-        def weigh_plane(half, j, engine):
-            g = T_PASSES - 1
+        def weigh_plane(g, half, j, engine, lo=0):
             if j == 0:
-                planes = work.tile([P, PACK, BANK], BF16, name=f"planes_{half}", tag="raw", bufs=6, align_bytes=64)
-                tiles["planes", half] = planes
-            dst = tiles["planes", half][:, j, :]
-            src = tiles["h", g, half][:, j, :]
+                planes = work.tile([P, PACK, BANK], BF16, name=f"planes_{g}_{half}", tag="raw", bufs=6, align_bytes=64)
+                tiles["planes", g, half] = planes
+            dst = tiles["planes", g, half][:, j, lo:]
+            src = tiles["h", g, half][:, j, lo:]
             if engine == "S":
                 nc.scalar.activation(out=dst, in_=src, func=COPY, scale=depth_sb[:, g, j : j + 1])
             else:
                 nc.vector.tensor_scalar(out=dst, in0=src, scalar1=depth_sb[:, g, j : j + 1], scalar2=None, op0=MULT)
 
-        def planes_interleave(ch, engine):
-            grouped = work.tile([P, CH, PACK], BF16, name=f"wg_last_{ch}", tag="ig", bufs=6, align_bytes=64)
-            tiles["wg", T_PASSES - 1, ch] = grouped
+        def planes_interleave(g, ch, engine):
+            grouped = work.tile([P, CH, PACK], BF16, name=f"wp_{g}_{ch}", tag="ig", bufs=6, align_bytes=64)
+            tiles["wg", g, ch] = grouped
             half, lo = divmod(ch * CH, BANK)
             dst = grouped[:].rearrange("p (n i) t -> p n t i", i=4)
-            src = tiles["planes", half][:, :, lo : lo + CH].rearrange("p t (n i) -> p n t i", i=4)
+            src = tiles["planes", g, half][:, :, lo : lo + CH].rearrange("p t (n i) -> p n t i", i=4)
             if engine == "S":
                 nc.scalar.copy(out=dst, in_=src)
             else:
@@ -283,35 +282,34 @@ def tile_cross_impact_hedge_s8_kernel(
                 in_=tiles.pop(("mg", q, half))[:].rearrange("p r m t -> p (r m t)"),
             )
 
-        def hedge_matmul(i, tag="hg", halves=(0, 1)):
+        def hedge_matmul(i, tag="hg", lo=0, hi=R, width=R):
             q, r = divmod(i, 2)
-            if halves[0] == 0:
-                bank = psum.tile([P, R], F32, name=f"hg_{i}", tag=tag, bufs=1 if tag == "hg" else 2)
-                tiles["hg", i] = bank
-            bank = tiles["hg", i]
-            for half in halves:
-                codes, scales = tiles["mc", q, half]
-                nc.tensor.matmul_mx(
-                    out=bank[:],
-                    lhsT=codes[:, r * P : (r + 1) * P].bitcast(FP8X4),
-                    lhsT_scale=scales[:, r * P : (r + 1) * P],
-                    rhs=w_words[:, half, :].bitcast(FP4X4),
-                    rhs_scale=w_scales[:, half, :],
-                    start=(half == 0),
-                    stop=(half == N_PASSES - 1),
-                )
+            bank = psum.tile([P, hi - lo], F32, name=f"hg_{i}_{lo}", tag=tag, bufs={"hg": 1, "xt": 3}.get(tag, 2))
+            tiles["hg", i, lo] = bank
+            for c0 in range(lo, hi, width):
+                for half in range(N_PASSES):
+                    codes, scales = tiles["mc", q, half]
+                    nc.tensor.matmul_mx(
+                        out=bank[:, c0 - lo : c0 - lo + width],
+                        lhsT=codes[:, r * P : (r + 1) * P].bitcast(FP8X4),
+                        lhsT_scale=scales[:, r * P : (r + 1) * P],
+                        rhs=w_words[:, half, 2 * c0 : 2 * (c0 + width)].bitcast(FP4X4),
+                        rhs_scale=w_scales[:, half, c0 : c0 + width],
+                        start=(half == 0),
+                        stop=(half == N_PASSES - 1),
+                    )
 
         hedge_view = hedge.rearrange("(g p j) r -> g j p r", p=P, j=PACK)
 
-        def hedge_exit(i, engine="S"):
+        def hedge_exit(i, engine="S", lo=0, hi=R):
             g, j = divmod(i, PACK)
-            res = work.tile([P, R], F32, name=f"hr_{i}", tag="hr", bufs=3, align_bytes=64)
-            bank = tiles.pop(("hg", i))
+            res = work.tile([P, hi - lo], F32, name=f"hr_{i}_{lo}", tag="hr", bufs=4, align_bytes=64)
+            bank = tiles.pop(("hg", i, lo))
             if engine == "S":
                 nc.scalar.copy(out=res[:], in_=bank[:])
             else:
                 nc.vector.tensor_copy(out=res[:], in_=bank[:])
-            nc.sync.dma_start(out=hedge_view[g, j], in_=res[:])
+            nc.sync.dma_start(out=hedge_view[g, j][:, lo:hi], in_=res[:])
 
         def sched_transpose(b):
             qt, gp = divmod(b, 2)
@@ -324,7 +322,7 @@ def tile_cross_impact_hedge_s8_kernel(
                     nc.tensor.transpose(bank[:, s, u, :], words[:, 256 * g + u : 256 * (g + 1) : 2], ident[:])
 
         def sched_exit(b):
-            grouped = work.tile([P, 2, P, PACK], BF16, name=f"sg_{b}", tag="sg", bufs=2, align_bytes=64)
+            grouped = work.tile([P, 2, P, PACK], BF16, name=f"sg_{b}", tag="sg", bufs=4, align_bytes=64)
             tiles["sg", b] = grouped
             words = grouped[:].rearrange("p s q t -> p (s q t)").bitcast(F32)
             nc.scalar.copy(
@@ -340,10 +338,9 @@ def tile_cross_impact_hedge_s8_kernel(
                 in_=tiles.pop(("sg", b))[:].rearrange("p s q t -> p (s q t)"),
             )
 
-        def cost_matmul(qt, half, g):
-            if g == 0:
-                last = (qt, half) == (1, 1)
-                bank = psum.tile([P, BANK], F32, name=f"cost_{qt}_{half}", tag="z" if last else "xt", bufs=2 if last else 3)
+        def cost_matmul(qt, half, g, tag=None):
+            if tag:
+                bank = psum.tile([P, BANK], F32, name=f"cost_{qt}_{half}", tag=tag, bufs={"hg": 1, "xt": 3}.get(tag, 2))
                 tiles["cb", qt, half] = bank
             cols = slice(half * BANK, (half + 1) * BANK)
             nc.tensor.matmul_mx(
@@ -442,9 +439,9 @@ def tile_cross_impact_hedge_s8_kernel(
             bank = (s - 7) // 2 if half == 1 and 7 <= s <= 13 else None
             before = divmod(s - 1, 2)
             chunk = divmod(s - 3, PACK) if 3 <= s < STEPS - 1 else None
-            if chunk:
+            if chunk and units:
                 weigh(*chunk)
-            if units and half == 1:
+            if units and half == 1 and s < 13:
                 flow_scale_out(q + 1, 1, 1, 2)
             for unit in units:
                 flow_transpose(*unit)
@@ -454,30 +451,40 @@ def tile_cross_impact_hedge_s8_kernel(
                 moves_transpose(2 * before[0] + r, before[1])
             if s >= 4:
                 hedge_exit(s - 4)
-            if s + 4 < TILES:
+            if 7 <= s + 4 < TILES:
                 regroup(s + 4)
             if s + 5 < TILES:
                 widen(s + 5)
+            if s == STEPS - 4:
+                for j in range(PACK):
+                    weigh_plane(last - 1, 1, j, "S", CH)
+                planes_interleave(last - 1, 3, "S")
             if before[0] >= PAIRS - 2:
                 for r in range(2):
-                    weigh_plane(before[1], 2 * (before[0] % 2) + r, "S")
+                    weigh_plane(last, before[1], 2 * (before[0] % 2) + r, "S")
             if bank is not None:
                 sched_exit(bank)
+            if s >= 13:
+                for r in range(2):
+                    moves_scale(2 * before[0] + r, before[1])
+            if units and half == 1 and s >= 13:
+                flow_scale_out(q + 1, 1, 1, 2)
             if units and half == 0:
                 flow_scale_out(q + 1, 0)
                 flow_scale_out(q + 1, 1, 0, 1)
             if units and half == 1:
                 flow_scale_out(q + 1, 2)
-            for r in range(2):
+            for r in range(2) if s < 13 else []:
                 moves_scale(2 * before[0] + r, before[1])
             if s == STEPS - 1:
-                planes_interleave(0, "V")
-                planes_interleave(1, "V")
+                planes_interleave(last, 0, "V")
+                planes_interleave(last, 1, "V")
             if units:
                 for c in (0,) if half == 0 else (1, 2):
                     flow_quantize(q + 1, c)
-            if bank is not None:
-                sched_quantize(bank)
+            if s == STEPS - 2:
+                for b in range(4):
+                    sched_quantize(b)
             if chunk:
                 weighted_quantize(*chunk)
             moves_quantize(*before)
@@ -486,37 +493,34 @@ def tile_cross_impact_hedge_s8_kernel(
                 saturate(2 * q + r, half)
             if s >= 3:
                 hedge_matmul(s - 3)
-            if s == STEPS - 2:
-                for g in range(last):
-                    cost_matmul(0, 0, g)
 
         weighted_quantize(last, 0)
         weighted_quantize(last, 1)
-        weigh_plane(1, 2, "V")
-        weigh_plane(1, 3, "V")
+        weigh_plane(last, 1, 2, "S")
+        weigh_plane(last, 1, 3, "S")
         moves_transpose(TILES - 2, 1)
         moves_transpose(TILES - 1, 1)
-        hedge_exit(TILES - 4)
-        planes_interleave(3, "S")
         moves_scale(TILES - 2, 1)
         moves_scale(TILES - 1, 1)
-        planes_interleave(2, "V")
+        hedge_exit(TILES - 4)
+        planes_interleave(last, 3, "S")
+        planes_interleave(last, 2, "V")
         moves_quantize(PAIRS - 1, 1)
         weighted_quantize(last, 2)
         weighted_quantize(last, 3)
-        hedge_matmul(TILES - 3)
-        cost_matmul(0, 0, last)
-        for g in range(T_PASSES):
-            cost_matmul(1, 0, g)
-        hedge_exit(TILES - 3)
-        cost_exit(0, 0, "S")
+        hedge_matmul(TILES - 3, "z")
+        for qt in range(2):
+            for g in range(T_PASSES):
+                cost_matmul(qt, 0, g, None if g else "xt")
         for g in range(last):
-            cost_matmul(0, 1, g)
+            cost_matmul(0, 1, g, None if g else "xt")
         hedge_matmul(TILES - 2, "ht")
         hedge_matmul(TILES - 1, "ht")
         cost_matmul(0, 1, last)
         for g in range(T_PASSES):
-            cost_matmul(1, 1, g)
+            cost_matmul(1, 1, g, None if g else "z")
+        hedge_exit(TILES - 3, "S")
+        cost_exit(0, 0, "S")
         cost_exit(1, 0, "V")
         hedge_exit(TILES - 2, "S")
         hedge_exit(TILES - 1, "V")

@@ -451,7 +451,7 @@ def tile_cross_impact_hedge_s8_kernel(
                 moves_transpose(2 * before[0] + r, before[1])
             if s >= 4:
                 hedge_exit(s - 4)
-            if 7 <= s + 4 < TILES:
+            if 8 <= s + 4 < TILES and s % 2 == 0:
                 regroup(s + 4)
             if s + 5 < TILES:
                 widen(s + 5)

@@ -51,12 +51,16 @@ def tile_cross_impact_hedge_s8_kernel(
         flow_view = flow_bytes.rearrange("(g p j) a -> g p j a", p=P, j=PACK)
         flow_sb = []
         for q in range(PAIRS):
-            t_f = keep.tile([P, 2, A], U8, name=f"flow_{q}", align_bytes=64)
+            t_f = keep.tile([P, 2, A if q else A - K_PASS], U8, name=f"flow_{q}", align_bytes=64)
             flow_sb.append(t_f)
+        flow_first = keep.tile([P, 2, K_PASS], U8, name="flow_first", align_bytes=64)
+
+        def load_first():
+            nc.sync.dma_start(out=flow_first[:], in_=flow_view[0, :, 0:2, 0:K_PASS])
 
         def load_flow(q):
             g, r = divmod(q, 2)
-            nc.sync.dma_start(out=flow_sb[q][:], in_=flow_view[g, :, 2 * r : 2 * r + 2, :])
+            nc.sync.dma_start(out=flow_sb[q][:], in_=flow_view[g, :, 2 * r : 2 * r + 2, 0 if q else K_PASS :])
 
         imp_view = impact.rearrange("(c p t) n -> c p t n", p=P, t=PACK)
         imp_raw = {}
@@ -72,6 +76,7 @@ def tile_cross_impact_hedge_s8_kernel(
         vol_sb = keep.tile([P, N_PASSES, PACK], BF16, name="vol_sb", align_bytes=64)
         depth_bf = keep.tile([P, T_PASSES, PACK], BF16, name="depth_bf", align_bytes=64)
         depth_sb = keep.tile([P, T_PASSES, PACK], F32, name="depth_sb", align_bytes=64)
+        vol_f32 = keep.tile([P, N_PASSES, PACK], F32, name="vol_f32", align_bytes=64)
         w_words = keep.tile([P, N_PASSES, 2 * R], U8, name="w_words", align_bytes=64)
         sched_sb = []
         for qt in range(2):
@@ -131,14 +136,16 @@ def tile_cross_impact_hedge_s8_kernel(
                 in_=tiles.pop(("ig", c, ch))[:].rearrange("p n t -> p (n t)"),
             )
 
-        def widen(i, engine="S"):
-            wide = work.tile([P, A], BF16, name=f"wide_{i}", tag="wide", bufs=4, align_bytes=64)
-            tiles["wide", i] = wide
-            src = flow_sb[i // 2][:, i % 2, :].bitcast(FP8)
+        def widen(i, engine="S", lo=0, hi=A):
+            if lo == 0:
+                wide = work.tile([P, A], BF16, name=f"wide_{i}", tag="wide", bufs=4, align_bytes=64)
+                tiles["wide", i] = wide
+            q, r = divmod(i, 2)
+            src = flow_first[:, r, :] if hi < A else flow_sb[q][:, r, :]
             if engine == "S":
-                nc.scalar.copy(out=wide[:], in_=src)
+                nc.scalar.copy(out=tiles["wide", i][:, lo:hi], in_=src.bitcast(FP8))
             else:
-                nc.vector.tensor_copy(out=wide[:], in_=src)
+                nc.vector.tensor_copy(out=tiles["wide", i][:, lo:hi], in_=src.bitcast(FP8))
 
         def regroup(i):
             sorted_words = work.tile([P, A_PASSES, 2, P], F32, name=f"words_{i}", tag="words", bufs=4, align_bytes=64)
@@ -262,7 +269,7 @@ def tile_cross_impact_hedge_s8_kernel(
 
         def moves_scale(i, half):
             q, r = divmod(i, 2)
-            if r == 0:
+            if ("mg", q, half) not in tiles:
                 grouped = work.tile([P, 2, P, PACK], BF16, name=f"mg_{q}_{half}", tag="mg", bufs=3, align_bytes=64)
                 tiles["mg", q, half] = grouped
             nc.vector.tensor_tensor(
@@ -270,6 +277,22 @@ def tile_cross_impact_hedge_s8_kernel(
                 in0=tiles.pop(("ht", i, half))[:].rearrange("p t m -> p m t"),
                 in1=vol_sb[:, half, :].unsqueeze(1).to_broadcast([P, P, PACK]),
                 op=MULT,
+            )
+
+        def moves_planes(i, half):
+            planes = work.tile([P, PACK, P], BF16, name=f"mp_{i}_{half}", tag="mp", bufs=2, align_bytes=64)
+            tiles["mp", i, half] = planes
+            bank = tiles.pop(("ht", i, half))
+            for t in range(PACK):
+                nc.scalar.activation(out=planes[:, t, :], in_=bank[:, t, :], func=COPY, scale=vol_f32[:, half, t : t + 1])
+
+        def moves_interleave(i, half):
+            q, r = divmod(i, 2)
+            grouped = work.tile([P, 2, P, PACK], BF16, name=f"mg_{q}_{half}", tag="mg", bufs=3, align_bytes=64)
+            tiles["mg", q, half] = grouped
+            nc.scalar.copy(
+                out=grouped[:, r, :, :].rearrange("p (m i) t -> p m t i", i=4),
+                in_=tiles.pop(("mp", i, half))[:].rearrange("p t (m i) -> p m t i", i=4),
             )
 
         def moves_quantize(q, half):
@@ -311,10 +334,10 @@ def tile_cross_impact_hedge_s8_kernel(
                 nc.vector.tensor_copy(out=res[:], in_=bank[:])
             nc.sync.dma_start(out=hedge_view[g, j][:, lo:hi], in_=res[:])
 
-        def sched_transpose(b):
+        def sched_transpose(b, tag="xt"):
             qt, gp = divmod(b, 2)
             words = sched_sb[qt][:].bitcast(F32)
-            bank = psum.tile([P, 2, 2, P], F32, name=f"st_{b}", tag="xt", bufs=3)
+            bank = psum.tile([P, 2, 2, P], F32, name=f"st_{b}", tag=tag, bufs=3 if tag == "xt" else 1)
             tiles["st", b] = bank
             for s in range(2):
                 g = 2 * gp + s
@@ -365,6 +388,7 @@ def tile_cross_impact_hedge_s8_kernel(
 
         load_scale()
         load_depth()
+        load_first()
         load_flow(0)
         load_impact(0, 0)
         load_impact(1, 0)
@@ -373,30 +397,33 @@ def tile_cross_impact_hedge_s8_kernel(
         load_impact(0, 1)
         load_impact(1, 1)
         load_impact(2, 1)
+        load_sched(0)
         load_flow(2)
         load_vol()
         load_sens()
         load_flow(3)
         load_flow(4)
-        load_sched(0)
         load_sched(1)
         for q in range(5, PAIRS):
             load_flow(q)
 
-        widen(0, "V")
-        widen(1, "S")
-        for c in range(A_PASSES):
-            flow_transpose(0, c)
+        widen(0, "V", 0, K_PASS)
+        widen(1, "S", 0, K_PASS)
+        flow_transpose(0, 0)
+        widen(0, "V", K_PASS)
+        widen(1, "S", K_PASS)
+        flow_transpose(0, 1)
+        flow_transpose(0, 2)
         impact_interleave(0, 0, "S")
-        impact_interleave(0, 1, "V")
+        impact_interleave(0, 1, "G")
         impact_interleave(1, 0, "S")
         impact_interleave(1, 1, "G")
         impact_interleave(2, 0, "S")
-        impact_interleave(2, 1, "G")
         widen(2)
         widen(3)
         for c in range(A_PASSES):
             flow_scale_out(0, c)
+        impact_interleave(2, 1, "V")
         for c in range(A_PASSES):
             flow_transpose(1, c)
         for c in range(A_PASSES):
@@ -412,11 +439,14 @@ def tile_cross_impact_hedge_s8_kernel(
             flow_scale_out(1, c)
         for r in range(2):
             impact_matmul(r, 0)
+        sched_transpose(0, "hg")
+        sched_transpose(1)
         impact_interleave(2, 3, "S")
         for r in range(2):
             saturate(r, 0)
         widen(4)
         widen(5)
+        sched_exit(1)
         for c in range(A_PASSES):
             impact_quantize(c, 2)
             impact_quantize(c, 3)
@@ -433,54 +463,69 @@ def tile_cross_impact_hedge_s8_kernel(
         widen(6)
 
         last = T_PASSES - 1
+        nc.scalar.copy(out=vol_f32[:], in_=vol_sb[:])
         for s in range(2, STEPS):
             q, half = divmod(s, 2)
             units = [(q + 1, c) for c in ((0, 1) if half == 0 else (2,))] if q + 1 < PAIRS else []
-            bank = (s - 7) // 2 if half == 1 and 7 <= s <= 13 else None
+            bank = {11: 2, 13: 3}.get(s)
             before = divmod(s - 1, 2)
+            first, second = 2 * before[0], 2 * before[0] + 1
             chunk = divmod(s - 3, PACK) if 3 <= s < STEPS - 1 else None
+            shared = half == 0 and 4 <= s <= 10
+            split = units and not (4 <= s - half <= 10)
             if chunk and units:
                 weigh(*chunk)
-            if units and half == 1 and s < 13:
+            if split and half == 1:
                 flow_scale_out(q + 1, 1, 1, 2)
+            if shared:
+                moves_transpose(first, before[1])
             for unit in units:
                 flow_transpose(*unit)
             if bank is not None:
                 sched_transpose(bank)
-            for r in range(2):
-                moves_transpose(2 * before[0] + r, before[1])
+            if not shared:
+                moves_transpose(first, before[1])
+            moves_transpose(second, before[1])
             if s >= 4:
                 hedge_exit(s - 4)
-            if 8 <= s + 4 < TILES and s % 2 == 0:
+            if shared:
+                moves_planes(first, before[1])
+            if 7 <= s + 4 < TILES and (s % 2 == 1 or s > 10):
                 regroup(s + 4)
+            if shared and not (s + 5 < TILES):
+                moves_interleave(first, before[1])
             if s + 5 < TILES:
                 widen(s + 5)
-            if s == STEPS - 4:
+                if shared:
+                    moves_interleave(first, before[1])
+            if s == 12:
                 for j in range(PACK):
                     weigh_plane(last - 1, 1, j, "S", CH)
                 planes_interleave(last - 1, 3, "S")
             if before[0] >= PAIRS - 2:
                 for r in range(2):
                     weigh_plane(last, before[1], 2 * (before[0] % 2) + r, "S")
+            if s == 2 and True:
+                sched_exit(0)
             if bank is not None:
                 sched_exit(bank)
-            if s >= 13:
-                for r in range(2):
-                    moves_scale(2 * before[0] + r, before[1])
-            if units and half == 1 and s >= 13:
-                flow_scale_out(q + 1, 1, 1, 2)
+            if s >= STEPS - 3:
+                moves_scale(first, before[1])
+                moves_scale(second, before[1])
             if units and half == 0:
                 flow_scale_out(q + 1, 0)
-                flow_scale_out(q + 1, 1, 0, 1)
+                flow_scale_out(q + 1, 1, 0, 1 if split else 2)
             if units and half == 1:
                 flow_scale_out(q + 1, 2)
-            for r in range(2) if s < 13 else []:
-                moves_scale(2 * before[0] + r, before[1])
+            if s < STEPS - 3:
+                if not shared:
+                    moves_scale(first, before[1])
+                moves_scale(second, before[1])
             if s == STEPS - 1:
                 planes_interleave(last, 0, "V")
                 planes_interleave(last, 1, "V")
             if units:
-                for c in (0,) if half == 0 else (1, 2):
+                for c in (((0,), (1, 2)) if split else ((0, 1), (2,)))[half]:
                     flow_quantize(q + 1, c)
             if s == STEPS - 2:
                 for b in range(4):
@@ -510,8 +555,10 @@ def tile_cross_impact_hedge_s8_kernel(
         weighted_quantize(last, 3)
         hedge_matmul(TILES - 3, "z")
         for qt in range(2):
-            for g in range(T_PASSES):
+            for g in range(last):
                 cost_matmul(qt, 0, g, None if g else "xt")
+        for qt in range(2):
+            cost_matmul(qt, 0, last)
         for g in range(last):
             cost_matmul(0, 1, g, None if g else "xt")
         hedge_matmul(TILES - 2, "ht")
@@ -521,8 +568,8 @@ def tile_cross_impact_hedge_s8_kernel(
             cost_matmul(1, 1, g, None if g else "z")
         hedge_exit(TILES - 3, "S")
         cost_exit(0, 0, "S")
-        cost_exit(1, 0, "V")
-        hedge_exit(TILES - 2, "S")
-        hedge_exit(TILES - 1, "V")
-        cost_exit(0, 1, "S")
-        cost_exit(1, 1, "V")
+        cost_exit(1, 0, "S")
+        hedge_exit(TILES - 2, "V")
+        hedge_exit(TILES - 1, "S")
+        cost_exit(0, 1, "V")
+        cost_exit(1, 1, "S")

@@ -30,7 +30,13 @@ TILES = T // P
 PAIRS = TILES // 2
 STEPS = PAIRS * N_PASSES
 BANK = 512
-CH = 256
+CHUNK = 256
+SCALAR, VECTOR, GPSIMD = "scalar", "vector", "gpsimd"
+
+PSUM_BUFS = {"z": 2, "turned_h": 2, "turned_x": 3, "hedge": 1}
+SHARED_STEPS = (4, 6, 8, 10)
+FIRST_SORTED = 7
+SCHED_SORT_STEP = 11
 
 
 def tile_cross_impact_hedge_s8_kernel(
@@ -51,12 +57,9 @@ def tile_cross_impact_hedge_s8_kernel(
         flow_view = flow_bytes.rearrange("(g p j) a -> g p j a", p=P, j=PACK)
         flow_sb = []
         for q in range(PAIRS):
-            t_f = keep.tile([P, 2, A if q else A - K_PASS], U8, name=f"flow_{q}", align_bytes=64)
-            flow_sb.append(t_f)
+            pair_bytes = keep.tile([P, 2, A if q else A - K_PASS], U8, name=f"flow_{q}", align_bytes=64)
+            flow_sb.append(pair_bytes)
         flow_first = keep.tile([P, 2, K_PASS], U8, name="flow_first", align_bytes=64)
-
-        def load_first():
-            nc.sync.dma_start(out=flow_first[:], in_=flow_view[0, :, 0:2, 0:K_PASS])
 
         def load_flow(q):
             g, r = divmod(q, 2)
@@ -66,38 +69,29 @@ def tile_cross_impact_hedge_s8_kernel(
         imp_raw = {}
         for c in range(A_PASSES):
             for half in range(N_PASSES):
-                t_i = work.tile([P, PACK, BANK], BF16, name=f"imp_raw_{c}_{half}", tag="raw", bufs=6, align_bytes=64)
-                imp_raw[c, half] = t_i
+                rows = work.tile([P, PACK, BANK], BF16, name=f"imp_raw_{c}_{half}", tag="raw", bufs=6, align_bytes=64)
+                imp_raw[c, half] = rows
 
-        def load_impact(c, half):
-            nc.sync.dma_start(out=imp_raw[c, half][:], in_=imp_view[c, :, :, half * BANK : (half + 1) * BANK])
+        def load_impact(half):
+            for c in range(A_PASSES):
+                nc.sync.dma_start(out=imp_raw[c, half][:], in_=imp_view[c, :, :, half * BANK : (half + 1) * BANK])
 
         scale_sb = keep.tile([P, A_PASSES, PACK], F32, name="scale_sb", align_bytes=64)
-        vol_sb = keep.tile([P, N_PASSES, PACK], BF16, name="vol_sb", align_bytes=64)
+        vol_bf = keep.tile([P, N_PASSES, PACK], BF16, name="vol_bf", align_bytes=64)
         depth_bf = keep.tile([P, T_PASSES, PACK], BF16, name="depth_bf", align_bytes=64)
-        depth_sb = keep.tile([P, T_PASSES, PACK], F32, name="depth_sb", align_bytes=64)
+        depth_f32 = keep.tile([P, T_PASSES, PACK], F32, name="depth_f32", align_bytes=64)
         vol_f32 = keep.tile([P, N_PASSES, PACK], F32, name="vol_f32", align_bytes=64)
         w_words = keep.tile([P, N_PASSES, 2 * R], U8, name="w_words", align_bytes=64)
         sched_sb = []
-        for qt in range(2):
-            t_s = keep.tile([P, T], BF16, name=f"sched_{qt}", align_bytes=64)
-            sched_sb.append(t_s)
-
-        def load_scale():
-            nc.scalar.dma_start(out=scale_sb[:], in_=flow_scale.rearrange("o (c p t) -> p (o c) t", p=P, t=PACK))
-
-        def load_depth():
-            nc.scalar.dma_start(out=depth_bf[:], in_=depth.rearrange("(g p j) -> p g j", p=P, j=PACK))
-            nc.scalar.activation(out=depth_sb[:], in_=depth_bf[:], func=COPY)
-
-        def load_vol():
-            nc.sync.dma_start(out=vol_sb[:], in_=vol.rearrange("(g p j) -> p g j", p=P, j=PACK))
+        for qt in range(Q // P):
+            rows = keep.tile([P, T], BF16, name=f"sched_{qt}", align_bytes=64)
+            sched_sb.append(rows)
 
         def load_sens():
-            for q4 in range(4):
+            for quad in range(4):
                 nc.sync.dma_start(
-                    out=w_scales[32 * q4 : 32 * q4 + 4, :, :].bitcast(I32),
-                    in_=sens_scales[:, 4 * q4 : 4 * q4 + 4, :].rearrange("g r n -> r g n").bitcast(I32),
+                    out=w_scales[32 * quad : 32 * quad + 4, :, :].bitcast(I32),
+                    in_=sens_scales[:, 4 * quad : 4 * quad + 4, :].rearrange("g r n -> r g n").bitcast(I32),
                 )
             nc.sync.dma_start(out=w_words[:].bitcast(I32), in_=sens_words.rearrange("g p b -> p g b").bitcast(I32))
 
@@ -108,105 +102,120 @@ def tile_cross_impact_hedge_s8_kernel(
         imp_scales = keep.tile([P, A_PASSES, N], U8, name="imp_scales", align_bytes=64)
         wt_codes = keep.tile([P, T_PASSES, N], U32, name="wt_codes", align_bytes=64)
         wt_scales = keep.tile([P, T_PASSES, N], U8, name="wt_scales", align_bytes=64)
-        sch_codes = keep.tile([P, 2, T_PASSES, P], U32, name="sch_codes", align_bytes=64)
-        sch_scales = keep.tile([P, 2, T_PASSES, P], U8, name="sch_scales", align_bytes=64)
+        sch_codes = keep.tile([P, Q // P, T_PASSES, P], U32, name="sch_codes", align_bytes=64)
+        sch_scales = keep.tile([P, Q // P, T_PASSES, P], U8, name="sch_scales", align_bytes=64)
         tiles = {}
 
-        def impact_interleave(c, ch, engine):
-            half, lo = divmod(ch * CH, BANK)
-            grouped = work.tile([P, CH, PACK], BF16, name=f"ig_{c}_{ch}", tag="ig", bufs=6, align_bytes=64)
-            tiles["ig", c, ch] = grouped
-            raw = imp_raw[c, half][:, :, lo : lo + CH]
-            dst = grouped[:].rearrange("p (n i) t -> p n t i", i=4)
-            src = raw.rearrange("p t (n i) -> p n t i", i=4)
-            if engine == "S":
-                nc.scalar.copy(out=dst, in_=src)
-            elif engine == "V":
-                nc.vector.tensor_copy(out=dst, in_=src)
-            else:
-                nc.gpsimd.tensor_scalar(
-                    out=grouped[:], in0=raw.rearrange("p t n -> p n t"), scalar1=1.0, scalar2=0.0, op0=MULT, op1=ADD
-                )
+        def bank_tile(shape, name, tag):
+            return psum.tile(shape, F32, name=name, tag=tag, bufs=PSUM_BUFS[tag])
 
-        def impact_quantize(c, ch):
-            cols = slice(ch * CH, (ch + 1) * CH)
-            nc.vector.quantize_mx(
-                out=imp_codes[:, c, cols].bitcast(FP8X4),
-                scales=imp_scales[:, c, cols],
-                in_=tiles.pop(("ig", c, ch))[:].rearrange("p n t -> p (n t)"),
+        def baton_tile(name):
+            return work.tile([P, CHUNK, PACK], BF16, name=name, tag="baton", bufs=1, align_bytes=64)
+
+        def move(engine, out, in_):
+            if engine == SCALAR:
+                nc.scalar.copy(out=out, in_=in_)
+            else:
+                nc.vector.tensor_copy(out=out, in_=in_)
+
+        def interleave(engine, grouped, planes):
+            move(engine, grouped.rearrange("p (n i) t -> p n t i", i=4), planes.rearrange("p t (n i) -> p n t i", i=4))
+
+        def quantize(codes, scales, grouped):
+            nc.vector.quantize_mx(out=codes.bitcast(FP8X4), scales=scales, in_=grouped)
+
+        def multiply(out, stationary, moving, first, final, moving_dtype=FP8X4):
+            nc.tensor.matmul_mx(
+                out=out,
+                lhsT=stationary[0].bitcast(FP8X4),
+                lhsT_scale=stationary[1],
+                rhs=moving[0].bitcast(moving_dtype),
+                rhs_scale=moving[1],
+                start=first,
+                stop=final,
             )
 
-        def widen(i, engine="S", lo=0, hi=A):
+        def impact_group(c, chunk, engine, baton=False):
+            half, lo = divmod(chunk * CHUNK, BANK)
+            if baton:
+                grouped = baton_tile(f"ig_{c}_{chunk}")
+            else:
+                grouped = work.tile([P, CHUNK, PACK], BF16, name=f"ig_{c}_{chunk}", tag="grouped", bufs=6, align_bytes=64)
+            tiles["impact", c, chunk] = grouped
+            planes = imp_raw[c, half][:, :, lo : lo + CHUNK]
+            if engine == GPSIMD:
+                nc.gpsimd.tensor_scalar(
+                    out=grouped[:], in0=planes.rearrange("p t n -> p n t"), scalar1=1.0, scalar2=0.0, op0=MULT, op1=ADD
+                )
+            else:
+                interleave(engine, grouped[:], planes)
+
+        def impact_quantize(c, chunk):
+            cols = slice(chunk * CHUNK, (chunk + 1) * CHUNK)
+            grouped = tiles.pop(("impact", c, chunk))
+            quantize(imp_codes[:, c, cols], imp_scales[:, c, cols], grouped[:].rearrange("p n t -> p (n t)"))
+
+        def widen(i, engine=SCALAR, lo=0, hi=A):
             if lo == 0:
                 wide = work.tile([P, A], BF16, name=f"wide_{i}", tag="wide", bufs=4, align_bytes=64)
                 tiles["wide", i] = wide
             q, r = divmod(i, 2)
-            src = flow_first[:, r, :] if hi < A else flow_sb[q][:, r, :]
-            if engine == "S":
-                nc.scalar.copy(out=tiles["wide", i][:, lo:hi], in_=src.bitcast(FP8))
-            else:
-                nc.vector.tensor_copy(out=tiles["wide", i][:, lo:hi], in_=src.bitcast(FP8))
+            codes = flow_first[:, r, :] if hi < A else flow_sb[q][:, r, :]
+            move(engine, tiles["wide", i][:, lo:hi], codes.bitcast(FP8))
 
-        def regroup(i):
-            sorted_words = work.tile([P, A_PASSES, 2, P], F32, name=f"words_{i}", tag="words", bufs=4, align_bytes=64)
-            tiles["words", i] = sorted_words
-            words = tiles["wide", i][:].bitcast(F32)
-            nc.scalar.copy(out=sorted_words[:], in_=words.rearrange("p (c m u) -> p c u m", c=A_PASSES, u=2))
+        def sort_words(out, rows):
+            nc.scalar.copy(out=out, in_=rows.bitcast(F32).rearrange("p (c m u) -> p c u m", m=P, u=2))
+
+        def words_of(key, rows, c, u):
+            if key in tiles:
+                return tiles[key][:, c, u, :]
+            return rows.bitcast(F32)[:, 2 * P * c + u : 2 * P * (c + 1) : 2]
+
+        def flow_sort(i):
+            words = work.tile([P, A_PASSES, 2, P], F32, name=f"words_{i}", tag="words", bufs=4, align_bytes=64)
+            tiles["flow_words", i] = words
+            sort_words(words[:], tiles["wide", i][:])
 
         def flow_transpose(q, c):
-            bank = psum.tile([P, 2, 2, P], F32, name=f"xt_{q}_{c}", tag="xt", bufs=3)
-            tiles["xt", q, c] = bank
+            bank = bank_tile([P, 2, 2, P], f"xt_{q}_{c}", "turned_x")
+            tiles["turned_flow", q, c] = bank
             for r in range(2):
                 i = 2 * q + r
                 for u in range(2):
-                    if ("words", i) in tiles:
-                        src = tiles["words", i][:, c, u, :]
-                    else:
-                        src = tiles["wide", i][:].bitcast(F32)[:, 256 * c + u : 256 * (c + 1) : 2]
-                    nc.tensor.transpose(bank[:, u, r, :], src, ident[:])
+                    nc.tensor.transpose(bank[:, u, r, :], words_of(("flow_words", i), tiles["wide", i][:], c, u), ident[:])
 
-        def flow_scale_out(q, c, lo=0, hi=2):
-            if lo == 0:
-                grouped = work.tile([P, 2 * P, PACK], BF16, name=f"fg_{q}_{c}", tag="fg", bufs=4, align_bytes=64)
-                tiles["fg", q, c] = grouped
-            halves = tiles["xt", q, c][:].rearrange("p u r m -> p (u r m)").bitcast(BF16)
+        def flow_scale_out(q, c, lo=0, hi=2, baton=False):
+            if baton:
+                tiles["flow", q, c] = baton_tile(f"fg_{q}_{c}")
+            elif lo == 0:
+                grouped = work.tile([P, 2 * P, PACK], BF16, name=f"fg_{q}_{c}", tag="flow", bufs=4, align_bytes=64)
+                tiles["flow", q, c] = grouped
+            values = tiles["turned_flow", q, c][:].rearrange("p u r m -> p (u r m)").bitcast(BF16)
             rows = slice(lo * P, hi * P)
+            scales = scale_sb[:, c, :].rearrange("p (u e) -> p u e", u=2)
             nc.vector.tensor_tensor(
-                out=tiles["fg", q, c][:, rows, :].rearrange("p m (u e) -> p m u e", u=2),
-                in0=halves.rearrange("p (u m e) -> p m u e", u=2, e=2)[:, rows, :, :],
-                in1=scale_sb[:, c, :]
-                .rearrange("p (u e) -> p u e", u=2)
-                .unsqueeze(1)
-                .to_broadcast([P, (hi - lo) * P, 2, 2]),
+                out=tiles["flow", q, c][:, rows, :].rearrange("p m (u e) -> p m u e", u=2),
+                in0=values.rearrange("p (u m e) -> p m u e", u=2, e=2)[:, rows, :, :],
+                in1=scales.unsqueeze(1).to_broadcast([P, (hi - lo) * P, 2, 2]),
                 op=MULT,
             )
 
         def flow_quantize(q, c):
-            codes = work.tile([P, 2 * P], U32, name=f"fc_{q}_{c}", tag="fc", bufs=9, align_bytes=64)
-            scales = work.tile([P, 2 * P], U8, name=f"fs_{q}_{c}", tag="fs", bufs=9, align_bytes=64)
-            tiles["fc", q, c] = (codes, scales)
-            nc.vector.quantize_mx(
-                out=codes[:].bitcast(FP8X4),
-                scales=scales[:],
-                in_=tiles.pop(("fg", q, c))[:].rearrange("p m t -> p (m t)"),
-            )
+            codes = work.tile([P, 2 * P], U32, name=f"fc_{q}_{c}", tag="flow_codes", bufs=9, align_bytes=64)
+            scales = work.tile([P, 2 * P], U8, name=f"fs_{q}_{c}", tag="flow_scales", bufs=9, align_bytes=64)
+            tiles["flow_codes", q, c] = (codes, scales)
+            quantize(codes[:], scales[:], tiles.pop(("flow", q, c))[:].rearrange("p m t -> p (m t)"))
 
         def impact_matmul(i, half):
             q, r = divmod(i, 2)
-            z = psum.tile([P, BANK], F32, name=f"z_{i}_{half}", tag="z", bufs=2)
+            z = bank_tile([P, BANK], f"z_{i}_{half}", "z")
             tiles["z", i, half] = z
             cols = slice(half * BANK, (half + 1) * BANK)
+            rows = slice(r * P, (r + 1) * P)
             for c in range(A_PASSES):
-                codes, scales = tiles["fc", q, c]
-                nc.tensor.matmul_mx(
-                    out=z[:],
-                    lhsT=codes[:, r * P : (r + 1) * P].bitcast(FP8X4),
-                    lhsT_scale=scales[:, r * P : (r + 1) * P],
-                    rhs=imp_codes[:, c, cols].bitcast(FP8X4),
-                    rhs_scale=imp_scales[:, c, cols],
-                    start=(c == 0),
-                    stop=(c == A_PASSES - 1),
-                )
+                codes, scales = tiles["flow_codes", q, c]
+                moving = (imp_codes[:, c, cols], imp_scales[:, c, cols])
+                multiply(z[:], (codes[:, rows], scales[:, rows]), moving, c == 0, c == A_PASSES - 1)
 
         def saturate(i, half):
             g, j = divmod(i, PACK)
@@ -219,187 +228,153 @@ def tile_cross_impact_hedge_s8_kernel(
                 func=TANH,
             )
 
-        def weigh(g, ch):
-            half, lo = divmod(ch * CH, BANK)
-            grouped = work.tile([P, CH, PACK], BF16, name=f"wg_{g}_{ch}", tag="wg", bufs=1, align_bytes=64)
-            tiles["wg", g, ch] = grouped
+        def weigh_chunk(g, chunk):
+            half, lo = divmod(chunk * CHUNK, BANK)
+            grouped = baton_tile(f"wg_{g}_{chunk}")
+            tiles["weighted", g, chunk] = grouped
             nc.gpsimd.tensor_tensor(
                 out=grouped[:],
-                in0=tiles["h", g, half][:, :, lo : lo + CH].rearrange("p j n -> p n j"),
-                in1=depth_sb[:, g, :].unsqueeze(1).to_broadcast([P, CH, PACK]),
+                in0=tiles["h", g, half][:, :, lo : lo + CHUNK].rearrange("p j n -> p n j"),
+                in1=depth_f32[:, g, :].unsqueeze(1).to_broadcast([P, CHUNK, PACK]),
                 op=MULT,
             )
 
-        def weigh_plane(g, half, j, engine, lo=0):
+        def weigh_plane(g, half, j, lo=0):
             if j == 0:
                 planes = work.tile([P, PACK, BANK], BF16, name=f"planes_{g}_{half}", tag="raw", bufs=6, align_bytes=64)
-                tiles["planes", g, half] = planes
-            dst = tiles["planes", g, half][:, j, lo:]
-            src = tiles["h", g, half][:, j, lo:]
-            if engine == "S":
-                nc.scalar.activation(out=dst, in_=src, func=COPY, scale=depth_sb[:, g, j : j + 1])
-            else:
-                nc.vector.tensor_scalar(out=dst, in0=src, scalar1=depth_sb[:, g, j : j + 1], scalar2=None, op0=MULT)
-
-        def planes_interleave(g, ch, engine):
-            grouped = work.tile([P, CH, PACK], BF16, name=f"wp_{g}_{ch}", tag="ig", bufs=6, align_bytes=64)
-            tiles["wg", g, ch] = grouped
-            half, lo = divmod(ch * CH, BANK)
-            dst = grouped[:].rearrange("p (n i) t -> p n t i", i=4)
-            src = tiles["planes", g, half][:, :, lo : lo + CH].rearrange("p t (n i) -> p n t i", i=4)
-            if engine == "S":
-                nc.scalar.copy(out=dst, in_=src)
-            else:
-                nc.vector.tensor_copy(out=dst, in_=src)
-
-        def weighted_quantize(g, ch):
-            cols = slice(ch * CH, (ch + 1) * CH)
-            nc.vector.quantize_mx(
-                out=wt_codes[:, g, cols].bitcast(FP8X4),
-                scales=wt_scales[:, g, cols],
-                in_=tiles.pop(("wg", g, ch))[:].rearrange("p n t -> p (n t)"),
+                tiles["weighted_planes", g, half] = planes
+            nc.scalar.activation(
+                out=tiles["weighted_planes", g, half][:, j, lo:],
+                in_=tiles["h", g, half][:, j, lo:],
+                func=COPY,
+                scale=depth_f32[:, g, j : j + 1],
             )
 
-        def moves_transpose(i, half, tag="ht"):
+        def weighted_group(g, chunk, engine):
+            half, lo = divmod(chunk * CHUNK, BANK)
+            grouped = work.tile([P, CHUNK, PACK], BF16, name=f"wp_{g}_{chunk}", tag="grouped", bufs=6, align_bytes=64)
+            tiles["weighted", g, chunk] = grouped
+            interleave(engine, grouped[:], tiles["weighted_planes", g, half][:, :, lo : lo + CHUNK])
+
+        def weighted_quantize(g, chunk):
+            cols = slice(chunk * CHUNK, (chunk + 1) * CHUNK)
+            grouped = tiles.pop(("weighted", g, chunk))
+            quantize(wt_codes[:, g, cols], wt_scales[:, g, cols], grouped[:].rearrange("p n t -> p (n t)"))
+
+        def moves_transpose(i, half):
             g, j = divmod(i, PACK)
-            bank = psum.tile([P, PACK, P], F32, name=f"ht_{i}_{half}", tag=tag, bufs=2)
-            tiles["ht", i, half] = bank
+            bank = bank_tile([P, PACK, P], f"ht_{i}_{half}", "turned_h")
+            tiles["turned_h", i, half] = bank
             for t in range(PACK):
                 nc.tensor.transpose(bank[:, t, :], tiles["h", g, half][:, j, t * P : (t + 1) * P], ident[:])
 
-        def moves_scale(i, half):
+        def moves_tile(i, half):
             q, r = divmod(i, 2)
-            if ("mg", q, half) not in tiles:
-                grouped = work.tile([P, 2, P, PACK], BF16, name=f"mg_{q}_{half}", tag="mg", bufs=3, align_bytes=64)
-                tiles["mg", q, half] = grouped
+            if ("moves", q, half) not in tiles:
+                grouped = work.tile([P, 2, P, PACK], BF16, name=f"mg_{q}_{half}", tag="moves", bufs=3, align_bytes=64)
+                tiles["moves", q, half] = grouped
+            return tiles["moves", q, half][:, r, :, :]
+
+        def moves_scale(i, half):
             nc.vector.tensor_tensor(
-                out=tiles["mg", q, half][:, r, :, :],
-                in0=tiles.pop(("ht", i, half))[:].rearrange("p t m -> p m t"),
-                in1=vol_sb[:, half, :].unsqueeze(1).to_broadcast([P, P, PACK]),
+                out=moves_tile(i, half),
+                in0=tiles.pop(("turned_h", i, half))[:].rearrange("p t m -> p m t"),
+                in1=vol_bf[:, half, :].unsqueeze(1).to_broadcast([P, P, PACK]),
                 op=MULT,
             )
 
         def moves_planes(i, half):
-            planes = work.tile([P, PACK, P], BF16, name=f"mp_{i}_{half}", tag="mp", bufs=2, align_bytes=64)
-            tiles["mp", i, half] = planes
-            bank = tiles.pop(("ht", i, half))
+            planes = work.tile([P, PACK, P], BF16, name=f"mp_{i}_{half}", tag="moves_planes", bufs=2, align_bytes=64)
+            tiles["moves_planes", i, half] = planes
+            bank = tiles.pop(("turned_h", i, half))
             for t in range(PACK):
                 nc.scalar.activation(out=planes[:, t, :], in_=bank[:, t, :], func=COPY, scale=vol_f32[:, half, t : t + 1])
 
-        def moves_interleave(i, half):
-            q, r = divmod(i, 2)
-            grouped = work.tile([P, 2, P, PACK], BF16, name=f"mg_{q}_{half}", tag="mg", bufs=3, align_bytes=64)
-            tiles["mg", q, half] = grouped
-            nc.scalar.copy(
-                out=grouped[:, r, :, :].rearrange("p (m i) t -> p m t i", i=4),
-                in_=tiles.pop(("mp", i, half))[:].rearrange("p t (m i) -> p m t i", i=4),
-            )
+        def moves_group(i, half):
+            interleave(SCALAR, moves_tile(i, half), tiles.pop(("moves_planes", i, half))[:])
 
         def moves_quantize(q, half):
-            codes = work.tile([P, 2 * P], U32, name=f"mc_{q}_{half}", tag="mc", bufs=5, align_bytes=64)
-            scales = work.tile([P, 2 * P], U8, name=f"ms_{q}_{half}", tag="ms", bufs=5, align_bytes=64)
-            tiles["mc", q, half] = (codes, scales)
-            nc.vector.quantize_mx(
-                out=codes[:].bitcast(FP8X4),
-                scales=scales[:],
-                in_=tiles.pop(("mg", q, half))[:].rearrange("p r m t -> p (r m t)"),
-            )
+            codes = work.tile([P, 2 * P], U32, name=f"mc_{q}_{half}", tag="moves_codes", bufs=5, align_bytes=64)
+            scales = work.tile([P, 2 * P], U8, name=f"ms_{q}_{half}", tag="moves_scales", bufs=5, align_bytes=64)
+            tiles["moves_codes", q, half] = (codes, scales)
+            quantize(codes[:], scales[:], tiles.pop(("moves", q, half))[:].rearrange("p r m t -> p (r m t)"))
 
-        def hedge_matmul(i, tag="hg", lo=0, hi=R, width=R):
+        def hedge_matmul(i, tag="hedge"):
             q, r = divmod(i, 2)
-            bank = psum.tile([P, hi - lo], F32, name=f"hg_{i}_{lo}", tag=tag, bufs={"hg": 1, "xt": 3}.get(tag, 2))
-            tiles["hg", i, lo] = bank
-            for c0 in range(lo, hi, width):
-                for half in range(N_PASSES):
-                    codes, scales = tiles["mc", q, half]
-                    nc.tensor.matmul_mx(
-                        out=bank[:, c0 - lo : c0 - lo + width],
-                        lhsT=codes[:, r * P : (r + 1) * P].bitcast(FP8X4),
-                        lhsT_scale=scales[:, r * P : (r + 1) * P],
-                        rhs=w_words[:, half, 2 * c0 : 2 * (c0 + width)].bitcast(FP4X4),
-                        rhs_scale=w_scales[:, half, c0 : c0 + width],
-                        start=(half == 0),
-                        stop=(half == N_PASSES - 1),
-                    )
+            bank = bank_tile([P, R], f"hg_{i}", tag)
+            tiles["hedge", i] = bank
+            rows = slice(r * P, (r + 1) * P)
+            for half in range(N_PASSES):
+                codes, scales = tiles["moves_codes", q, half]
+                moving = (w_words[:, half, :], w_scales[:, half, :])
+                multiply(bank[:], (codes[:, rows], scales[:, rows]), moving, half == 0, half == N_PASSES - 1, FP4X4)
 
         hedge_view = hedge.rearrange("(g p j) r -> g j p r", p=P, j=PACK)
 
-        def hedge_exit(i, engine="S", lo=0, hi=R):
+        def hedge_store(i, engine=SCALAR):
             g, j = divmod(i, PACK)
-            res = work.tile([P, hi - lo], F32, name=f"hr_{i}_{lo}", tag="hr", bufs=4, align_bytes=64)
-            bank = tiles.pop(("hg", i, lo))
-            if engine == "S":
-                nc.scalar.copy(out=res[:], in_=bank[:])
-            else:
-                nc.vector.tensor_copy(out=res[:], in_=bank[:])
-            nc.sync.dma_start(out=hedge_view[g, j][:, lo:hi], in_=res[:])
+            result = work.tile([P, R], F32, name=f"hr_{i}", tag="hedge_out", bufs=4, align_bytes=64)
+            move(engine, result[:], tiles.pop(("hedge", i))[:])
+            nc.sync.dma_start(out=hedge_view[g, j], in_=result[:])
 
-        def sched_transpose(b, tag="xt"):
-            qt, gp = divmod(b, 2)
-            words = sched_sb[qt][:].bitcast(F32)
-            bank = psum.tile([P, 2, 2, P], F32, name=f"st_{b}", tag=tag, bufs=3 if tag == "xt" else 1)
-            tiles["st", b] = bank
+        def sched_sort(qt):
+            words = work.tile([P, T_PASSES, 2, P], F32, name=f"sched_words_{qt}", tag="raw", bufs=6, align_bytes=64)
+            tiles["sched_words", qt] = words
+            sort_words(words[:], sched_sb[qt][:])
+
+        def sched_transpose(b, tag="turned_x"):
+            qt, two = divmod(b, 2)
+            bank = bank_tile([P, 2, 2, P], f"st_{b}", tag)
+            tiles["turned_sched", b] = bank
             for s in range(2):
-                g = 2 * gp + s
                 for u in range(2):
-                    nc.tensor.transpose(bank[:, s, u, :], words[:, 256 * g + u : 256 * (g + 1) : 2], ident[:])
+                    words = words_of(("sched_words", qt), sched_sb[qt][:], 2 * two + s, u)
+                    nc.tensor.transpose(bank[:, s, u, :], words, ident[:])
 
-        def sched_exit(b):
-            grouped = work.tile([P, 2, P, PACK], BF16, name=f"sg_{b}", tag="sg", bufs=4, align_bytes=64)
-            tiles["sg", b] = grouped
+        def sched_group(b):
+            grouped = work.tile([P, 2, P, PACK], BF16, name=f"sg_{b}", tag="sched", bufs=4, align_bytes=64)
+            tiles["sched", b] = grouped
             words = grouped[:].rearrange("p s q t -> p (s q t)").bitcast(F32)
             nc.scalar.copy(
                 out=words.rearrange("p (s q u) -> p s q u", s=2, u=2),
-                in_=tiles.pop(("st", b))[:].rearrange("p s u q -> p s q u"),
+                in_=tiles.pop(("turned_sched", b))[:].rearrange("p s u q -> p s q u"),
             )
 
         def sched_quantize(b):
-            qt, gp = divmod(b, 2)
-            nc.vector.quantize_mx(
-                out=sch_codes[:, qt, 2 * gp : 2 * gp + 2, :].rearrange("p s q -> p (s q)").bitcast(FP8X4),
-                scales=sch_scales[:, qt, 2 * gp : 2 * gp + 2, :].rearrange("p s q -> p (s q)"),
-                in_=tiles.pop(("sg", b))[:].rearrange("p s q t -> p (s q t)"),
+            qt, two = divmod(b, 2)
+            passes = slice(2 * two, 2 * two + 2)
+            quantize(
+                sch_codes[:, qt, passes, :].rearrange("p s q -> p (s q)"),
+                sch_scales[:, qt, passes, :].rearrange("p s q -> p (s q)"),
+                tiles.pop(("sched", b))[:].rearrange("p s q t -> p (s q t)"),
             )
 
-        def cost_matmul(qt, half, g, tag=None):
-            if tag:
-                bank = psum.tile([P, BANK], F32, name=f"cost_{qt}_{half}", tag=tag, bufs={"hg": 1, "xt": 3}.get(tag, 2))
-                tiles["cb", qt, half] = bank
+        def cost_matmul(qt, half, passes, tag="turned_x"):
+            if passes[0] == 0:
+                tiles["cost", qt, half] = bank_tile([P, BANK], f"cost_{qt}_{half}", tag)
             cols = slice(half * BANK, (half + 1) * BANK)
-            nc.tensor.matmul_mx(
-                out=tiles["cb", qt, half][:],
-                lhsT=sch_codes[:, qt, g, :].bitcast(FP8X4),
-                lhsT_scale=sch_scales[:, qt, g, :],
-                rhs=wt_codes[:, g, cols].bitcast(FP8X4),
-                rhs_scale=wt_scales[:, g, cols],
-                start=(g == 0),
-                stop=(g == T_PASSES - 1),
-            )
+            for g in passes:
+                stationary = (sch_codes[:, qt, g, :], sch_scales[:, qt, g, :])
+                moving = (wt_codes[:, g, cols], wt_scales[:, g, cols])
+                multiply(tiles["cost", qt, half][:], stationary, moving, g == 0, g == T_PASSES - 1)
 
-        def cost_exit(qt, half, engine):
-            res = work.tile([P, BANK], F32, name=f"cr_{qt}_{half}", tag="cr", bufs=4, align_bytes=64)
-            dst = res[:].rearrange("p (m t) -> p m t", t=PACK)
-            src = tiles.pop(("cb", qt, half))[:].rearrange("p (t m) -> p m t", t=PACK)
-            if engine == "S":
-                nc.scalar.copy(out=dst, in_=src)
-            else:
-                nc.vector.tensor_copy(out=dst, in_=src)
-            nc.sync.dma_start(out=cost[qt * P : (qt + 1) * P, half * BANK : (half + 1) * BANK], in_=res[:])
+        def cost_store(qt, half, engine):
+            result = work.tile([P, BANK], F32, name=f"cr_{qt}_{half}", tag="cost_out", bufs=4, align_bytes=64)
+            sums = tiles.pop(("cost", qt, half))[:].rearrange("p (t m) -> p m t", t=PACK)
+            move(engine, result[:].rearrange("p (m t) -> p m t", t=PACK), sums)
+            nc.sync.dma_start(out=cost[qt * P : (qt + 1) * P, half * BANK : (half + 1) * BANK], in_=result[:])
 
-        load_scale()
-        load_depth()
-        load_first()
+        nc.scalar.dma_start(out=scale_sb[:], in_=flow_scale.rearrange("o (c p t) -> p (o c) t", p=P, t=PACK))
+        nc.scalar.dma_start(out=depth_bf[:], in_=depth.rearrange("(g p j) -> p g j", p=P, j=PACK))
+        nc.scalar.activation(out=depth_f32[:], in_=depth_bf[:], func=COPY)
+        nc.sync.dma_start(out=flow_first[:], in_=flow_view[0, :, 0:2, 0:K_PASS])
         load_flow(0)
-        load_impact(0, 0)
-        load_impact(1, 0)
-        load_impact(2, 0)
+        load_impact(0)
         load_flow(1)
-        load_impact(0, 1)
-        load_impact(1, 1)
-        load_impact(2, 1)
+        load_impact(1)
         load_sched(0)
         load_flow(2)
-        load_vol()
+        nc.sync.dma_start(out=vol_bf[:], in_=vol.rearrange("(g p j) -> p g j", p=P, j=PACK))
         load_sens()
         load_flow(3)
         load_flow(4)
@@ -407,169 +382,172 @@ def tile_cross_impact_hedge_s8_kernel(
         for q in range(5, PAIRS):
             load_flow(q)
 
-        widen(0, "V", 0, K_PASS)
-        widen(1, "S", 0, K_PASS)
-        flow_transpose(0, 0)
-        widen(0, "V", K_PASS)
-        widen(1, "S", K_PASS)
-        flow_transpose(0, 1)
-        flow_transpose(0, 2)
-        impact_interleave(0, 0, "S")
-        impact_interleave(0, 1, "G")
-        impact_interleave(1, 0, "S")
-        impact_interleave(1, 1, "G")
-        impact_interleave(2, 0, "S")
+        for lo, hi in ((0, K_PASS), (K_PASS, A)):
+            widen(0, VECTOR, lo, hi)
+            widen(1, SCALAR, lo, hi)
+            for c in range(lo // K_PASS, hi // K_PASS):
+                flow_transpose(0, c)
+        for c in range(A_PASSES - 1):
+            impact_group(c, 0, SCALAR)
+            impact_group(c, 1, GPSIMD)
+        impact_group(A_PASSES - 1, 0, SCALAR)
         widen(2)
         widen(3)
         for c in range(A_PASSES):
             flow_scale_out(0, c)
-        impact_interleave(2, 1, "V")
+        impact_group(A_PASSES - 1, 1, VECTOR, baton=True)
         for c in range(A_PASSES):
             flow_transpose(1, c)
         for c in range(A_PASSES):
             impact_quantize(c, 0)
             impact_quantize(c, 1)
             flow_quantize(0, c)
-        impact_interleave(0, 2, "S")
-        impact_interleave(0, 3, "G")
-        impact_interleave(1, 2, "S")
-        impact_interleave(1, 3, "G")
-        impact_interleave(2, 2, "S")
+        for c in range(A_PASSES - 1):
+            impact_group(c, 2, SCALAR)
+            impact_group(c, 3, GPSIMD, baton=(c == 0))
+        impact_group(A_PASSES - 1, 2, SCALAR)
         for c in range(A_PASSES):
             flow_scale_out(1, c)
-        for r in range(2):
-            impact_matmul(r, 0)
-        sched_transpose(0, "hg")
+        for i in range(2):
+            impact_matmul(i, 0)
+        sched_transpose(0, "hedge")
         sched_transpose(1)
-        impact_interleave(2, 3, "S")
-        for r in range(2):
-            saturate(r, 0)
+        impact_group(A_PASSES - 1, 3, SCALAR)
+        for i in range(2):
+            saturate(i, 0)
         widen(4)
         widen(5)
-        sched_exit(1)
+        sched_group(1)
         for c in range(A_PASSES):
             impact_quantize(c, 2)
             impact_quantize(c, 3)
         for c in range(A_PASSES):
             flow_quantize(1, c)
-        for r in range(2):
-            moves_transpose(r, 0)
-        for r in range(2):
-            impact_matmul(r, 1)
-            saturate(r, 1)
-        for r in range(2):
-            moves_scale(r, 0)
+        for i in range(2):
+            moves_transpose(i, 0)
+        for i in range(2):
+            impact_matmul(i, 1)
+            saturate(i, 1)
+        for i in range(2):
+            moves_scale(i, 0)
         moves_quantize(0, 0)
         widen(6)
+        nc.scalar.copy(out=vol_f32[:], in_=vol_bf[:])
 
         last = T_PASSES - 1
-        nc.scalar.copy(out=vol_f32[:], in_=vol_sb[:])
         for s in range(2, STEPS):
             q, half = divmod(s, 2)
-            units = [(q + 1, c) for c in ((0, 1) if half == 0 else (2,))] if q + 1 < PAIRS else []
-            bank = {11: 2, 13: 3}.get(s)
-            before = divmod(s - 1, 2)
-            first, second = 2 * before[0], 2 * before[0] + 1
+            ahead = q + 1
+            flowing = ahead < PAIRS
+            moved_pair, moved_half = divmod(s - 1, 2)
+            first, second = 2 * moved_pair, 2 * moved_pair + 1
             chunk = divmod(s - 3, PACK) if 3 <= s < STEPS - 1 else None
-            shared = half == 0 and 4 <= s <= 10
-            split = units and not (4 <= s - half <= 10)
-            if chunk and units:
-                weigh(*chunk)
-            if split and half == 1:
-                flow_scale_out(q + 1, 1, 1, 2)
+            shared = s in SHARED_STEPS
+            split = s - half not in SHARED_STEPS
+            sched_part = s - SCHED_SORT_STEP if s - SCHED_SORT_STEP in (2, 3) else None
+
+            if chunk and flowing:
+                weigh_chunk(*chunk)
+            if flowing and split and half == 1:
+                flow_scale_out(ahead, 1, 1, 2)
+
             if shared:
-                moves_transpose(first, before[1])
-            for unit in units:
-                flow_transpose(*unit)
-            if bank is not None:
-                sched_transpose(bank)
+                moves_transpose(first, moved_half)
+            if flowing:
+                for c in ((0, 1), (2,))[half]:
+                    flow_transpose(ahead, c)
+            if sched_part:
+                sched_transpose(sched_part)
             if not shared:
-                moves_transpose(first, before[1])
-            moves_transpose(second, before[1])
+                moves_transpose(first, moved_half)
+            moves_transpose(second, moved_half)
+
             if s >= 4:
-                hedge_exit(s - 4)
+                hedge_store(s - 4)
             if shared:
-                moves_planes(first, before[1])
-            if 7 <= s + 4 < TILES and (s % 2 == 1 or s > 10):
-                regroup(s + 4)
-            if shared and not (s + 5 < TILES):
-                moves_interleave(first, before[1])
+                moves_planes(first, moved_half)
+            if FIRST_SORTED <= s + 4 < TILES and not shared:
+                flow_sort(s + 4)
             if s + 5 < TILES:
                 widen(s + 5)
-                if shared:
-                    moves_interleave(first, before[1])
-            if s == 12:
+            if shared:
+                moves_group(first, moved_half)
+            if s == SCHED_SORT_STEP:
+                sched_sort(1)
+            if s == SCHED_SORT_STEP + 1:
                 for j in range(PACK):
-                    weigh_plane(last - 1, 1, j, "S", CH)
-                planes_interleave(last - 1, 3, "S")
-            if before[0] >= PAIRS - 2:
-                for r in range(2):
-                    weigh_plane(last, before[1], 2 * (before[0] % 2) + r, "S")
-            if s == 2 and True:
-                sched_exit(0)
-            if bank is not None:
-                sched_exit(bank)
-            if s >= STEPS - 3:
-                moves_scale(first, before[1])
-                moves_scale(second, before[1])
-            if units and half == 0:
-                flow_scale_out(q + 1, 0)
-                flow_scale_out(q + 1, 1, 0, 1 if split else 2)
-            if units and half == 1:
-                flow_scale_out(q + 1, 2)
-            if s < STEPS - 3:
+                    weigh_plane(last - 1, 1, j, CHUNK)
+                weighted_group(last - 1, 3, SCALAR)
+            if first >= PACK * last:
+                weigh_plane(last, moved_half, first % PACK)
+                weigh_plane(last, moved_half, second % PACK)
+            if s == 2:
+                sched_group(0)
+            if sched_part:
+                sched_group(sched_part)
+
+            moves_first = s >= STEPS - 3
+            if moves_first:
+                moves_scale(first, moved_half)
+                moves_scale(second, moved_half)
+            if flowing and half == 0:
+                flow_scale_out(ahead, 0, baton=(s == 2))
+                flow_scale_out(ahead, 1, 0, 1 if split else 2)
+            if flowing and half == 1:
+                flow_scale_out(ahead, 2)
+            if not moves_first:
                 if not shared:
-                    moves_scale(first, before[1])
-                moves_scale(second, before[1])
+                    moves_scale(first, moved_half)
+                moves_scale(second, moved_half)
+
             if s == STEPS - 1:
-                planes_interleave(last, 0, "V")
-                planes_interleave(last, 1, "V")
-            if units:
+                weighted_group(last, 0, VECTOR)
+                weighted_group(last, 1, VECTOR)
+            if flowing:
                 for c in (((0,), (1, 2)) if split else ((0, 1), (2,)))[half]:
-                    flow_quantize(q + 1, c)
+                    flow_quantize(ahead, c)
             if s == STEPS - 2:
                 for b in range(4):
                     sched_quantize(b)
             if chunk:
                 weighted_quantize(*chunk)
-            moves_quantize(*before)
-            for r in range(2):
-                impact_matmul(2 * q + r, half)
-                saturate(2 * q + r, half)
+            moves_quantize(moved_pair, moved_half)
+
+            for i in (2 * q, 2 * q + 1):
+                impact_matmul(i, half)
+                saturate(i, half)
             if s >= 3:
                 hedge_matmul(s - 3)
 
         weighted_quantize(last, 0)
         weighted_quantize(last, 1)
-        weigh_plane(last, 1, 2, "S")
-        weigh_plane(last, 1, 3, "S")
-        moves_transpose(TILES - 2, 1)
-        moves_transpose(TILES - 1, 1)
-        moves_scale(TILES - 2, 1)
-        moves_scale(TILES - 1, 1)
-        hedge_exit(TILES - 4)
-        planes_interleave(last, 3, "S")
-        planes_interleave(last, 2, "V")
+        for i in (TILES - 2, TILES - 1):
+            weigh_plane(last, 1, i % PACK)
+        for i in (TILES - 2, TILES - 1):
+            moves_transpose(i, 1)
+        for i in (TILES - 2, TILES - 1):
+            moves_scale(i, 1)
+        hedge_store(TILES - 4)
+        weighted_group(last, 3, SCALAR)
+        weighted_group(last, 2, VECTOR)
         moves_quantize(PAIRS - 1, 1)
         weighted_quantize(last, 2)
         weighted_quantize(last, 3)
+        early = range(last)
         hedge_matmul(TILES - 3, "z")
-        for qt in range(2):
-            for g in range(last):
-                cost_matmul(qt, 0, g, None if g else "xt")
-        for qt in range(2):
-            cost_matmul(qt, 0, last)
-        for g in range(last):
-            cost_matmul(0, 1, g, None if g else "xt")
-        hedge_matmul(TILES - 2, "ht")
-        hedge_matmul(TILES - 1, "ht")
-        cost_matmul(0, 1, last)
-        for g in range(T_PASSES):
-            cost_matmul(1, 1, g, None if g else "z")
-        hedge_exit(TILES - 3, "S")
-        cost_exit(0, 0, "S")
-        cost_exit(1, 0, "S")
-        hedge_exit(TILES - 2, "V")
-        hedge_exit(TILES - 1, "S")
-        cost_exit(0, 1, "V")
-        cost_exit(1, 1, "S")
+        for qt in range(Q // P):
+            cost_matmul(qt, 0, early)
+        for qt in range(Q // P):
+            cost_matmul(qt, 0, [last])
+        cost_matmul(0, 1, early)
+        hedge_matmul(TILES - 2, "turned_h")
+        hedge_matmul(TILES - 1, "turned_h")
+        cost_matmul(0, 1, [last])
+        cost_matmul(1, 1, range(T_PASSES), "z")
+        hedge_store(TILES - 3)
+        cost_store(0, 0, SCALAR)
+        cost_store(1, 0, SCALAR)
+        hedge_store(TILES - 2, VECTOR)
+        hedge_store(TILES - 1, SCALAR)
+        cost_store(0, 1, VECTOR)
+        cost_store(1, 1, SCALAR)

@@ -358,11 +358,15 @@ def tile_cross_impact_hedge_s8_kernel(
                 moving = (wt_codes[:, g, cols], wt_scales[:, g, cols])
                 multiply(tiles["cost", qt, half][:], stationary, moving, g == 0, g == T_PASSES - 1)
 
-        def cost_store(qt, half, engine):
-            result = work.tile([P, BANK], F32, name=f"cr_{qt}_{half}", tag="cost_out", bufs=4, align_bytes=64)
-            sums = tiles.pop(("cost", qt, half))[:].rearrange("p (t m) -> p m t", t=PACK)
-            move(engine, result[:].rearrange("p (m t) -> p m t", t=PACK), sums)
-            nc.sync.dma_start(out=cost[qt * P : (qt + 1) * P, half * BANK : (half + 1) * BANK], in_=result[:])
+        def cost_store(qt, half, engine, pieces=1):
+            bank = tiles.pop(("cost", qt, half))
+            width = BANK // pieces
+            for lo in range(0, BANK, width):
+                result = work.tile([P, width], F32, name=f"cr_{qt}_{half}_{lo}", tag="cost_out", bufs=5, align_bytes=64)
+                sums = bank[:].rearrange("p (t m) -> p m t", t=PACK)[:, lo // PACK : (lo + width) // PACK, :]
+                move(engine, result[:].rearrange("p (m t) -> p m t", t=PACK), sums)
+                col = half * BANK + lo
+                nc.sync.dma_start(out=cost[qt * P : (qt + 1) * P, col : col + width], in_=result[:])
 
         nc.scalar.dma_start(out=scale_sb[:], in_=flow_scale.rearrange("o (c p t) -> p (o c) t", p=P, t=PACK))
         nc.scalar.dma_start(out=depth_bf[:], in_=depth.rearrange("(g p j) -> p g j", p=P, j=PACK))
@@ -421,7 +425,7 @@ def tile_cross_impact_hedge_s8_kernel(
         for c in range(A_PASSES):
             impact_quantize(c, 2)
             impact_quantize(c, 3)
-        for c in range(A_PASSES):
+        for c in range(A_PASSES - 1):
             flow_quantize(1, c)
         for i in range(2):
             moves_transpose(i, 0)
@@ -430,6 +434,7 @@ def tile_cross_impact_hedge_s8_kernel(
             saturate(i, 1)
         for i in range(2):
             moves_scale(i, 0)
+        flow_quantize(1, A_PASSES - 1)
         moves_quantize(0, 0)
         widen(6)
         nc.scalar.copy(out=vol_f32[:], in_=vol_bf[:])
@@ -539,10 +544,9 @@ def tile_cross_impact_hedge_s8_kernel(
             cost_matmul(qt, 0, early)
         for qt in range(Q // P):
             cost_matmul(qt, 0, [last])
-        cost_matmul(0, 1, early)
         hedge_matmul(TILES - 2, "turned_h")
         hedge_matmul(TILES - 1, "turned_h")
-        cost_matmul(0, 1, [last])
+        cost_matmul(0, 1, range(T_PASSES))
         cost_matmul(1, 1, range(T_PASSES), "z")
         hedge_store(TILES - 3)
         cost_store(0, 0, SCALAR)
@@ -550,4 +554,4 @@ def tile_cross_impact_hedge_s8_kernel(
         hedge_store(TILES - 2, VECTOR)
         hedge_store(TILES - 1, SCALAR)
         cost_store(0, 1, VECTOR)
-        cost_store(1, 1, SCALAR)
+        cost_store(1, 1, SCALAR, pieces=2)

@@ -261,9 +261,9 @@ def tile_cross_impact_hedge_s8_kernel(
             grouped = tiles.pop(("weighted", g, chunk))
             quantize(wt_codes[:, g, cols], wt_scales[:, g, cols], grouped[:].rearrange("p n t -> p (n t)"))
 
-        def moves_transpose(i, half):
+        def moves_transpose(i, half, tag="turned_h"):
             g, j = divmod(i, PACK)
-            bank = bank_tile([P, PACK, P], f"ht_{i}_{half}", "turned_h")
+            bank = bank_tile([P, PACK, P], f"ht_{i}_{half}", tag)
             tiles["turned_h", i, half] = bank
             for t in range(PACK):
                 nc.tensor.transpose(bank[:, t, :], tiles["h", g, half][:, j, t * P : (t + 1) * P], ident[:])
@@ -440,13 +440,13 @@ def tile_cross_impact_hedge_s8_kernel(
         nc.scalar.copy(out=vol_f32[:], in_=vol_bf[:])
 
         last = T_PASSES - 1
-        for s in range(2, STEPS):
+        for s in range(2, STEPS - 1):
             q, half = divmod(s, 2)
             ahead = q + 1
             flowing = ahead < PAIRS
             moved_pair, moved_half = divmod(s - 1, 2)
             first, second = 2 * moved_pair, 2 * moved_pair + 1
-            chunk = divmod(s - 3, PACK) if 3 <= s < STEPS - 1 else None
+            chunk = divmod(s - 3, PACK) if s >= 3 else None
             shared = s in SHARED_STEPS
             split = s - half not in SHARED_STEPS
             sched_part = s - SCHED_SORT_STEP if s - SCHED_SORT_STEP in (2, 3) else None
@@ -505,9 +505,6 @@ def tile_cross_impact_hedge_s8_kernel(
                     moves_scale(first, moved_half)
                 moves_scale(second, moved_half)
 
-            if s == STEPS - 1:
-                weighted_group(last, 0, VECTOR)
-                weighted_group(last, 1, VECTOR)
             if flowing:
                 for c in (((0,), (1, 2)) if split else ((0, 1), (2,)))[half]:
                     flow_quantize(ahead, c)
@@ -524,34 +521,45 @@ def tile_cross_impact_hedge_s8_kernel(
             if s >= 3:
                 hedge_matmul(s - 3)
 
-        weighted_quantize(last, 0)
-        weighted_quantize(last, 1)
-        for i in (TILES - 2, TILES - 1):
+        final = (TILES - 2, TILES - 1)
+        for i in final:
+            weigh_plane(last, 0, i % PACK)
+        for i in final:
+            impact_matmul(i, 1)
+            saturate(i, 1)
+        hedge_matmul(TILES - 4, "turned_x")
+        for i in final:
+            moves_transpose(i, 0)
+        for i in final:
+            moves_transpose(i, 1, "z")
             weigh_plane(last, 1, i % PACK)
-        for i in (TILES - 2, TILES - 1):
-            moves_transpose(i, 1)
-        for i in (TILES - 2, TILES - 1):
-            moves_scale(i, 1)
-        hedge_store(TILES - 4)
+        for chunk in range(2):
+            weighted_group(last, chunk, VECTOR)
+        for chunk in range(2):
+            weighted_quantize(last, chunk)
+        for half in range(N_PASSES):
+            for i in final:
+                moves_scale(i, half)
         weighted_group(last, 3, SCALAR)
+        hedge_store(TILES - 5)
+        hedge_store(TILES - 4)
+        moves_quantize(PAIRS - 1, 0)
         weighted_group(last, 2, VECTOR)
         moves_quantize(PAIRS - 1, 1)
         weighted_quantize(last, 2)
         weighted_quantize(last, 3)
-        early = range(last)
-        hedge_matmul(TILES - 3, "z")
         for qt in range(Q // P):
-            cost_matmul(qt, 0, early)
-        for qt in range(Q // P):
-            cost_matmul(qt, 0, [last])
-        hedge_matmul(TILES - 2, "turned_h")
-        hedge_matmul(TILES - 1, "turned_h")
-        cost_matmul(0, 1, range(T_PASSES))
-        cost_matmul(1, 1, range(T_PASSES), "z")
-        hedge_store(TILES - 3)
+            cost_matmul(qt, 0, range(T_PASSES))
+        hedge_matmul(TILES - 3)
+        cost_matmul(0, 1, range(last), "turned_h")
+        for i in final:
+            hedge_matmul(i, "z")
+        cost_matmul(0, 1, [last])
+        cost_matmul(1, 1, range(T_PASSES), "turned_h")
         cost_store(0, 0, SCALAR)
         cost_store(1, 0, SCALAR)
-        hedge_store(TILES - 2, VECTOR)
-        hedge_store(TILES - 1, SCALAR)
-        cost_store(0, 1, VECTOR)
+        hedge_store(TILES - 3, VECTOR)
+        hedge_store(TILES - 2, SCALAR)
+        hedge_store(TILES - 1, VECTOR)
+        cost_store(0, 1, SCALAR)
         cost_store(1, 1, SCALAR, pieces=2)

@@ -33,10 +33,10 @@ BANK = 512
 CHUNK = 256
 SCALAR, VECTOR, GPSIMD = "scalar", "vector", "gpsimd"
 
-PSUM_BUFS = {"z": 2, "turned_h": 2, "turned_x": 3, "hedge": 1}
-SHARED_STEPS = (4, 6, 8, 10)
-FIRST_SORTED = 7
-SCHED_SORT_STEP = 11
+FIRST_SORTED = 6
+SORT_EVERY = 2
+SHARED_STEPS = (4, 6, 8, 10, 12)
+TURN_BANKS = 5
 
 
 def tile_cross_impact_hedge_s8_kernel(
@@ -46,7 +46,7 @@ def tile_cross_impact_hedge_s8_kernel(
     with ExitStack() as ctx:
         keep = ctx.enter_context(tc.tile_pool(name="keep", bufs=1))
         work = ctx.enter_context(tc.tile_pool(name="work", bufs=3))
-        psum = ctx.enter_context(tc.psum_pool(name="psum", bufs=2))
+        psum = ctx.enter_context(tc.psum_pool(name="psum", bufs=1))
         ctx.enter_context(tc.manual_schedule())
 
         w_scales = keep.tile([P, N_PASSES, R], U8, name="w_scales", align_bytes=64)
@@ -55,37 +55,30 @@ def tile_cross_impact_hedge_s8_kernel(
         make_identity(nc, ident[:])
 
         flow_view = flow_bytes.rearrange("(g p j) a -> g p j a", p=P, j=PACK)
-        flow_sb = []
-        for q in range(PAIRS):
-            pair_bytes = keep.tile([P, 2, A if q else A - K_PASS], U8, name=f"flow_{q}", align_bytes=64)
-            flow_sb.append(pair_bytes)
-        flow_first = keep.tile([P, 2, K_PASS], U8, name="flow_first", align_bytes=64)
+        flow_sb = {}
 
-        def load_flow(q):
-            g, r = divmod(q, 2)
-            nc.sync.dma_start(out=flow_sb[q][:], in_=flow_view[g, :, 2 * r : 2 * r + 2, 0 if q else K_PASS :])
+        def load_flow(first, count):
+            g, j = divmod(first, PACK)
+            rows = keep.tile([P, count, A], U8, name=f"flow_{first}", align_bytes=64)
+            for r in range(count):
+                flow_sb[first + r] = rows[:, r, :]
+            nc.sync.dma_start(out=rows[:], in_=flow_view[g, :, j : j + count, :])
 
         imp_view = impact.rearrange("(c p t) n -> c p t n", p=P, t=PACK)
         imp_raw = {}
-        for c in range(A_PASSES):
-            for half in range(N_PASSES):
-                rows = work.tile([P, PACK, BANK], BF16, name=f"imp_raw_{c}_{half}", tag="raw", bufs=6, align_bytes=64)
-                imp_raw[c, half] = rows
 
-        def load_impact(half):
-            for c in range(A_PASSES):
-                nc.sync.dma_start(out=imp_raw[c, half][:], in_=imp_view[c, :, :, half * BANK : (half + 1) * BANK])
+        def load_impact(c, half):
+            rows = work.tile([P, PACK, BANK], BF16, name=f"imp_raw_{c}_{half}", tag="raw", bufs=6, align_bytes=64)
+            imp_raw[c, half] = rows
+            nc.sync.dma_start(out=rows[:], in_=imp_view[c, :, :, half * BANK : (half + 1) * BANK])
 
         scale_sb = keep.tile([P, A_PASSES, PACK], F32, name="scale_sb", align_bytes=64)
+        vol_f32 = keep.tile([P, N_PASSES, PACK], F32, name="vol_f32", align_bytes=64)
         vol_bf = keep.tile([P, N_PASSES, PACK], BF16, name="vol_bf", align_bytes=64)
         depth_bf = keep.tile([P, T_PASSES, PACK], BF16, name="depth_bf", align_bytes=64)
         depth_f32 = keep.tile([P, T_PASSES, PACK], F32, name="depth_f32", align_bytes=64)
-        vol_f32 = keep.tile([P, N_PASSES, PACK], F32, name="vol_f32", align_bytes=64)
         w_words = keep.tile([P, N_PASSES, 2 * R], U8, name="w_words", align_bytes=64)
-        sched_sb = []
-        for qt in range(Q // P):
-            rows = keep.tile([P, T], BF16, name=f"sched_{qt}", align_bytes=64)
-            sched_sb.append(rows)
+        sched_sb = {}
 
         def load_sens():
             for quad in range(4):
@@ -96,21 +89,31 @@ def tile_cross_impact_hedge_s8_kernel(
             nc.sync.dma_start(out=w_words[:].bitcast(I32), in_=sens_words.rearrange("g p b -> p g b").bitcast(I32))
 
         def load_sched(qt):
-            nc.sync.dma_start(out=sched_sb[qt][:], in_=sched[qt * P : (qt + 1) * P, :])
+            rows = keep.tile([P, T], BF16, name=f"sched_{qt}", align_bytes=64)
+            sched_sb[qt] = rows
+            nc.sync.dma_start(out=rows[:], in_=sched[qt * P : (qt + 1) * P, :])
 
-        imp_codes = keep.tile([P, A_PASSES, N], U32, name="imp_codes", align_bytes=64)
-        imp_scales = keep.tile([P, A_PASSES, N], U8, name="imp_scales", align_bytes=64)
-        wt_codes = keep.tile([P, T_PASSES, N], U32, name="wt_codes", align_bytes=64)
-        wt_scales = keep.tile([P, T_PASSES, N], U8, name="wt_scales", align_bytes=64)
-        sch_codes = keep.tile([P, Q // P, T_PASSES, P], U32, name="sch_codes", align_bytes=64)
-        sch_scales = keep.tile([P, Q // P, T_PASSES, P], U8, name="sch_scales", align_bytes=64)
+        imp_codes = keep.tile([P, A_PASSES * N], U32, name="imp_codes", align_bytes=64)
+        imp_scales = keep.tile([P, A_PASSES * N], U8, name="imp_scales", align_bytes=64)
+        sch_codes = keep.tile([P, (Q // P) * T_PASSES * P], U32, name="sch_codes", align_bytes=64)
+        sch_scales = keep.tile([P, (Q // P) * T_PASSES * P], U8, name="sch_scales", align_bytes=64)
+        wm_codes = keep.tile([P, STEPS * 2 * CHUNK], U32, name="wm_codes", align_bytes=64)
+        wm_scales = keep.tile([P, STEPS * 2 * CHUNK], U8, name="wm_scales", align_bytes=64)
+        stage = keep.tile([P, 4 * CHUNK * PACK], BF16, name="stage", align_bytes=64)
         tiles = {}
+        free_banks = [f"turn_{b}" for b in range(TURN_BANKS)]
 
-        def bank_tile(shape, name, tag):
-            return psum.tile(shape, F32, name=name, tag=tag, bufs=PSUM_BUFS[tag])
+        def take_bank(key, shape, name, tag=None, dtype=F32):
+            tag = tag or free_banks.pop(0)
+            bank = psum.tile(shape, dtype, name=name, tag=tag, bufs=1)
+            tiles[key] = (bank, tag)
+            return bank
 
-        def baton_tile(name):
-            return work.tile([P, CHUNK, PACK], BF16, name=name, tag="baton", bufs=1, align_bytes=64)
+        def leave_bank(key):
+            bank, tag = tiles.pop(key)
+            if tag.startswith("turn"):
+                free_banks.append(tag)
+            return bank
 
         def move(engine, out, in_):
             if engine == SCALAR:
@@ -119,7 +122,12 @@ def tile_cross_impact_hedge_s8_kernel(
                 nc.vector.tensor_copy(out=out, in_=in_)
 
         def interleave(engine, grouped, planes):
-            move(engine, grouped.rearrange("p (n i) t -> p n t i", i=4), planes.rearrange("p t (n i) -> p n t i", i=4))
+            if engine == GPSIMD:
+                nc.gpsimd.tensor_scalar(
+                    out=grouped, in0=planes.rearrange("p t n -> p n t"), scalar1=1.0, scalar2=0.0, op0=MULT, op1=ADD
+                )
+            else:
+                move(engine, grouped.rearrange("p (n i) t -> p n t i", i=4), planes.rearrange("p t (n i) -> p n t i", i=4))
 
         def quantize(codes, scales, grouped):
             nc.vector.quantize_mx(out=codes.bitcast(FP8X4), scales=scales, in_=grouped)
@@ -135,33 +143,27 @@ def tile_cross_impact_hedge_s8_kernel(
                 stop=final,
             )
 
-        def impact_group(c, chunk, engine, baton=False):
-            half, lo = divmod(chunk * CHUNK, BANK)
-            if baton:
-                grouped = baton_tile(f"ig_{c}_{chunk}")
-            else:
-                grouped = work.tile([P, CHUNK, PACK], BF16, name=f"ig_{c}_{chunk}", tag="grouped", bufs=6, align_bytes=64)
-            tiles["impact", c, chunk] = grouped
-            planes = imp_raw[c, half][:, :, lo : lo + CHUNK]
-            if engine == GPSIMD:
-                nc.gpsimd.tensor_scalar(
-                    out=grouped[:], in0=planes.rearrange("p t n -> p n t"), scalar1=1.0, scalar2=0.0, op0=MULT, op1=ADD
-                )
-            else:
-                interleave(engine, grouped[:], planes)
+        def impact_group(c, half, engine, lo=0, hi=BANK, slot=None):
+            if ("impact", c, half) not in tiles:
+                tag = f"grouped_{c if slot is None else slot}"
+                grouped = work.tile([P, BANK * PACK], BF16, name=f"ig_{c}_{half}", tag=tag, bufs=1, align_bytes=64)
+                tiles["impact", c, half] = grouped
+            grouped = tiles["impact", c, half][:, lo * PACK : hi * PACK].rearrange("p (n t) -> p n t", t=PACK)
+            interleave(engine, grouped, imp_raw[c, half][:, :, lo:hi])
 
-        def impact_quantize(c, chunk):
-            cols = slice(chunk * CHUNK, (chunk + 1) * CHUNK)
-            grouped = tiles.pop(("impact", c, chunk))
-            quantize(imp_codes[:, c, cols], imp_scales[:, c, cols], grouped[:].rearrange("p n t -> p (n t)"))
+        def impact_quantize(c, half, lo=0, hi=BANK):
+            cols = slice(c * N + half * BANK + lo, c * N + half * BANK + hi)
+            quantize(imp_codes[:, cols], imp_scales[:, cols], tiles["impact", c, half][:, lo * PACK : hi * PACK])
 
-        def widen(i, engine=SCALAR, lo=0, hi=A):
-            if lo == 0:
+        def widen(i, engine=SCALAR, lo=0, hi=A, table=False):
+            if ("wide", i) not in tiles:
                 wide = work.tile([P, A], BF16, name=f"wide_{i}", tag="wide", bufs=4, align_bytes=64)
                 tiles["wide", i] = wide
-            q, r = divmod(i, 2)
-            codes = flow_first[:, r, :] if hi < A else flow_sb[q][:, r, :]
-            move(engine, tiles["wide", i][:, lo:hi], codes.bitcast(FP8))
+            codes = flow_sb[i][:, lo:hi].bitcast(FP8)
+            if table:
+                nc.scalar.activation(out=tiles["wide", i][:, lo:hi], in_=codes, func=COPY)
+            else:
+                move(engine, tiles["wide", i][:, lo:hi], codes)
 
         def sort_words(out, rows):
             nc.scalar.copy(out=out, in_=rows.bitcast(F32).rearrange("p (c m u) -> p c u m", m=P, u=2))
@@ -172,49 +174,66 @@ def tile_cross_impact_hedge_s8_kernel(
             return rows.bitcast(F32)[:, 2 * P * c + u : 2 * P * (c + 1) : 2]
 
         def flow_sort(i):
-            words = work.tile([P, A_PASSES, 2, P], F32, name=f"words_{i}", tag="words", bufs=4, align_bytes=64)
+            words = work.tile([P, A_PASSES, 2, P], F32, name=f"words_{i}", tag="words", bufs=2, align_bytes=64)
             tiles["flow_words", i] = words
             sort_words(words[:], tiles["wide", i][:])
 
-        def flow_transpose(q, c):
-            bank = bank_tile([P, 2, 2, P], f"xt_{q}_{c}", "turned_x")
-            tiles["turned_flow", q, c] = bank
-            for r in range(2):
-                i = 2 * q + r
+        def flow_transpose(i, lo, hi, tag=None):
+            bank = take_bank(("turned_flow", i, lo), [P, 2, hi - lo, P], f"xt_{i}_{lo}", tag)
+            for c in range(lo, hi):
                 for u in range(2):
-                    nc.tensor.transpose(bank[:, u, r, :], words_of(("flow_words", i), tiles["wide", i][:], c, u), ident[:])
+                    nc.tensor.transpose(bank[:, u, c - lo, :], words_of(("flow_words", i), tiles["wide", i][:], c, u), ident[:])
 
-        def flow_scale_out(q, c, lo=0, hi=2, baton=False):
-            if baton:
-                tiles["flow", q, c] = baton_tile(f"fg_{q}_{c}")
-            elif lo == 0:
-                grouped = work.tile([P, 2 * P, PACK], BF16, name=f"fg_{q}_{c}", tag="flow", bufs=4, align_bytes=64)
-                tiles["flow", q, c] = grouped
-            values = tiles["turned_flow", q, c][:].rearrange("p u r m -> p (u r m)").bitcast(BF16)
-            rows = slice(lo * P, hi * P)
-            scales = scale_sb[:, c, :].rearrange("p (u e) -> p u e", u=2)
+        def flow_scale_out(i, lo, hi):
+            if ("flow", i) not in tiles:
+                grouped = work.tile([P, A], BF16, name=f"fg_{i}", tag="flow", bufs=3, align_bytes=64)
+                tiles["flow", i] = grouped
+            n = hi - lo
+            values = leave_bank(("turned_flow", i, lo))[:].rearrange("p u c m -> p (u c m)").bitcast(BF16)
+            scales = scale_sb[:, lo:hi, :].rearrange("p c (u e) -> p c u e", u=2)
             nc.vector.tensor_tensor(
-                out=tiles["flow", q, c][:, rows, :].rearrange("p m (u e) -> p m u e", u=2),
-                in0=values.rearrange("p (u m e) -> p m u e", u=2, e=2)[:, rows, :, :],
-                in1=scales.unsqueeze(1).to_broadcast([P, (hi - lo) * P, 2, 2]),
+                out=tiles["flow", i][:, lo * K_PASS : hi * K_PASS].rearrange("p (c m u e) -> p c m u e", c=n, u=2, e=2),
+                in0=values.rearrange("p (u c m e) -> p c m u e", u=2, c=n, e=2),
+                in1=scales.unsqueeze(2).to_broadcast([P, n, P, 2, 2]),
                 op=MULT,
             )
 
-        def flow_quantize(q, c):
-            codes = work.tile([P, 2 * P], U32, name=f"fc_{q}_{c}", tag="flow_codes", bufs=9, align_bytes=64)
-            scales = work.tile([P, 2 * P], U8, name=f"fs_{q}_{c}", tag="flow_scales", bufs=9, align_bytes=64)
-            tiles["flow_codes", q, c] = (codes, scales)
-            quantize(codes[:], scales[:], tiles.pop(("flow", q, c))[:].rearrange("p m t -> p (m t)"))
+        def last_transpose(q):
+            bank = take_bank(("turned_last", q), [P, 2, 2, P], f"xl_{q}")
+            for r in range(2):
+                i = 2 * q + r
+                for u in range(2):
+                    nc.tensor.transpose(bank[:, u, r, :], words_of(("flow_words", i), tiles["wide", i][:], 2, u), ident[:])
 
-        def impact_matmul(i, half):
+        def last_scale_out(i, lo=0, hi=P):
             q, r = divmod(i, 2)
-            z = bank_tile([P, BANK], f"z_{i}_{half}", "z")
-            tiles["z", i, half] = z
-            cols = slice(half * BANK, (half + 1) * BANK)
-            rows = slice(r * P, (r + 1) * P)
+            if ("flow", i) not in tiles:
+                grouped = work.tile([P, A], BF16, name=f"fg_{i}", tag="flow", bufs=3, align_bytes=64)
+                tiles["flow", i] = grouped
+            bank = leave_bank(("turned_last", q)) if (r, hi) == (1, P) else tiles["turned_last", q][0]
+            values = bank[:].rearrange("p u r m -> p (u r m)").bitcast(BF16).rearrange("p (u m e) -> p m u e", u=2, e=2)
+            scales = scale_sb[:, 2, :].rearrange("p (u e) -> p u e", u=2)
+            out = tiles["flow", i][:, 2 * K_PASS + lo * PACK : 2 * K_PASS + hi * PACK]
+            nc.vector.tensor_tensor(
+                out=out.rearrange("p (m u e) -> p m u e", u=2, e=2),
+                in0=values[:, r * P + lo : r * P + hi, :, :],
+                in1=scales.unsqueeze(1).to_broadcast([P, hi - lo, 2, 2]),
+                op=MULT,
+            )
+
+        def flow_quantize(i):
+            codes = work.tile([P, A_PASSES * P], U32, name=f"fc_{i}", tag="flow_codes", bufs=5, align_bytes=64)
+            scales = work.tile([P, A_PASSES * P], U8, name=f"fs_{i}", tag="flow_scales", bufs=5, align_bytes=64)
+            tiles["flow_codes", i] = (codes, scales)
+            quantize(codes[:], scales[:], tiles.pop(("flow", i))[:])
+
+        def impact_matmul(i, half, tag):
+            z = take_bank(("z", i, half), [P, BANK], f"z_{i}_{half}", tag)
+            codes, scales = tiles["flow_codes", i]
             for c in range(A_PASSES):
-                codes, scales = tiles["flow_codes", q, c]
-                moving = (imp_codes[:, c, cols], imp_scales[:, c, cols])
+                rows = slice(c * P, (c + 1) * P)
+                cols = slice(c * N + half * BANK, c * N + (half + 1) * BANK)
+                moving = (imp_codes[:, cols], imp_scales[:, cols])
                 multiply(z[:], (codes[:, rows], scales[:, rows]), moving, c == 0, c == A_PASSES - 1)
 
         def saturate(i, half):
@@ -224,61 +243,85 @@ def tile_cross_impact_hedge_s8_kernel(
                 tiles["h", g, half] = h
             nc.scalar.activation(
                 out=tiles["h", g, half][:, j, :].rearrange("p (t m) -> p t m", t=PACK),
-                in_=tiles.pop(("z", i, half))[:].rearrange("p (m t) -> p t m", t=PACK),
+                in_=leave_bank(("z", i, half))[:].rearrange("p (m t) -> p t m", t=PACK),
                 func=TANH,
             )
 
-        def weigh_chunk(g, chunk):
+        STAGE = CHUNK * PACK
+
+        def weigh_chunk(k):
+            g, chunk = divmod(k, PACK)
             half, lo = divmod(chunk * CHUNK, BANK)
-            grouped = baton_tile(f"wg_{g}_{chunk}")
-            tiles["weighted", g, chunk] = grouped
             nc.gpsimd.tensor_tensor(
-                out=grouped[:],
+                out=weighted_stage(k).rearrange("p (n j) -> p n j", j=PACK),
                 in0=tiles["h", g, half][:, :, lo : lo + CHUNK].rearrange("p j n -> p n j"),
                 in1=depth_f32[:, g, :].unsqueeze(1).to_broadcast([P, CHUNK, PACK]),
                 op=MULT,
             )
 
-        def weigh_plane(g, half, j, lo=0):
-            if j == 0:
+        def weigh_plane(g, half, j, lo=0, hi=BANK, engine=SCALAR):
+            if ("planes", g, half) not in tiles:
                 planes = work.tile([P, PACK, BANK], BF16, name=f"planes_{g}_{half}", tag="raw", bufs=6, align_bytes=64)
-                tiles["weighted_planes", g, half] = planes
-            nc.scalar.activation(
-                out=tiles["weighted_planes", g, half][:, j, lo:],
-                in_=tiles["h", g, half][:, j, lo:],
-                func=COPY,
-                scale=depth_f32[:, g, j : j + 1],
-            )
+                tiles["planes", g, half] = planes
+            out, in_ = tiles["planes", g, half][:, j, lo:hi], tiles["h", g, half][:, j, lo:hi]
+            if engine == SCALAR:
+                nc.scalar.activation(out=out, in_=in_, func=COPY, scale=depth_f32[:, g, j : j + 1])
+            else:
+                nc.vector.tensor_scalar(out=out, in0=in_, scalar1=depth_f32[:, g, j : j + 1], scalar2=None, op0=MULT)
 
-        def weighted_group(g, chunk, engine):
+        def weighted_group(k, engine):
+            g, chunk = divmod(k, PACK)
             half, lo = divmod(chunk * CHUNK, BANK)
-            grouped = work.tile([P, CHUNK, PACK], BF16, name=f"wp_{g}_{chunk}", tag="grouped", bufs=6, align_bytes=64)
-            tiles["weighted", g, chunk] = grouped
-            interleave(engine, grouped[:], tiles["weighted_planes", g, half][:, :, lo : lo + CHUNK])
+            grouped = work.tile([P, STAGE], BF16, name=f"wp_{k}", tag="late", bufs=3, align_bytes=64)
+            tiles["weighted", k] = grouped
+            interleave(engine, grouped[:].rearrange("p (n t) -> p n t", t=PACK), tiles["planes", g, half][:, :, lo : lo + CHUNK])
 
-        def weighted_quantize(g, chunk):
-            cols = slice(chunk * CHUNK, (chunk + 1) * CHUNK)
-            grouped = tiles.pop(("weighted", g, chunk))
-            quantize(wt_codes[:, g, cols], wt_scales[:, g, cols], grouped[:].rearrange("p n t -> p (n t)"))
+        def weighted_cols(k):
+            lo = (2 * k + 1 - k % 2) * CHUNK
+            return slice(lo, lo + CHUNK)
 
-        def moves_transpose(i, half, tag="turned_h"):
+        def moves_cols(step):
+            k = (step - 1) % STEPS
+            lo = (2 * k + k % 2) * CHUNK
+            return slice(lo, lo + CHUNK)
+
+        extra = keep.tile([P, STAGE], BF16, name="extra", align_bytes=64)
+
+        def weighted_stage(k):
+            lo = (1 + k % 2) * STAGE if k < 12 else 2 * STAGE
+            return stage[:, lo : lo + STAGE]
+
+        def moves_stage(step):
+            if step == 0:
+                return weighted_stage(0)
+            if step == 13:
+                return extra[:]
+            lo = 3 * STAGE * ((step - 1) % 2)
+            return stage[:, lo : lo + STAGE]
+
+        def weighted_quantize(k):
+            grouped = tiles.pop(("weighted", k))[:] if ("weighted", k) in tiles else weighted_stage(k)
+            quantize(wm_codes[:, weighted_cols(k)], wm_scales[:, weighted_cols(k)], grouped)
+
+        def moves_quantize(step):
+            quantize(wm_codes[:, moves_cols(step)], wm_scales[:, moves_cols(step)], moves_stage(step))
+
+        def both_quantize(k):
+            cols = slice(2 * k * CHUNK, 2 * (k + 1) * CHUNK)
+            lo = 2 * STAGE * (k % 2)
+            quantize(wm_codes[:, cols], wm_scales[:, cols], stage[:, lo : lo + 2 * STAGE])
+
+        def moves_transpose(i, half, tag=None):
             g, j = divmod(i, PACK)
-            bank = bank_tile([P, PACK, P], f"ht_{i}_{half}", tag)
-            tiles["turned_h", i, half] = bank
+            bank = take_bank(("turned_h", i, half), [P, PACK, P], f"ht_{i}_{half}", tag)
             for t in range(PACK):
                 nc.tensor.transpose(bank[:, t, :], tiles["h", g, half][:, j, t * P : (t + 1) * P], ident[:])
 
-        def moves_tile(i, half):
-            q, r = divmod(i, 2)
-            if ("moves", q, half) not in tiles:
-                grouped = work.tile([P, 2, P, PACK], BF16, name=f"mg_{q}_{half}", tag="moves", bufs=3, align_bytes=64)
-                tiles["moves", q, half] = grouped
-            return tiles["moves", q, half][:, r, :, :]
-
         def moves_scale(i, half):
+            q, r = divmod(i, 2)
             nc.vector.tensor_tensor(
-                out=moves_tile(i, half),
-                in0=tiles.pop(("turned_h", i, half))[:].rearrange("p t m -> p m t"),
+                out=moves_stage(2 * q + half)[:, r * K_PASS : (r + 1) * K_PASS].rearrange("p (m t) -> p m t", t=PACK),
+                in0=leave_bank(("turned_h", i, half))[:].rearrange("p t m -> p m t"),
                 in1=vol_bf[:, half, :].unsqueeze(1).to_broadcast([P, P, PACK]),
                 op=MULT,
             )
@@ -286,280 +329,287 @@ def tile_cross_impact_hedge_s8_kernel(
         def moves_planes(i, half):
             planes = work.tile([P, PACK, P], BF16, name=f"mp_{i}_{half}", tag="moves_planes", bufs=2, align_bytes=64)
             tiles["moves_planes", i, half] = planes
-            bank = tiles.pop(("turned_h", i, half))
+            bank = leave_bank(("turned_h", i, half))
             for t in range(PACK):
                 nc.scalar.activation(out=planes[:, t, :], in_=bank[:, t, :], func=COPY, scale=vol_f32[:, half, t : t + 1])
 
         def moves_group(i, half):
-            interleave(SCALAR, moves_tile(i, half), tiles.pop(("moves_planes", i, half))[:])
-
-        def moves_quantize(q, half):
-            codes = work.tile([P, 2 * P], U32, name=f"mc_{q}_{half}", tag="moves_codes", bufs=5, align_bytes=64)
-            scales = work.tile([P, 2 * P], U8, name=f"ms_{q}_{half}", tag="moves_scales", bufs=5, align_bytes=64)
-            tiles["moves_codes", q, half] = (codes, scales)
-            quantize(codes[:], scales[:], tiles.pop(("moves", q, half))[:].rearrange("p r m t -> p (r m t)"))
+            q, r = divmod(i, 2)
+            grouped = moves_stage(2 * q + half)[:, r * K_PASS : (r + 1) * K_PASS].rearrange("p (m t) -> p m t", t=PACK)
+            interleave(SCALAR, grouped, tiles.pop(("moves_planes", i, half))[:])
 
         def hedge_matmul(i, tag="hedge"):
             q, r = divmod(i, 2)
-            bank = bank_tile([P, R], f"hg_{i}", tag)
-            tiles["hedge", i] = bank
-            rows = slice(r * P, (r + 1) * P)
+            bank = take_bank(("hedge", i), [P, R], f"hg_{i}", tag)
             for half in range(N_PASSES):
-                codes, scales = tiles["moves_codes", q, half]
+                lo = moves_cols(2 * q + half).start + r * P
+                rows = slice(lo, lo + P)
                 moving = (w_words[:, half, :], w_scales[:, half, :])
-                multiply(bank[:], (codes[:, rows], scales[:, rows]), moving, half == 0, half == N_PASSES - 1, FP4X4)
+                multiply(bank[:], (wm_codes[:, rows], wm_scales[:, rows]), moving, half == 0, half == N_PASSES - 1, FP4X4)
 
         hedge_view = hedge.rearrange("(g p j) r -> g j p r", p=P, j=PACK)
 
         def hedge_store(i, engine=SCALAR):
             g, j = divmod(i, PACK)
             result = work.tile([P, R], F32, name=f"hr_{i}", tag="hedge_out", bufs=4, align_bytes=64)
-            move(engine, result[:], tiles.pop(("hedge", i))[:])
+            move(engine, result[:], leave_bank(("hedge", i))[:])
             nc.sync.dma_start(out=hedge_view[g, j], in_=result[:])
 
-        def sched_sort(qt):
-            words = work.tile([P, T_PASSES, 2, P], F32, name=f"sched_words_{qt}", tag="raw", bufs=6, align_bytes=64)
-            tiles["sched_words", qt] = words
-            sort_words(words[:], sched_sb[qt][:])
+        sched_grouped = keep.tile([P, 3 * STAGE], BF16, name="sched_grouped", align_bytes=64)
 
-        def sched_transpose(b, tag="turned_x"):
+        def sched_stage(b):
+            if b == 0:
+                return weighted_stage(1)
+            return sched_grouped[:, STAGE * (b - 1) : STAGE * b]
+
+        def sched_transpose(b, tag=None):
             qt, two = divmod(b, 2)
-            bank = bank_tile([P, 2, 2, P], f"st_{b}", tag)
-            tiles["turned_sched", b] = bank
+            bank = take_bank(("turned_sched", b), [P, 2, 2, P], f"st_{b}", tag)
             for s in range(2):
                 for u in range(2):
                     words = words_of(("sched_words", qt), sched_sb[qt][:], 2 * two + s, u)
                     nc.tensor.transpose(bank[:, s, u, :], words, ident[:])
 
-        def sched_group(b):
-            grouped = work.tile([P, 2, P, PACK], BF16, name=f"sg_{b}", tag="sched", bufs=4, align_bytes=64)
-            tiles["sched", b] = grouped
-            words = grouped[:].rearrange("p s q t -> p (s q t)").bitcast(F32)
-            nc.scalar.copy(
-                out=words.rearrange("p (s q u) -> p s q u", s=2, u=2),
-                in_=tiles.pop(("turned_sched", b))[:].rearrange("p s u q -> p s q u"),
-            )
+        def sched_group(b, engine=SCALAR):
+            words = sched_stage(b).bitcast(F32)
+            bank = leave_bank(("turned_sched", b))
+            move(engine, words.rearrange("p (s q u) -> p s q u", s=2, u=2), bank[:].rearrange("p s u q -> p s q u"))
 
-        def sched_quantize(b):
-            qt, two = divmod(b, 2)
-            passes = slice(2 * two, 2 * two + 2)
-            quantize(
-                sch_codes[:, qt, passes, :].rearrange("p s q -> p (s q)"),
-                sch_scales[:, qt, passes, :].rearrange("p s q -> p (s q)"),
-                tiles.pop(("sched", b))[:].rearrange("p s q t -> p (s q t)"),
-            )
+        def sched_quantize(b, parts=1):
+            cols = slice(b * 2 * P, (b + parts) * 2 * P)
+            grouped = sched_stage(b) if parts == 1 else sched_grouped[:, STAGE * (b - 1) : STAGE * (b - 1 + parts)]
+            quantize(sch_codes[:, cols], sch_scales[:, cols], grouped)
 
-        def cost_matmul(qt, half, passes, tag="turned_x"):
+        def cost_matmul(qt, half, passes, tag=None):
             if passes[0] == 0:
-                tiles["cost", qt, half] = bank_tile([P, BANK], f"cost_{qt}_{half}", tag)
-            cols = slice(half * BANK, (half + 1) * BANK)
+                take_bank(("cost", qt, half), [P, BANK], f"cost_{qt}_{half}", tag)
+            bank = tiles["cost", qt, half][0]
             for g in passes:
-                stationary = (sch_codes[:, qt, g, :], sch_scales[:, qt, g, :])
-                moving = (wt_codes[:, g, cols], wt_scales[:, g, cols])
-                multiply(tiles["cost", qt, half][:], stationary, moving, g == 0, g == T_PASSES - 1)
+                rows = slice((qt * T_PASSES + g) * P, (qt * T_PASSES + g + 1) * P)
+                lo = weighted_cols(PACK * g + 2 * half).start
+                moving = (wm_codes[:, lo : lo + BANK], wm_scales[:, lo : lo + BANK])
+                multiply(bank[:], (sch_codes[:, rows], sch_scales[:, rows]), moving, g == 0, g == T_PASSES - 1)
 
         def cost_store(qt, half, engine, pieces=1):
-            bank = tiles.pop(("cost", qt, half))
+            bank = leave_bank(("cost", qt, half))
             width = BANK // pieces
             for lo in range(0, BANK, width):
-                result = work.tile([P, width], F32, name=f"cr_{qt}_{half}_{lo}", tag="cost_out", bufs=5, align_bytes=64)
+                result = work.tile([P, width], F32, name=f"cr_{qt}_{half}_{lo}", tag="raw", bufs=6, align_bytes=64)
                 sums = bank[:].rearrange("p (t m) -> p m t", t=PACK)[:, lo // PACK : (lo + width) // PACK, :]
                 move(engine, result[:].rearrange("p (m t) -> p m t", t=PACK), sums)
                 col = half * BANK + lo
                 nc.sync.dma_start(out=cost[qt * P : (qt + 1) * P, col : col + width], in_=result[:])
 
         nc.scalar.dma_start(out=scale_sb[:], in_=flow_scale.rearrange("o (c p t) -> p (o c) t", p=P, t=PACK))
-        nc.scalar.dma_start(out=depth_bf[:], in_=depth.rearrange("(g p j) -> p g j", p=P, j=PACK))
-        nc.scalar.activation(out=depth_f32[:], in_=depth_bf[:], func=COPY)
-        nc.sync.dma_start(out=flow_first[:], in_=flow_view[0, :, 0:2, 0:K_PASS])
-        load_flow(0)
-        load_impact(0)
-        load_flow(1)
-        load_impact(1)
-        load_sched(0)
-        load_flow(2)
+        load_flow(0, 1)
+        load_flow(1, 1)
+        load_impact(0, 0)
+        load_impact(1, 0)
+        load_flow(2, 1)
+        load_impact(2, 0)
+        load_flow(3, 1)
+        for c in range(A_PASSES):
+            load_impact(c, 1)
+        load_flow(4, 2)
         nc.sync.dma_start(out=vol_bf[:], in_=vol.rearrange("(g p j) -> p g j", p=P, j=PACK))
+        load_sched(0)
+        load_flow(6, 2)
+        nc.sync.dma_start(out=depth_bf[:], in_=depth.rearrange("(g p j) -> p g j", p=P, j=PACK))
         load_sens()
-        load_flow(3)
-        load_flow(4)
+        for first in range(8, TILES, 2):
+            load_flow(first, 2)
         load_sched(1)
-        for q in range(5, PAIRS):
-            load_flow(q)
 
-        for lo, hi in ((0, K_PASS), (K_PASS, A)):
-            widen(0, VECTOR, lo, hi)
-            widen(1, SCALAR, lo, hi)
-            for c in range(lo // K_PASS, hi // K_PASS):
-                flow_transpose(0, c)
+        widen(0, VECTOR, 0, K_PASS)
+        widen(0, SCALAR, K_PASS, 2 * K_PASS, table=True)
+        widen(0, SCALAR, 2 * K_PASS, A)
+        widen(1, VECTOR, 0, 2 * K_PASS)
+        widen(1, SCALAR, 2 * K_PASS, A)
+        for c in range(A_PASSES):
+            flow_transpose(0, c, c + 1)
+        flow_transpose(1, 0, 2)
+        flow_transpose(1, 2, 3)
         for c in range(A_PASSES - 1):
-            impact_group(c, 0, SCALAR)
-            impact_group(c, 1, GPSIMD)
-        impact_group(A_PASSES - 1, 0, SCALAR)
+            impact_group(c, 0, SCALAR, 0, CHUNK)
+            impact_group(c, 0, GPSIMD, CHUNK, BANK)
+        for c in range(A_PASSES):
+            flow_scale_out(0, c, c + 1)
+        flow_scale_out(1, 0, 2)
+        flow_scale_out(1, 2, 3)
         widen(2)
+        impact_group(2, 0, SCALAR, 0, CHUNK)
+        impact_group(2, 0, VECTOR, CHUNK, BANK)
         widen(3)
-        for c in range(A_PASSES):
-            flow_scale_out(0, c)
-        impact_group(A_PASSES - 1, 1, VECTOR, baton=True)
-        for c in range(A_PASSES):
-            flow_transpose(1, c)
-        for c in range(A_PASSES):
-            impact_quantize(c, 0)
-            impact_quantize(c, 1)
-            flow_quantize(0, c)
-        for c in range(A_PASSES - 1):
-            impact_group(c, 2, SCALAR)
-            impact_group(c, 3, GPSIMD, baton=(c == 0))
-        impact_group(A_PASSES - 1, 2, SCALAR)
-        for c in range(A_PASSES):
-            flow_scale_out(1, c)
+        for i in (2, 3):
+            flow_transpose(i, 0, 2)
+            flow_transpose(i, 2, 3)
+        impact_quantize(0, 0)
+        flow_quantize(0)
+        impact_quantize(1, 0)
+        impact_quantize(2, 0)
+        flow_quantize(1)
+        impact_group(0, 1, SCALAR, slot=0)
+        impact_group(1, 1, GPSIMD, slot=2)
+        impact_group(2, 1, SCALAR, 0, CHUNK, slot=1)
         for i in range(2):
-            impact_matmul(i, 0)
-        sched_transpose(0, "hedge")
-        sched_transpose(1)
-        impact_group(A_PASSES - 1, 3, SCALAR)
-        for i in range(2):
+            impact_matmul(i, 0, f"z_{i}")
             saturate(i, 0)
+        impact_group(2, 1, SCALAR, CHUNK, BANK)
+        for i in (2, 3):
+            flow_scale_out(i, 0, 2)
+            flow_scale_out(i, 2, 3)
         widen(4)
         widen(5)
-        sched_group(1)
-        for c in range(A_PASSES):
-            impact_quantize(c, 2)
-            impact_quantize(c, 3)
-        for c in range(A_PASSES - 1):
-            flow_quantize(1, c)
+        sched_transpose(0, "hedge")
         for i in range(2):
             moves_transpose(i, 0)
+        for c in range(A_PASSES):
+            impact_quantize(c, 1)
         for i in range(2):
-            impact_matmul(i, 1)
+            impact_matmul(i, 1, f"z_{i}")
             saturate(i, 1)
-        for i in range(2):
-            moves_scale(i, 0)
-        flow_quantize(1, A_PASSES - 1)
-        moves_quantize(0, 0)
+        flow_quantize(2)
+        flow_quantize(3)
         widen(6)
+        nc.scalar.copy(out=depth_f32[:], in_=depth_bf[:])
         nc.scalar.copy(out=vol_f32[:], in_=vol_bf[:])
+        sched_group(0)
 
         last = T_PASSES - 1
-        for s in range(2, STEPS - 1):
+        for s in range(2, STEPS - 2):
             q, half = divmod(s, 2)
-            ahead = q + 1
-            flowing = ahead < PAIRS
-            moved_pair, moved_half = divmod(s - 1, 2)
+            ahead = s + 2
+            moved_pair, moved_half = divmod(s - 2, 2)
             first, second = 2 * moved_pair, 2 * moved_pair + 1
-            chunk = divmod(s - 3, PACK) if s >= 3 else None
             shared = s in SHARED_STEPS
-            split = s - half not in SHARED_STEPS
-            sched_part = s - SCHED_SORT_STEP if s - SCHED_SORT_STEP in (2, 3) else None
+            cut = P // 2 if s - half in SHARED_STEPS else 0
 
-            if chunk and flowing:
-                weigh_chunk(*chunk)
-            if flowing and split and half == 1:
-                flow_scale_out(ahead, 1, 1, 2)
-
+            if s >= 3:
+                weigh_chunk(s - 3)
             if shared:
                 moves_transpose(first, moved_half)
-            if flowing:
-                for c in ((0, 1), (2,))[half]:
-                    flow_transpose(ahead, c)
-            if sched_part:
-                sched_transpose(sched_part)
-            if not shared:
-                moves_transpose(first, moved_half)
-            moves_transpose(second, moved_half)
+            flow_transpose(ahead, 0, 2)
+            if half == 0:
+                last_transpose(q + 1)
+            if s == 4:
+                sched_transpose(1, "hedge")
+            if s == 13:
+                sched_transpose(2)
+            if s > 2:
+                if not shared:
+                    moves_transpose(first, moved_half)
+                moves_transpose(second, moved_half)
 
-            if s >= 4:
-                hedge_store(s - 4)
             if shared:
                 moves_planes(first, moved_half)
-            if FIRST_SORTED <= s + 4 < TILES and not shared:
-                flow_sort(s + 4)
-            if s + 5 < TILES:
-                widen(s + 5)
+            moves_scale(second, moved_half)
+            if not shared:
+                moves_scale(first, moved_half)
+            flow_scale_out(ahead, 0, 2)
+            if half == 0:
+                last_scale_out(ahead)
+                if cut:
+                    last_scale_out(ahead + 1, 0, cut)
+            else:
+                last_scale_out(ahead, cut, P)
+            if s > 3:
+                both_quantize(s - 4)
+            elif s == 3:
+                sched_quantize(0)
+            else:
+                moves_quantize(0)
+            flow_quantize(ahead)
+
+            if s == 4:
+                sched_group(1)
+            if s == 13:
+                sched_group(2)
+            impact_matmul(2 * q, half, "z_0")
+            saturate(2 * q, half)
+            if s >= 5:
+                hedge_matmul(s - 5)
             if shared:
                 moves_group(first, moved_half)
-            if s == SCHED_SORT_STEP:
-                sched_sort(1)
-            if s == SCHED_SORT_STEP + 1:
-                for j in range(PACK):
-                    weigh_plane(last - 1, 1, j, CHUNK)
-                weighted_group(last - 1, 3, SCALAR)
-            if first >= PACK * last:
-                weigh_plane(last, moved_half, first % PACK)
-                weigh_plane(last, moved_half, second % PACK)
+            elif half == 1 and s + 5 < TILES:
+                widen(s + 5)
+            impact_matmul(2 * q + 1, half, "z_1")
+            saturate(2 * q + 1, half)
+            if s >= 5:
+                hedge_store(s - 5)
+            if half == 1 and s + 6 < TILES:
+                widen(s + 6)
+            if half == 0 and FIRST_SORTED <= s + 4 < TILES:
+                flow_sort(s + 4)
             if s == 2:
-                sched_group(0)
-            if sched_part:
-                sched_group(sched_part)
-
-            moves_first = s >= STEPS - 3
-            if moves_first:
-                moves_scale(first, moved_half)
-                moves_scale(second, moved_half)
-            if flowing and half == 0:
-                flow_scale_out(ahead, 0, baton=(s == 2))
-                flow_scale_out(ahead, 1, 0, 1 if split else 2)
-            if flowing and half == 1:
-                flow_scale_out(ahead, 2)
-            if not moves_first:
-                if not shared:
-                    moves_scale(first, moved_half)
-                moves_scale(second, moved_half)
-
-            if flowing:
-                for c in (((0,), (1, 2)) if split else ((0, 1), (2,)))[half]:
-                    flow_quantize(ahead, c)
-            if s == STEPS - 2:
-                for b in range(4):
-                    sched_quantize(b)
-            if chunk:
-                weighted_quantize(*chunk)
-            moves_quantize(moved_pair, moved_half)
-
-            for i in (2 * q, 2 * q + 1):
-                impact_matmul(i, half)
-                saturate(i, half)
-            if s >= 3:
-                hedge_matmul(s - 3)
+                widen(7)
+            if s == 11:
+                words = work.tile([P, T_PASSES, 2, P], F32, name="sched_words", tag="raw", bufs=6, align_bytes=64)
+                tiles["sched_words", 1] = words
+                sort_words(words[:], sched_sb[1][:])
+            if 2 * q >= PACK * last:
+                for j in range(2):
+                    weigh_plane(last, half, j, 0 if half else CHUNK)
 
         final = (TILES - 2, TILES - 1)
-        for i in final:
-            weigh_plane(last, 0, i % PACK)
-        for i in final:
-            impact_matmul(i, 1)
-            saturate(i, 1)
-        hedge_matmul(TILES - 4, "turned_x")
-        for i in final:
-            moves_transpose(i, 0)
-        for i in final:
-            moves_transpose(i, 1, "z")
-            weigh_plane(last, 1, i % PACK)
-        for chunk in range(2):
-            weighted_group(last, chunk, VECTOR)
-        for chunk in range(2):
-            weighted_quantize(last, chunk)
+        weigh_chunk(11)
+        sched_transpose(3)
         for half in range(N_PASSES):
-            for i in final:
+            for i in (12, 13):
+                moves_transpose(i, half)
+        sched_group(3)
+        for half in range(N_PASSES):
+            for i in (12, 13):
                 moves_scale(i, half)
-        weighted_group(last, 3, SCALAR)
-        hedge_store(TILES - 5)
-        hedge_store(TILES - 4)
-        moves_quantize(PAIRS - 1, 0)
-        weighted_group(last, 2, VECTOR)
-        moves_quantize(PAIRS - 1, 1)
-        weighted_quantize(last, 2)
-        weighted_quantize(last, 3)
-        for qt in range(Q // P):
-            cost_matmul(qt, 0, range(T_PASSES))
-        hedge_matmul(TILES - 3)
-        cost_matmul(0, 1, range(last), "turned_h")
+        hedge_matmul(9)
+        impact_matmul(14, 0, "z_0")
+        impact_matmul(14, 1, "z_1")
+        impact_matmul(15, 0, None)
+        impact_matmul(15, 1, None)
+        hedge_store(9)
+        saturate(14, 0)
+        saturate(14, 1)
+        weigh_plane(last, 0, 2, CHUNK)
+        saturate(15, 0)
+        saturate(15, 1)
+        weigh_plane(last, 0, 3, CHUNK)
+        weigh_plane(last, 1, 2)
+        weigh_plane(last, 1, 3)
+        both_quantize(10)
+        moves_quantize(13)
+        sched_quantize(2, 2)
+        both_quantize(11)
+        weigh_chunk(12)
+        sched_quantize(1)
+        moves_transpose(14, 0, "z_0")
+        moves_transpose(14, 1, "z_1")
+        moves_transpose(15, 0)
+        moves_transpose(15, 1)
+        hedge_matmul(10)
+        for i in (11, 12, 13):
+            hedge_matmul(i, None)
         for i in final:
-            hedge_matmul(i, "z")
-        cost_matmul(0, 1, [last])
-        cost_matmul(1, 1, range(T_PASSES), "turned_h")
+            for half in range(N_PASSES):
+                moves_scale(i, half)
+        weighted_group(13, SCALAR)
+        for i in (10, 11, 12, 13):
+            hedge_store(i)
+        moves_quantize(14)
+        weighted_quantize(12)
+        weighted_quantize(13)
+        moves_quantize(15)
+        weighted_group(14, VECTOR)
+        weighted_group(15, VECTOR)
+        weighted_quantize(14)
+        weighted_quantize(15)
+        cost_matmul(0, 0, range(T_PASSES), "z_0")
+        cost_matmul(1, 0, range(T_PASSES), "z_1")
+        hedge_matmul(14)
+        hedge_matmul(15, None)
+        cost_matmul(0, 1, range(T_PASSES))
+        cost_matmul(1, 1, range(T_PASSES))
         cost_store(0, 0, SCALAR)
-        cost_store(1, 0, SCALAR)
-        hedge_store(TILES - 3, VECTOR)
-        hedge_store(TILES - 2, SCALAR)
-        hedge_store(TILES - 1, VECTOR)
+        cost_store(1, 0, VECTOR)
+        hedge_store(14, SCALAR)
+        hedge_store(15, VECTOR)
         cost_store(0, 1, SCALAR)
-        cost_store(1, 1, SCALAR, pieces=2)
+        cost_store(1, 1, VECTOR, pieces=2)

@@ -33,9 +33,9 @@ BANK = 512
 CHUNK = 256
 SCALAR, VECTOR, GPSIMD = "scalar", "vector", "gpsimd"
 
-FIRST_SORTED = 6
-SORT_EVERY = 2
-SHARED_STEPS = (4, 6, 8, 10, 12)
+SORTED = (6, 8, 10, 12, 14)
+SHARED_STEPS = (6, 8, 10, 12)
+ORDER = [(0, 0), (1, 0), (0, 1), (1, 1)] + [divmod(s, 2) for s in range(4, STEPS)]
 TURN_BANKS = 5
 
 
@@ -99,7 +99,7 @@ def tile_cross_impact_hedge_s8_kernel(
         sch_scales = keep.tile([P, (Q // P) * T_PASSES * P], U8, name="sch_scales", align_bytes=64)
         wm_codes = keep.tile([P, STEPS * 2 * CHUNK], U32, name="wm_codes", align_bytes=64)
         wm_scales = keep.tile([P, STEPS * 2 * CHUNK], U8, name="wm_scales", align_bytes=64)
-        stage = keep.tile([P, 4 * CHUNK * PACK], BF16, name="stage", align_bytes=64)
+        stage = keep.tile([P, 6 * CHUNK * PACK], BF16, name="stage", align_bytes=64)
         tiles = {}
         free_banks = [f"turn_{b}" for b in range(TURN_BANKS)]
 
@@ -169,14 +169,14 @@ def tile_cross_impact_hedge_s8_kernel(
             nc.scalar.copy(out=out, in_=rows.bitcast(F32).rearrange("p (c m u) -> p c u m", m=P, u=2))
 
         def words_of(key, rows, c, u):
-            if key in tiles:
+            if key in tiles and c < tiles[key].shape[1]:
                 return tiles[key][:, c, u, :]
             return rows.bitcast(F32)[:, 2 * P * c + u : 2 * P * (c + 1) : 2]
 
-        def flow_sort(i):
-            words = work.tile([P, A_PASSES, 2, P], F32, name=f"words_{i}", tag="words", bufs=2, align_bytes=64)
+        def flow_sort(i, passes=A_PASSES):
+            words = work.tile([P, passes, 2, P], F32, name=f"words_{i}", tag="words", bufs=2, align_bytes=64)
             tiles["flow_words", i] = words
-            sort_words(words[:], tiles["wide", i][:])
+            sort_words(words[:], tiles["wide", i][:, : passes * K_PASS])
 
         def flow_transpose(i, lo, hi, tag=None):
             bank = take_bank(("turned_flow", i, lo), [P, 2, hi - lo, P], f"xt_{i}_{lo}", tag)
@@ -251,7 +251,7 @@ def tile_cross_impact_hedge_s8_kernel(
 
         def weigh_chunk(k):
             g, chunk = divmod(k, PACK)
-            half, lo = divmod(chunk * CHUNK, BANK)
+            half, lo = chunk // 2, (0, 1, 1, 0)[chunk] * CHUNK
             nc.gpsimd.tensor_tensor(
                 out=weighted_stage(k).rearrange("p (n j) -> p n j", j=PACK),
                 in0=tiles["h", g, half][:, :, lo : lo + CHUNK].rearrange("p j n -> p n j"),
@@ -271,32 +271,32 @@ def tile_cross_impact_hedge_s8_kernel(
 
         def weighted_group(k, engine):
             g, chunk = divmod(k, PACK)
-            half, lo = divmod(chunk * CHUNK, BANK)
+            half, lo = chunk // 2, (0, 1, 1, 0)[chunk] * CHUNK
             grouped = work.tile([P, STAGE], BF16, name=f"wp_{k}", tag="late", bufs=3, align_bytes=64)
             tiles["weighted", k] = grouped
             interleave(engine, grouped[:].rearrange("p (n t) -> p n t", t=PACK), tiles["planes", g, half][:, :, lo : lo + CHUNK])
 
+        def slot(k):
+            return 2 * CHUNK * (k - k % 4 + (0, 1, 3, 2)[k % 4]), k % 4 in (0, 3)
+
         def weighted_cols(k):
-            lo = (2 * k + 1 - k % 2) * CHUNK
+            lo, moves_first = slot(k)
+            lo = lo + CHUNK * moves_first
             return slice(lo, lo + CHUNK)
 
         def moves_cols(step):
-            k = (step - 1) % STEPS
-            lo = (2 * k + k % 2) * CHUNK
+            lo, moves_first = slot((step - 1) % STEPS)
+            lo = lo + CHUNK * (not moves_first)
             return slice(lo, lo + CHUNK)
 
-        extra = keep.tile([P, STAGE], BF16, name="extra", align_bytes=64)
-
         def weighted_stage(k):
-            lo = (1 + k % 2) * STAGE if k < 12 else 2 * STAGE
+            lo = (1 + 3 * (k % 2 if k < 12 else 1)) * STAGE
             return stage[:, lo : lo + STAGE]
 
         def moves_stage(step):
             if step == 0:
                 return weighted_stage(0)
-            if step == 13:
-                return extra[:]
-            lo = 3 * STAGE * ((step - 1) % 2)
+            lo = (0, 5, 2, 3)[(step - 1) % 4] * STAGE
             return stage[:, lo : lo + STAGE]
 
         def weighted_quantize(k):
@@ -307,8 +307,8 @@ def tile_cross_impact_hedge_s8_kernel(
             quantize(wm_codes[:, moves_cols(step)], wm_scales[:, moves_cols(step)], moves_stage(step))
 
         def both_quantize(k):
-            cols = slice(2 * k * CHUNK, 2 * (k + 1) * CHUNK)
-            lo = 2 * STAGE * (k % 2)
+            cols = slice(slot(k)[0], slot(k)[0] + 2 * CHUNK)
+            lo = (0, 4, 1, 3)[k % 4] * STAGE
             quantize(wm_codes[:, cols], wm_scales[:, cols], stage[:, lo : lo + 2 * STAGE])
 
         def moves_transpose(i, half, tag=None):
@@ -320,7 +320,7 @@ def tile_cross_impact_hedge_s8_kernel(
         def moves_scale(i, half):
             q, r = divmod(i, 2)
             nc.vector.tensor_tensor(
-                out=moves_stage(2 * q + half)[:, r * K_PASS : (r + 1) * K_PASS].rearrange("p (m t) -> p m t", t=PACK),
+                out=moves_stage(ORDER.index((q, half)))[:, r * K_PASS : (r + 1) * K_PASS].rearrange("p (m t) -> p m t", t=PACK),
                 in0=leave_bank(("turned_h", i, half))[:].rearrange("p t m -> p m t"),
                 in1=vol_bf[:, half, :].unsqueeze(1).to_broadcast([P, P, PACK]),
                 op=MULT,
@@ -335,14 +335,14 @@ def tile_cross_impact_hedge_s8_kernel(
 
         def moves_group(i, half):
             q, r = divmod(i, 2)
-            grouped = moves_stage(2 * q + half)[:, r * K_PASS : (r + 1) * K_PASS].rearrange("p (m t) -> p m t", t=PACK)
+            grouped = moves_stage(ORDER.index((q, half)))[:, r * K_PASS : (r + 1) * K_PASS].rearrange("p (m t) -> p m t", t=PACK)
             interleave(SCALAR, grouped, tiles.pop(("moves_planes", i, half))[:])
 
         def hedge_matmul(i, tag="hedge"):
             q, r = divmod(i, 2)
             bank = take_bank(("hedge", i), [P, R], f"hg_{i}", tag)
             for half in range(N_PASSES):
-                lo = moves_cols(2 * q + half).start + r * P
+                lo = moves_cols(ORDER.index((q, half))).start + r * P
                 rows = slice(lo, lo + P)
                 moving = (w_words[:, half, :], w_scales[:, half, :])
                 multiply(bank[:], (wm_codes[:, rows], wm_scales[:, rows]), moving, half == 0, half == N_PASSES - 1, FP4X4)
@@ -351,16 +351,18 @@ def tile_cross_impact_hedge_s8_kernel(
 
         def hedge_store(i, engine=SCALAR):
             g, j = divmod(i, PACK)
-            result = work.tile([P, R], F32, name=f"hr_{i}", tag="hedge_out", bufs=4, align_bytes=64)
+            result = work.tile([P, R], F32, name=f"hr_{i}", tag="hedge_out", bufs=6, align_bytes=64)
             move(engine, result[:], leave_bank(("hedge", i))[:])
             nc.sync.dma_start(out=hedge_view[g, j], in_=result[:])
 
-        sched_grouped = keep.tile([P, 3 * STAGE], BF16, name="sched_grouped", align_bytes=64)
 
         def sched_stage(b):
             if b == 0:
                 return weighted_stage(1)
-            return sched_grouped[:, STAGE * (b - 1) : STAGE * b]
+            if ("sched", b // 2) not in tiles:
+                grouped = work.tile([P, 2 * STAGE], BF16, name=f"sg_{b}", tag=f"grouped_{b // 2}", bufs=1, align_bytes=64)
+                tiles["sched", b // 2] = grouped
+            return tiles["sched", b // 2][:, STAGE * (b % 2) : STAGE * (b % 2 + 1)]
 
         def sched_transpose(b, tag=None):
             qt, two = divmod(b, 2)
@@ -377,7 +379,7 @@ def tile_cross_impact_hedge_s8_kernel(
 
         def sched_quantize(b, parts=1):
             cols = slice(b * 2 * P, (b + parts) * 2 * P)
-            grouped = sched_stage(b) if parts == 1 else sched_grouped[:, STAGE * (b - 1) : STAGE * (b - 1 + parts)]
+            grouped = sched_stage(b) if parts == 1 else tiles["sched", b // 2][:]
             quantize(sch_codes[:, cols], sch_scales[:, cols], grouped)
 
         def cost_matmul(qt, half, passes, tag=None):
@@ -386,7 +388,7 @@ def tile_cross_impact_hedge_s8_kernel(
             bank = tiles["cost", qt, half][0]
             for g in passes:
                 rows = slice((qt * T_PASSES + g) * P, (qt * T_PASSES + g + 1) * P)
-                lo = weighted_cols(PACK * g + 2 * half).start
+                lo = weighted_cols(PACK * g + 3 * half).start
                 moving = (wm_codes[:, lo : lo + BANK], wm_scales[:, lo : lo + BANK])
                 multiply(bank[:], (sch_codes[:, rows], sch_scales[:, rows]), moving, g == 0, g == T_PASSES - 1)
 
@@ -463,13 +465,24 @@ def tile_cross_impact_hedge_s8_kernel(
         sched_transpose(0, "hedge")
         for i in range(2):
             moves_transpose(i, 0)
-        for c in range(A_PASSES):
-            impact_quantize(c, 1)
-        for i in range(2):
-            impact_matmul(i, 1, f"z_{i}")
-            saturate(i, 1)
         flow_quantize(2)
         flow_quantize(3)
+        for c in range(A_PASSES):
+            impact_quantize(c, 1)
+        words = work.tile([P, 2, 2, P], F32, name="words_5", tag="grouped_2", bufs=1, align_bytes=64)
+        tiles["flow_words", 5] = words
+        for c in range(2):
+            nc.gpsimd.tensor_scalar(
+                out=words[:, c, :, :].rearrange("p u m -> p (u m)").bitcast(BF16).rearrange("p (u m e) -> p u m e", u=2, e=2),
+                in0=tiles["wide", 5][:, c * K_PASS : (c + 1) * K_PASS].rearrange("p (m u e) -> p u m e", u=2, e=2),
+                scalar1=1.0,
+                scalar2=0.0,
+                op0=MULT,
+                op1=ADD,
+            )
+        for i in (2, 3):
+            impact_matmul(i, 0, f"z_{i % 2}")
+            saturate(i, 0)
         widen(6)
         nc.scalar.copy(out=depth_f32[:], in_=depth_bf[:])
         nc.scalar.copy(out=vol_f32[:], in_=vol_bf[:])
@@ -477,9 +490,10 @@ def tile_cross_impact_hedge_s8_kernel(
 
         last = T_PASSES - 1
         for s in range(2, STEPS - 2):
+            pair, part = ORDER[s]
             q, half = divmod(s, 2)
             ahead = s + 2
-            moved_pair, moved_half = divmod(s - 2, 2)
+            moved_pair, moved_half = ORDER[s - 2]
             first, second = 2 * moved_pair, 2 * moved_pair + 1
             shared = s in SHARED_STEPS
             cut = P // 2 if s - half in SHARED_STEPS else 0
@@ -491,7 +505,7 @@ def tile_cross_impact_hedge_s8_kernel(
             flow_transpose(ahead, 0, 2)
             if half == 0:
                 last_transpose(q + 1)
-            if s == 4:
+            if s == 5:
                 sched_transpose(1, "hedge")
             if s == 13:
                 sched_transpose(2)
@@ -520,26 +534,30 @@ def tile_cross_impact_hedge_s8_kernel(
                 moves_quantize(0)
             flow_quantize(ahead)
 
-            if s == 4:
+            if s == 5:
                 sched_group(1)
             if s == 13:
                 sched_group(2)
-            impact_matmul(2 * q, half, "z_0")
-            saturate(2 * q, half)
-            if s >= 5:
+            impact_matmul(2 * pair, part, "z_0")
+            saturate(2 * pair, part)
+            if s == 6:
+                hedge_matmul(0, None)
+            if s >= 6:
                 hedge_matmul(s - 5)
             if shared:
                 moves_group(first, moved_half)
             elif half == 1 and s + 5 < TILES:
                 widen(s + 5)
-            impact_matmul(2 * q + 1, half, "z_1")
-            saturate(2 * q + 1, half)
-            if s >= 5:
+            impact_matmul(2 * pair + 1, part, "z_1")
+            saturate(2 * pair + 1, part)
+            if s == 6:
+                hedge_store(0)
+            if s >= 6:
                 hedge_store(s - 5)
             if half == 1 and s + 6 < TILES:
                 widen(s + 6)
-            if half == 0 and FIRST_SORTED <= s + 4 < TILES:
-                flow_sort(s + 4)
+            if s + 4 in SORTED:
+                flow_sort(s + 4, A_PASSES - half)
             if s == 2:
                 widen(7)
             if s == 11:

@@ -49,7 +49,7 @@ def tile_cross_impact_hedge_s8_kernel(
         psum = ctx.enter_context(tc.psum_pool(name="psum", bufs=1))
         ctx.enter_context(tc.manual_schedule())
 
-        w_scales = keep.tile([P, N_PASSES, R], U8, name="w_scales", align_bytes=64)
+        w_scales = keep.tile([P, N_PASSES, R], U8, name="w_scales", align_bytes=256)
         nc.vector.memset(w_scales[:].bitcast(I32), 0)
         ident = keep.tile([P, P], F32, name="ident")
         make_identity(nc, ident[:])
@@ -77,7 +77,7 @@ def tile_cross_impact_hedge_s8_kernel(
         vol_bf = keep.tile([P, N_PASSES, PACK], BF16, name="vol_bf", align_bytes=64)
         depth_bf = keep.tile([P, T_PASSES, PACK], BF16, name="depth_bf", align_bytes=64)
         depth_f32 = keep.tile([P, T_PASSES, PACK], F32, name="depth_f32", align_bytes=64)
-        w_words = keep.tile([P, N_PASSES, 2 * R], U8, name="w_words", align_bytes=64)
+        w_words = keep.tile([P, N_PASSES, 2 * R], U8, name="w_words", align_bytes=256)
         sched_sb = {}
 
         def load_sens():
@@ -93,12 +93,12 @@ def tile_cross_impact_hedge_s8_kernel(
             sched_sb[qt] = rows
             nc.sync.dma_start(out=rows[:], in_=sched[qt * P : (qt + 1) * P, :])
 
-        imp_codes = keep.tile([P, A_PASSES * N], U32, name="imp_codes", align_bytes=64)
-        imp_scales = keep.tile([P, A_PASSES * N], U8, name="imp_scales", align_bytes=64)
-        sch_codes = keep.tile([P, (Q // P) * T_PASSES * P], U32, name="sch_codes", align_bytes=64)
-        sch_scales = keep.tile([P, (Q // P) * T_PASSES * P], U8, name="sch_scales", align_bytes=64)
-        wm_codes = keep.tile([P, STEPS * 2 * CHUNK], U32, name="wm_codes", align_bytes=64)
-        wm_scales = keep.tile([P, STEPS * 2 * CHUNK], U8, name="wm_scales", align_bytes=64)
+        imp_codes = keep.tile([P, A_PASSES * N], U32, name="imp_codes", align_bytes=256)
+        imp_scales = keep.tile([P, A_PASSES * N], U8, name="imp_scales", align_bytes=256)
+        sch_codes = keep.tile([P, (Q // P) * T_PASSES * P], U32, name="sch_codes", align_bytes=256)
+        sch_scales = keep.tile([P, (Q // P) * T_PASSES * P], U8, name="sch_scales", align_bytes=256)
+        wm_codes = keep.tile([P, STEPS * 2 * CHUNK], U32, name="wm_codes", align_bytes=256)
+        wm_scales = keep.tile([P, STEPS * 2 * CHUNK], U8, name="wm_scales", align_bytes=256)
         stage = keep.tile([P, 6 * CHUNK * PACK], BF16, name="stage", align_bytes=64)
         tiles = {}
         free_banks = [f"turn_{b}" for b in range(TURN_BANKS)]
@@ -222,8 +222,8 @@ def tile_cross_impact_hedge_s8_kernel(
             )
 
         def flow_quantize(i):
-            codes = work.tile([P, A_PASSES * P], U32, name=f"fc_{i}", tag="flow_codes", bufs=5, align_bytes=64)
-            scales = work.tile([P, A_PASSES * P], U8, name=f"fs_{i}", tag="flow_scales", bufs=5, align_bytes=64)
+            codes = work.tile([P, A_PASSES * P], U32, name=f"fc_{i}", tag="flow_codes", bufs=5, align_bytes=256)
+            scales = work.tile([P, A_PASSES * P], U8, name=f"fs_{i}", tag="flow_scales", bufs=5, align_bytes=256)
             tiles["flow_codes", i] = (codes, scales)
             quantize(codes[:], scales[:], tiles.pop(("flow", i))[:])
 
@@ -351,7 +351,7 @@ def tile_cross_impact_hedge_s8_kernel(
 
         def hedge_store(i, engine=SCALAR):
             g, j = divmod(i, PACK)
-            result = work.tile([P, R], F32, name=f"hr_{i}", tag="hedge_out", bufs=6, align_bytes=64)
+            result = work.tile([P, R], F32, name=f"hr_{i}", tag="hedge_out", bufs=5, align_bytes=64)
             move(engine, result[:], leave_bank(("hedge", i))[:])
             nc.sync.dma_start(out=hedge_view[g, j], in_=result[:])
 

@@ -34,7 +34,7 @@ CHUNK = 256
 SCALAR, VECTOR, GPSIMD = "scalar", "vector", "gpsimd"
 
 SORTED = (6, 8, 10, 12, 14)
-SHARED_STEPS = (6, 8, 10, 12)
+SHARED_STEPS = (4, 6, 8, 10, 12)
 ORDER = [(0, 0), (1, 0), (0, 1), (1, 1)] + [divmod(s, 2) for s in range(4, STEPS)]
 TURN_BANKS = 5
 
@@ -557,7 +557,7 @@ def tile_cross_impact_hedge_s8_kernel(
             if half == 1 and s + 6 < TILES:
                 widen(s + 6)
             if s + 4 in SORTED:
-                flow_sort(s + 4, A_PASSES - half)
+                flow_sort(s + 4, A_PASSES - 1)
             if s == 2:
                 widen(7)
             if s == 11:
@@ -619,8 +619,10 @@ def tile_cross_impact_hedge_s8_kernel(
         weighted_group(15, VECTOR)
         weighted_quantize(14)
         weighted_quantize(15)
-        cost_matmul(0, 0, range(T_PASSES), "z_0")
-        cost_matmul(1, 0, range(T_PASSES), "z_1")
+        cost_matmul(0, 0, range(last), "z_0")
+        cost_matmul(1, 0, range(last), "z_1")
+        cost_matmul(0, 0, [last])
+        cost_matmul(1, 0, [last])
         hedge_matmul(14)
         hedge_matmul(15, None)
         cost_matmul(0, 1, range(T_PASSES))

@@ -33,9 +33,15 @@ BANK = 512
 CHUNK = 256
 SCALAR, VECTOR, GPSIMD = "scalar", "vector", "gpsimd"
 
-SORTED = (6, 8, 10, 12, 14)
-SHARED_STEPS = (4, 6, 8, 10, 12)
+SORTED = (6, 8, 10, 12, 14, 15)
+SHARED_STEPS = (4, 6, 8, 10)
 ORDER = [(0, 0), (1, 0), (0, 1), (1, 1)] + [divmod(s, 2) for s in range(4, STEPS)]
+SCH1 = 5
+HEAD1 = 0
+LASTS = {10: (14, 15)}
+FF = ()
+LATE = 0
+SMALL = 0
 TURN_BANKS = 5
 
 
@@ -159,7 +165,10 @@ def tile_cross_impact_hedge_s8_kernel(
             if ("wide", i) not in tiles:
                 wide = work.tile([P, A], BF16, name=f"wide_{i}", tag="wide", bufs=4, align_bytes=64)
                 tiles["wide", i] = wide
-            codes = flow_sb[i][:, lo:hi].bitcast(FP8)
+            if i == 0 and SMALL:
+                codes = (first_pass[:] if lo == 0 else rest[:, lo - K_PASS : hi - K_PASS]).bitcast(FP8)
+            else:
+                codes = flow_sb[i][:, lo:hi].bitcast(FP8)
             if table:
                 nc.scalar.activation(out=tiles["wide", i][:, lo:hi], in_=codes, func=COPY)
             else:
@@ -169,14 +178,15 @@ def tile_cross_impact_hedge_s8_kernel(
             nc.scalar.copy(out=out, in_=rows.bitcast(F32).rearrange("p (c m u) -> p c u m", m=P, u=2))
 
         def words_of(key, rows, c, u):
-            if key in tiles and c < tiles[key].shape[1]:
-                return tiles[key][:, c, u, :]
+            if key + (c,) in tiles:
+                return tiles[key + (c,)][:, u, :]
             return rows.bitcast(F32)[:, 2 * P * c + u : 2 * P * (c + 1) : 2]
 
-        def flow_sort(i, passes=A_PASSES):
-            words = work.tile([P, passes, 2, P], F32, name=f"words_{i}", tag="words", bufs=2, align_bytes=64)
-            tiles["flow_words", i] = words
-            sort_words(words[:], tiles["wide", i][:, : passes * K_PASS])
+        def flow_sort(i, lo, hi):
+            words = work.tile([P, hi - lo, 2, P], F32, name=f"words_{i}_{lo}", tag="words", bufs=4, align_bytes=64)
+            for c in range(lo, hi):
+                tiles["flow_words", i, c] = words[:, c - lo, :, :]
+            sort_words(words[:], tiles["wide", i][:, lo * K_PASS : hi * K_PASS])
 
         def flow_transpose(i, lo, hi, tag=None):
             bank = take_bank(("turned_flow", i, lo), [P, 2, hi - lo, P], f"xt_{i}_{lo}", tag)
@@ -403,7 +413,13 @@ def tile_cross_impact_hedge_s8_kernel(
                 nc.sync.dma_start(out=cost[qt * P : (qt + 1) * P, col : col + width], in_=result[:])
 
         nc.scalar.dma_start(out=scale_sb[:], in_=flow_scale.rearrange("o (c p t) -> p (o c) t", p=P, t=PACK))
-        load_flow(0, 1)
+        if SMALL:
+            first_pass = keep.tile([P, K_PASS], U8, name="flow_first", align_bytes=64)
+            nc.sync.dma_start(out=first_pass[:], in_=flow_view[0, :, 0, :K_PASS])
+            rest = keep.tile([P, A - K_PASS], U8, name="flow_rest", align_bytes=64)
+            nc.sync.dma_start(out=rest[:], in_=flow_view[0, :, 0, K_PASS:])
+        else:
+            load_flow(0, 1)
         load_flow(1, 1)
         load_impact(0, 0)
         load_impact(1, 0)
@@ -412,9 +428,9 @@ def tile_cross_impact_hedge_s8_kernel(
         load_flow(3, 1)
         for c in range(A_PASSES):
             load_impact(c, 1)
+        load_sched(0)
         load_flow(4, 2)
         nc.sync.dma_start(out=vol_bf[:], in_=vol.rearrange("(g p j) -> p g j", p=P, j=PACK))
-        load_sched(0)
         load_flow(6, 2)
         nc.sync.dma_start(out=depth_bf[:], in_=depth.rearrange("(g p j) -> p g j", p=P, j=PACK))
         load_sens()
@@ -442,27 +458,30 @@ def tile_cross_impact_hedge_s8_kernel(
         impact_group(2, 0, SCALAR, 0, CHUNK)
         impact_group(2, 0, VECTOR, CHUNK, BANK)
         widen(3)
-        for i in (2, 3):
-            flow_transpose(i, 0, 2)
-            flow_transpose(i, 2, 3)
-        impact_quantize(0, 0)
+        flow_transpose(2, 0, 2)
+        flow_transpose(2, 2, 3)
         flow_quantize(0)
-        impact_quantize(1, 0)
-        impact_quantize(2, 0)
+        for c in range(A_PASSES):
+            impact_quantize(c, 0)
         flow_quantize(1)
         impact_group(0, 1, SCALAR, slot=0)
         impact_group(1, 1, GPSIMD, slot=2)
         impact_group(2, 1, SCALAR, 0, CHUNK, slot=1)
+        impact_matmul(0, 0, "z_0")
+        flow_transpose(3, 0, 2)
+        flow_transpose(3, 2, 3)
+        impact_matmul(1, 0, "z_1")
         for i in range(2):
-            impact_matmul(i, 0, f"z_{i}")
             saturate(i, 0)
         impact_group(2, 1, SCALAR, CHUNK, BANK)
         for i in (2, 3):
             flow_scale_out(i, 0, 2)
             flow_scale_out(i, 2, 3)
         widen(4)
-        widen(5)
+        widen(5, SCALAR, 2 * K_PASS * LATE, A)
         sched_transpose(0, "hedge")
+        if HEAD1:
+            sched_transpose(1)
         for i in range(2):
             moves_transpose(i, 0)
         flow_quantize(2)
@@ -470,8 +489,8 @@ def tile_cross_impact_hedge_s8_kernel(
         for c in range(A_PASSES):
             impact_quantize(c, 1)
         words = work.tile([P, 2, 2, P], F32, name="words_5", tag="grouped_2", bufs=1, align_bytes=64)
-        tiles["flow_words", 5] = words
         for c in range(2):
+            tiles["flow_words", 5, c] = words[:, c, :, :]
             nc.gpsimd.tensor_scalar(
                 out=words[:, c, :, :].rearrange("p u m -> p (u m)").bitcast(BF16).rearrange("p (u m e) -> p u m e", u=2, e=2),
                 in0=tiles["wide", 5][:, c * K_PASS : (c + 1) * K_PASS].rearrange("p (m u e) -> p u m e", u=2, e=2),
@@ -483,6 +502,8 @@ def tile_cross_impact_hedge_s8_kernel(
         for i in (2, 3):
             impact_matmul(i, 0, f"z_{i % 2}")
             saturate(i, 0)
+        if LATE:
+            widen(5, SCALAR, 0, 2 * K_PASS)
         widen(6)
         nc.scalar.copy(out=depth_f32[:], in_=depth_bf[:])
         nc.scalar.copy(out=vol_f32[:], in_=vol_bf[:])
@@ -505,7 +526,7 @@ def tile_cross_impact_hedge_s8_kernel(
             flow_transpose(ahead, 0, 2)
             if half == 0:
                 last_transpose(q + 1)
-            if s == 5:
+            if s == SCH1 and not HEAD1:
                 sched_transpose(1, "hedge")
             if s == 13:
                 sched_transpose(2)
@@ -516,10 +537,13 @@ def tile_cross_impact_hedge_s8_kernel(
 
             if shared:
                 moves_planes(first, moved_half)
+            if s in FF:
+                flow_scale_out(ahead, 0, 2)
             moves_scale(second, moved_half)
             if not shared:
                 moves_scale(first, moved_half)
-            flow_scale_out(ahead, 0, 2)
+            if s not in FF:
+                flow_scale_out(ahead, 0, 2)
             if half == 0:
                 last_scale_out(ahead)
                 if cut:
@@ -534,7 +558,7 @@ def tile_cross_impact_hedge_s8_kernel(
                 moves_quantize(0)
             flow_quantize(ahead)
 
-            if s == 5:
+            if s == SCH1:
                 sched_group(1)
             if s == 13:
                 sched_group(2)
@@ -554,15 +578,22 @@ def tile_cross_impact_hedge_s8_kernel(
                 hedge_store(0)
             if s >= 6:
                 hedge_store(s - 5)
-            if half == 1 and s + 6 < TILES:
+            if half == 1 and s + 6 < TILES and not LATE:
                 widen(s + 6)
+            if LATE and half == 0 and s + 5 < TILES:
+                widen(s + 5, SCALAR, 2 * K_PASS, A)
+            if LATE and half == 1 and s + 4 < TILES:
+                widen(s + 4, SCALAR, 0, 2 * K_PASS)
             if s + 4 in SORTED:
-                flow_sort(s + 4, A_PASSES - 1)
-            if s == 2:
+                flow_sort(s + 4, 0, 2)
+            for i in LASTS.get(s, ()):
+                flow_sort(i, 2, 3)
+            if s == 2 and not LATE:
                 widen(7)
             if s == 11:
                 words = work.tile([P, T_PASSES, 2, P], F32, name="sched_words", tag="raw", bufs=6, align_bytes=64)
-                tiles["sched_words", 1] = words
+                for c in range(T_PASSES):
+                    tiles["sched_words", 1, c] = words[:, c, :, :]
                 sort_words(words[:], sched_sb[1][:])
             if 2 * q >= PACK * last:
                 for j in range(2):

@@ -33,15 +33,8 @@ BANK = 512
 CHUNK = 256
 SCALAR, VECTOR, GPSIMD = "scalar", "vector", "gpsimd"
 
-SORTED = (6, 8, 10, 12, 14, 15)
 SHARED_STEPS = (4, 6, 8, 10)
 ORDER = [(0, 0), (1, 0), (0, 1), (1, 1)] + [divmod(s, 2) for s in range(4, STEPS)]
-SCH1 = 5
-HEAD1 = 0
-LASTS = {10: (14, 15)}
-FF = ()
-LATE = 0
-SMALL = 0
 TURN_BANKS = 5
 
 
@@ -165,10 +158,7 @@ def tile_cross_impact_hedge_s8_kernel(
             if ("wide", i) not in tiles:
                 wide = work.tile([P, A], BF16, name=f"wide_{i}", tag="wide", bufs=4, align_bytes=64)
                 tiles["wide", i] = wide
-            if i == 0 and SMALL:
-                codes = (first_pass[:] if lo == 0 else rest[:, lo - K_PASS : hi - K_PASS]).bitcast(FP8)
-            else:
-                codes = flow_sb[i][:, lo:hi].bitcast(FP8)
+            codes = flow_sb[i][:, lo:hi].bitcast(FP8)
             if table:
                 nc.scalar.activation(out=tiles["wide", i][:, lo:hi], in_=codes, func=COPY)
             else:
@@ -183,7 +173,7 @@ def tile_cross_impact_hedge_s8_kernel(
             return rows.bitcast(F32)[:, 2 * P * c + u : 2 * P * (c + 1) : 2]
 
         def flow_sort(i, lo, hi):
-            words = work.tile([P, hi - lo, 2, P], F32, name=f"words_{i}_{lo}", tag="words", bufs=4, align_bytes=64)
+            words = work.tile([P, hi - lo, 2, P], F32, name=f"words_{i}_{lo}", tag="words", bufs=3, align_bytes=64)
             for c in range(lo, hi):
                 tiles["flow_words", i, c] = words[:, c - lo, :, :]
             sort_words(words[:], tiles["wide", i][:, lo * K_PASS : hi * K_PASS])
@@ -413,13 +403,7 @@ def tile_cross_impact_hedge_s8_kernel(
                 nc.sync.dma_start(out=cost[qt * P : (qt + 1) * P, col : col + width], in_=result[:])
 
         nc.scalar.dma_start(out=scale_sb[:], in_=flow_scale.rearrange("o (c p t) -> p (o c) t", p=P, t=PACK))
-        if SMALL:
-            first_pass = keep.tile([P, K_PASS], U8, name="flow_first", align_bytes=64)
-            nc.sync.dma_start(out=first_pass[:], in_=flow_view[0, :, 0, :K_PASS])
-            rest = keep.tile([P, A - K_PASS], U8, name="flow_rest", align_bytes=64)
-            nc.sync.dma_start(out=rest[:], in_=flow_view[0, :, 0, K_PASS:])
-        else:
-            load_flow(0, 1)
+        load_flow(0, 1)
         load_flow(1, 1)
         load_impact(0, 0)
         load_impact(1, 0)
@@ -478,10 +462,9 @@ def tile_cross_impact_hedge_s8_kernel(
             flow_scale_out(i, 0, 2)
             flow_scale_out(i, 2, 3)
         widen(4)
-        widen(5, SCALAR, 2 * K_PASS * LATE, A)
+        widen(5)
         sched_transpose(0, "hedge")
-        if HEAD1:
-            sched_transpose(1)
+        sched_transpose(1)
         for i in range(2):
             moves_transpose(i, 0)
         flow_quantize(2)
@@ -502,8 +485,6 @@ def tile_cross_impact_hedge_s8_kernel(
         for i in (2, 3):
             impact_matmul(i, 0, f"z_{i % 2}")
             saturate(i, 0)
-        if LATE:
-            widen(5, SCALAR, 0, 2 * K_PASS)
         widen(6)
         nc.scalar.copy(out=depth_f32[:], in_=depth_bf[:])
         nc.scalar.copy(out=vol_f32[:], in_=vol_bf[:])
@@ -526,8 +507,6 @@ def tile_cross_impact_hedge_s8_kernel(
             flow_transpose(ahead, 0, 2)
             if half == 0:
                 last_transpose(q + 1)
-            if s == SCH1 and not HEAD1:
-                sched_transpose(1, "hedge")
             if s == 13:
                 sched_transpose(2)
             if s > 2:
@@ -537,13 +516,10 @@ def tile_cross_impact_hedge_s8_kernel(
 
             if shared:
                 moves_planes(first, moved_half)
-            if s in FF:
-                flow_scale_out(ahead, 0, 2)
             moves_scale(second, moved_half)
             if not shared:
                 moves_scale(first, moved_half)
-            if s not in FF:
-                flow_scale_out(ahead, 0, 2)
+            flow_scale_out(ahead, 0, 2)
             if half == 0:
                 last_scale_out(ahead)
                 if cut:
@@ -558,8 +534,8 @@ def tile_cross_impact_hedge_s8_kernel(
                 moves_quantize(0)
             flow_quantize(ahead)
 
-            if s == SCH1:
-                sched_group(1)
+            if s == 2:
+                sched_group(1, VECTOR)
             if s == 13:
                 sched_group(2)
             impact_matmul(2 * pair, part, "z_0")
@@ -568,27 +544,27 @@ def tile_cross_impact_hedge_s8_kernel(
                 hedge_matmul(0, None)
             if s >= 6:
                 hedge_matmul(s - 5)
-            if shared:
-                moves_group(first, moved_half)
-            elif half == 1 and s + 5 < TILES:
-                widen(s + 5)
-            impact_matmul(2 * pair + 1, part, "z_1")
-            saturate(2 * pair + 1, part)
             if s == 6:
                 hedge_store(0)
             if s >= 6:
                 hedge_store(s - 5)
-            if half == 1 and s + 6 < TILES and not LATE:
+            impact_matmul(2 * pair + 1, part, "z_1")
+            if half == 1 and s + 5 < TILES and s < 6:
+                widen(s + 5)
+            saturate(2 * pair + 1, part)
+            if half == 1 and s + 5 < TILES and s >= 6:
+                widen(s + 5)
+            if half == 0 and s + 4 < TILES:
+                flow_sort(s + 4, 0, 2 if s == 2 else A_PASSES)
+            if shared:
+                moves_group(first, moved_half)
+            if half == 1 and s + 6 < TILES:
                 widen(s + 6)
-            if LATE and half == 0 and s + 5 < TILES:
-                widen(s + 5, SCALAR, 2 * K_PASS, A)
-            if LATE and half == 1 and s + 4 < TILES:
-                widen(s + 4, SCALAR, 0, 2 * K_PASS)
-            if s + 4 in SORTED:
+            if s in (5, 11):
                 flow_sort(s + 4, 0, 2)
-            for i in LASTS.get(s, ()):
-                flow_sort(i, 2, 3)
-            if s == 2 and not LATE:
+            if s == 10:
+                flow_sort(15, 2, 3)
+            if s == 2:
                 widen(7)
             if s == 11:
                 words = work.tile([P, T_PASSES, 2, P], F32, name="sched_words", tag="raw", bufs=6, align_bytes=64)
@@ -601,47 +577,49 @@ def tile_cross_impact_hedge_s8_kernel(
 
         final = (TILES - 2, TILES - 1)
         weigh_chunk(11)
-        sched_transpose(3)
+        impact_matmul(14, 0, "z_0")
         for half in range(N_PASSES):
             for i in (12, 13):
                 moves_transpose(i, half)
-        sched_group(3)
         for half in range(N_PASSES):
             for i in (12, 13):
                 moves_scale(i, half)
-        hedge_matmul(9)
-        impact_matmul(14, 0, "z_0")
         impact_matmul(14, 1, "z_1")
         impact_matmul(15, 0, None)
         impact_matmul(15, 1, None)
-        hedge_store(9)
+        hedge_matmul(9)
         saturate(14, 0)
         saturate(14, 1)
         weigh_plane(last, 0, 2, CHUNK)
         saturate(15, 0)
         saturate(15, 1)
-        weigh_plane(last, 0, 3, CHUNK)
-        weigh_plane(last, 1, 2)
-        weigh_plane(last, 1, 3)
         both_quantize(10)
         moves_quantize(13)
-        sched_quantize(2, 2)
+        sched_quantize(2)
         both_quantize(11)
         weigh_chunk(12)
         sched_quantize(1)
+        sched_transpose(3)
         moves_transpose(14, 0, "z_0")
         moves_transpose(14, 1, "z_1")
         moves_transpose(15, 0)
         moves_transpose(15, 1)
-        hedge_matmul(10)
-        for i in (11, 12, 13):
-            hedge_matmul(i, None)
+        hedge_store(9)
+        weigh_plane(last, 0, 3, CHUNK)
+        sched_group(3)
         for i in final:
             for half in range(N_PASSES):
                 moves_scale(i, half)
+        hedge_matmul(10, None)
+        hedge_matmul(11, None)
+        hedge_matmul(12)
+        hedge_matmul(13, None)
         weighted_group(13, SCALAR)
+        weigh_plane(last, 1, 2)
+        weigh_plane(last, 1, 3)
         for i in (10, 11, 12, 13):
             hedge_store(i)
+        sched_quantize(3)
         moves_quantize(14)
         weighted_quantize(12)
         weighted_quantize(13)
@@ -654,8 +632,8 @@ def tile_cross_impact_hedge_s8_kernel(
         cost_matmul(1, 0, range(last), "z_1")
         cost_matmul(0, 0, [last])
         cost_matmul(1, 0, [last])
-        hedge_matmul(14)
-        hedge_matmul(15, None)
+        hedge_matmul(14, None)
+        hedge_matmul(15)
         cost_matmul(0, 1, range(T_PASSES))
         cost_matmul(1, 1, range(T_PASSES))
         cost_store(0, 0, SCALAR)

@@ -450,23 +450,22 @@ def tile_cross_impact_hedge_s8_kernel(
         flow_quantize(1)
         impact_group(0, 1, SCALAR, slot=0)
         impact_group(1, 1, GPSIMD, slot=2)
-        impact_group(2, 1, SCALAR, 0, CHUNK, slot=1)
         impact_matmul(0, 0, "z_0")
+        saturate(0, 0)
+        impact_group(2, 1, SCALAR, 0, CHUNK, slot=1)
         flow_transpose(3, 0, 2)
         flow_transpose(3, 2, 3)
+        sched_transpose(0, "hedge")
         impact_matmul(1, 0, "z_1")
-        for i in range(2):
-            saturate(i, 0)
+        sched_transpose(1)
         impact_group(2, 1, SCALAR, CHUNK, BANK)
+        saturate(1, 0)
         for i in (2, 3):
             flow_scale_out(i, 0, 2)
             flow_scale_out(i, 2, 3)
         widen(4)
         widen(5)
-        sched_transpose(0, "hedge")
-        sched_transpose(1)
-        for i in range(2):
-            moves_transpose(i, 0)
+        moves_transpose(0, 0)
         flow_quantize(2)
         flow_quantize(3)
         for c in range(A_PASSES):
@@ -504,6 +503,8 @@ def tile_cross_impact_hedge_s8_kernel(
                 weigh_chunk(s - 3)
             if shared:
                 moves_transpose(first, moved_half)
+            if s == 2:
+                moves_transpose(second, moved_half)
             flow_transpose(ahead, 0, 2)
             if half == 0:
                 last_transpose(q + 1)
@@ -512,12 +513,14 @@ def tile_cross_impact_hedge_s8_kernel(
             if s > 2:
                 if not shared:
                     moves_transpose(first, moved_half)
-                moves_transpose(second, moved_half)
+                moves_transpose(second, moved_half, "hedge" if s == 6 else None)
 
             if shared:
                 moves_planes(first, moved_half)
+            if s == 2:
+                moves_scale(first, moved_half)
             moves_scale(second, moved_half)
-            if not shared:
+            if not shared and s > 2:
                 moves_scale(first, moved_half)
             flow_scale_out(ahead, 0, 2)
             if half == 0:
@@ -542,16 +545,18 @@ def tile_cross_impact_hedge_s8_kernel(
             saturate(2 * pair, part)
             if s == 6:
                 hedge_matmul(0, None)
-            if s >= 6:
+            if s > 6:
                 hedge_matmul(s - 5)
-            if s == 6:
-                hedge_store(0)
             if s >= 6:
-                hedge_store(s - 5)
+                hedge_store(s - 5 if s > 6 else 0)
             impact_matmul(2 * pair + 1, part, "z_1")
+            if s == 6:
+                hedge_matmul(1)
             if half == 1 and s + 5 < TILES and s < 6:
                 widen(s + 5)
             saturate(2 * pair + 1, part)
+            if s == 6:
+                hedge_store(1)
             if half == 1 and s + 5 < TILES and s >= 6:
                 widen(s + 5)
             if half == 0 and s + 4 < TILES:

@@ -410,9 +410,10 @@ def tile_cross_impact_hedge_s8_kernel(
         load_flow(2, 1)
         load_impact(2, 0)
         load_flow(3, 1)
-        for c in range(A_PASSES):
-            load_impact(c, 1)
+        load_impact(0, 1)
+        load_impact(1, 1)
         load_sched(0)
+        load_impact(2, 1)
         load_flow(4, 2)
         nc.sync.dma_start(out=vol_bf[:], in_=vol.rearrange("(g p j) -> p g j", p=P, j=PACK))
         load_flow(6, 2)
@@ -560,7 +561,7 @@ def tile_cross_impact_hedge_s8_kernel(
             if half == 1 and s + 5 < TILES and s >= 6:
                 widen(s + 5)
             if half == 0 and s + 4 < TILES:
-                flow_sort(s + 4, 0, 2 if s == 2 else A_PASSES)
+                flow_sort(s + 4, 0, A_PASSES if s >= 10 else 2)
             if shared:
                 moves_group(first, moved_half)
             if half == 1 and s + 6 < TILES:

@@ -518,12 +518,15 @@ def tile_cross_impact_hedge_s8_kernel(
 
             if shared:
                 moves_planes(first, moved_half)
+            if s == 3:
+                flow_scale_out(ahead, 0, 2)
             if s == 2:
                 moves_scale(first, moved_half)
             moves_scale(second, moved_half)
             if not shared and s > 2:
                 moves_scale(first, moved_half)
-            flow_scale_out(ahead, 0, 2)
+            if s != 3:
+                flow_scale_out(ahead, 0, 2)
             if half == 0:
                 last_scale_out(ahead)
                 if cut:

@@ -1,3 +1,4 @@
+import math
 from contextlib import ExitStack
 
 import concourse.mybir as mybir
@@ -31,6 +32,9 @@ PAIRS = TILES // 2
 STEPS = PAIRS * N_PASSES
 BANK = 512
 CHUNK = 256
+SIZES = {F32: 4, U32: 4, BF16: 2, U8: 1}
+LINE_ROUND = 256
+SKEW = {"ident": 128, "imp_scales": 128, "wm_scales": 128, "w_words": 64, "w_scales": 192, "flow_codes": 64, "flow_scales": 192, "sch_codes": 64, "sch_scales": 192}
 SCALAR, VECTOR, GPSIMD = "scalar", "vector", "gpsimd"
 
 SHARED_STEPS = (4, 6, 8, 10)
@@ -43,14 +47,23 @@ def tile_cross_impact_hedge_s8_kernel(
 ):
     nc = tc.nc
     with ExitStack() as ctx:
-        keep = ctx.enter_context(tc.tile_pool(name="keep", bufs=1))
-        work = ctx.enter_context(tc.tile_pool(name="work", bufs=3))
+        sbuf = ctx.enter_context(tc.tile_pool(name="sbuf", bufs=1))
         psum = ctx.enter_context(tc.psum_pool(name="psum", bufs=1))
         ctx.enter_context(tc.manual_schedule())
 
-        w_scales = keep.tile([P, N_PASSES, R], U8, name="w_scales", align_bytes=256)
+        places = {"end": 0}
+
+        def tile(shape, dtype, name, tag=None, bufs=1, room=None):
+            tag = tag or name
+            if tag not in places:
+                size = room or math.prod(shape[1:]) * SIZES[dtype]
+                places[tag] = -(-places["end"] // LINE_ROUND) * LINE_ROUND + SKEW.get(tag, 0)
+                places["end"] = places[tag] + bufs * size
+            return sbuf.tile(shape, dtype, name=name, tag=tag, bufs=bufs, align_bytes=64, offset=places[tag])
+
+        w_scales = tile([P, N_PASSES, R], U8, name="w_scales")
         nc.vector.memset(w_scales[:].bitcast(I32), 0)
-        ident = keep.tile([P, P], F32, name="ident")
+        ident = tile([P, P], F32, name="ident")
         make_identity(nc, ident[:])
 
         flow_view = flow_bytes.rearrange("(g p j) a -> g p j a", p=P, j=PACK)
@@ -58,7 +71,7 @@ def tile_cross_impact_hedge_s8_kernel(
 
         def load_flow(first, count):
             g, j = divmod(first, PACK)
-            rows = keep.tile([P, count, A], U8, name=f"flow_{first}", align_bytes=64)
+            rows = tile([P, count, A], U8, name=f"flow_{first}")
             for r in range(count):
                 flow_sb[first + r] = rows[:, r, :]
             nc.sync.dma_start(out=rows[:], in_=flow_view[g, :, j : j + count, :])
@@ -67,16 +80,16 @@ def tile_cross_impact_hedge_s8_kernel(
         imp_raw = {}
 
         def load_impact(c, half):
-            rows = work.tile([P, PACK, BANK], BF16, name=f"imp_raw_{c}_{half}", tag="raw", bufs=6, align_bytes=64)
+            rows = tile([P, PACK, BANK], BF16, name=f"imp_raw_{c}_{half}", tag="raw", bufs=6)
             imp_raw[c, half] = rows
             nc.sync.dma_start(out=rows[:], in_=imp_view[c, :, :, half * BANK : (half + 1) * BANK])
 
-        scale_sb = keep.tile([P, A_PASSES, PACK], F32, name="scale_sb", align_bytes=64)
-        vol_f32 = keep.tile([P, N_PASSES, PACK], F32, name="vol_f32", align_bytes=64)
-        vol_bf = keep.tile([P, N_PASSES, PACK], BF16, name="vol_bf", align_bytes=64)
-        depth_bf = keep.tile([P, T_PASSES, PACK], BF16, name="depth_bf", align_bytes=64)
-        depth_f32 = keep.tile([P, T_PASSES, PACK], F32, name="depth_f32", align_bytes=64)
-        w_words = keep.tile([P, N_PASSES, 2 * R], U8, name="w_words", align_bytes=256)
+        scale_sb = tile([P, A_PASSES, PACK], F32, name="scale_sb")
+        vol_f32 = tile([P, N_PASSES, PACK], F32, name="vol_f32")
+        vol_bf = tile([P, N_PASSES, PACK], BF16, name="vol_bf")
+        depth_bf = tile([P, T_PASSES, PACK], BF16, name="depth_bf")
+        depth_f32 = tile([P, T_PASSES, PACK], F32, name="depth_f32")
+        w_words = tile([P, N_PASSES, 2 * R], U8, name="w_words")
         sched_sb = {}
 
         def load_sens():
@@ -88,17 +101,17 @@ def tile_cross_impact_hedge_s8_kernel(
             nc.sync.dma_start(out=w_words[:].bitcast(I32), in_=sens_words.rearrange("g p b -> p g b").bitcast(I32))
 
         def load_sched(qt):
-            rows = keep.tile([P, T], BF16, name=f"sched_{qt}", align_bytes=64)
+            rows = tile([P, T], BF16, name=f"sched_{qt}")
             sched_sb[qt] = rows
             nc.sync.dma_start(out=rows[:], in_=sched[qt * P : (qt + 1) * P, :])
 
-        imp_codes = keep.tile([P, A_PASSES * N], U32, name="imp_codes", align_bytes=256)
-        imp_scales = keep.tile([P, A_PASSES * N], U8, name="imp_scales", align_bytes=256)
-        sch_codes = keep.tile([P, (Q // P) * T_PASSES * P], U32, name="sch_codes", align_bytes=256)
-        sch_scales = keep.tile([P, (Q // P) * T_PASSES * P], U8, name="sch_scales", align_bytes=256)
-        wm_codes = keep.tile([P, STEPS * 2 * CHUNK], U32, name="wm_codes", align_bytes=256)
-        wm_scales = keep.tile([P, STEPS * 2 * CHUNK], U8, name="wm_scales", align_bytes=256)
-        stage = keep.tile([P, 6 * CHUNK * PACK], BF16, name="stage", align_bytes=64)
+        imp_codes = tile([P, A_PASSES * N], U32, name="imp_codes")
+        imp_scales = tile([P, A_PASSES * N], U8, name="imp_scales")
+        sch_codes = tile([P, (Q // P) * T_PASSES * P], U32, name="sch_codes")
+        sch_scales = tile([P, (Q // P) * T_PASSES * P], U8, name="sch_scales")
+        wm_codes = tile([P, STEPS * 2 * CHUNK], U32, name="wm_codes")
+        wm_scales = tile([P, STEPS * 2 * CHUNK], U8, name="wm_scales")
+        stage = tile([P, 6 * CHUNK * PACK], BF16, name="stage")
         tiles = {}
         free_banks = [f"turn_{b}" for b in range(TURN_BANKS)]
 
@@ -145,7 +158,7 @@ def tile_cross_impact_hedge_s8_kernel(
         def impact_group(c, half, engine, lo=0, hi=BANK, slot=None):
             if ("impact", c, half) not in tiles:
                 tag = f"grouped_{c if slot is None else slot}"
-                grouped = work.tile([P, BANK * PACK], BF16, name=f"ig_{c}_{half}", tag=tag, bufs=1, align_bytes=64)
+                grouped = tile([P, BANK * PACK], BF16, name=f"ig_{c}_{half}", tag=tag, bufs=1)
                 tiles["impact", c, half] = grouped
             grouped = tiles["impact", c, half][:, lo * PACK : hi * PACK].rearrange("p (n t) -> p n t", t=PACK)
             interleave(engine, grouped, imp_raw[c, half][:, :, lo:hi])
@@ -156,7 +169,7 @@ def tile_cross_impact_hedge_s8_kernel(
 
         def widen(i, engine=SCALAR, lo=0, hi=A, table=False):
             if ("wide", i) not in tiles:
-                wide = work.tile([P, A], BF16, name=f"wide_{i}", tag="wide", bufs=4, align_bytes=64)
+                wide = tile([P, A], BF16, name=f"wide_{i}", tag="wide", bufs=4)
                 tiles["wide", i] = wide
             codes = flow_sb[i][:, lo:hi].bitcast(FP8)
             if table:
@@ -173,7 +186,7 @@ def tile_cross_impact_hedge_s8_kernel(
             return rows.bitcast(F32)[:, 2 * P * c + u : 2 * P * (c + 1) : 2]
 
         def flow_sort(i, lo, hi):
-            words = work.tile([P, hi - lo, 2, P], F32, name=f"words_{i}_{lo}", tag="words", bufs=3, align_bytes=64)
+            words = tile([P, hi - lo, 2, P], F32, name=f"words_{i}_{lo}", tag="words", bufs=3, room=A * 2)
             for c in range(lo, hi):
                 tiles["flow_words", i, c] = words[:, c - lo, :, :]
             sort_words(words[:], tiles["wide", i][:, lo * K_PASS : hi * K_PASS])
@@ -186,7 +199,7 @@ def tile_cross_impact_hedge_s8_kernel(
 
         def flow_scale_out(i, lo, hi):
             if ("flow", i) not in tiles:
-                grouped = work.tile([P, A], BF16, name=f"fg_{i}", tag="flow", bufs=3, align_bytes=64)
+                grouped = tile([P, A], BF16, name=f"fg_{i}", tag="flow", bufs=3)
                 tiles["flow", i] = grouped
             n = hi - lo
             values = leave_bank(("turned_flow", i, lo))[:].rearrange("p u c m -> p (u c m)").bitcast(BF16)
@@ -208,7 +221,7 @@ def tile_cross_impact_hedge_s8_kernel(
         def last_scale_out(i, lo=0, hi=P):
             q, r = divmod(i, 2)
             if ("flow", i) not in tiles:
-                grouped = work.tile([P, A], BF16, name=f"fg_{i}", tag="flow", bufs=3, align_bytes=64)
+                grouped = tile([P, A], BF16, name=f"fg_{i}", tag="flow", bufs=3)
                 tiles["flow", i] = grouped
             bank = leave_bank(("turned_last", q)) if (r, hi) == (1, P) else tiles["turned_last", q][0]
             values = bank[:].rearrange("p u r m -> p (u r m)").bitcast(BF16).rearrange("p (u m e) -> p m u e", u=2, e=2)
@@ -222,8 +235,8 @@ def tile_cross_impact_hedge_s8_kernel(
             )
 
         def flow_quantize(i):
-            codes = work.tile([P, A_PASSES * P], U32, name=f"fc_{i}", tag="flow_codes", bufs=5, align_bytes=256)
-            scales = work.tile([P, A_PASSES * P], U8, name=f"fs_{i}", tag="flow_scales", bufs=5, align_bytes=256)
+            codes = tile([P, A_PASSES * P], U32, name=f"fc_{i}", tag="flow_codes", bufs=5)
+            scales = tile([P, A_PASSES * P], U8, name=f"fs_{i}", tag="flow_scales", bufs=5)
             tiles["flow_codes", i] = (codes, scales)
             quantize(codes[:], scales[:], tiles.pop(("flow", i))[:])
 
@@ -239,7 +252,7 @@ def tile_cross_impact_hedge_s8_kernel(
         def saturate(i, half):
             g, j = divmod(i, PACK)
             if j == 0:
-                h = work.tile([P, PACK, BANK], F32, name=f"h_{g}_{half}", tag="h", bufs=4, align_bytes=64)
+                h = tile([P, PACK, BANK], F32, name=f"h_{g}_{half}", tag="h", bufs=4)
                 tiles["h", g, half] = h
             nc.scalar.activation(
                 out=tiles["h", g, half][:, j, :].rearrange("p (t m) -> p t m", t=PACK),
@@ -261,7 +274,7 @@ def tile_cross_impact_hedge_s8_kernel(
 
         def weigh_plane(g, half, j, lo=0, hi=BANK, engine=SCALAR):
             if ("planes", g, half) not in tiles:
-                planes = work.tile([P, PACK, BANK], BF16, name=f"planes_{g}_{half}", tag="raw", bufs=6, align_bytes=64)
+                planes = tile([P, PACK, BANK], BF16, name=f"planes_{g}_{half}", tag="raw", bufs=6)
                 tiles["planes", g, half] = planes
             out, in_ = tiles["planes", g, half][:, j, lo:hi], tiles["h", g, half][:, j, lo:hi]
             if engine == SCALAR:
@@ -272,7 +285,7 @@ def tile_cross_impact_hedge_s8_kernel(
         def weighted_group(k, engine):
             g, chunk = divmod(k, PACK)
             half, lo = chunk // 2, (0, 1, 1, 0)[chunk] * CHUNK
-            grouped = work.tile([P, STAGE], BF16, name=f"wp_{k}", tag="late", bufs=3, align_bytes=64)
+            grouped = tile([P, STAGE], BF16, name=f"wp_{k}", tag="late", bufs=3)
             tiles["weighted", k] = grouped
             interleave(engine, grouped[:].rearrange("p (n t) -> p n t", t=PACK), tiles["planes", g, half][:, :, lo : lo + CHUNK])
 
@@ -327,7 +340,7 @@ def tile_cross_impact_hedge_s8_kernel(
             )
 
         def moves_planes(i, half):
-            planes = work.tile([P, PACK, P], BF16, name=f"mp_{i}_{half}", tag="moves_planes", bufs=2, align_bytes=64)
+            planes = tile([P, PACK, P], BF16, name=f"mp_{i}_{half}", tag="moves_planes", bufs=2)
             tiles["moves_planes", i, half] = planes
             bank = leave_bank(("turned_h", i, half))
             for t in range(PACK):
@@ -351,7 +364,7 @@ def tile_cross_impact_hedge_s8_kernel(
 
         def hedge_store(i, engine=SCALAR):
             g, j = divmod(i, PACK)
-            result = work.tile([P, R], F32, name=f"hr_{i}", tag="hedge_out", bufs=5, align_bytes=64)
+            result = tile([P, R], F32, name=f"hr_{i}", tag="hedge_out", bufs=5)
             move(engine, result[:], leave_bank(("hedge", i))[:])
             nc.sync.dma_start(out=hedge_view[g, j], in_=result[:])
 
@@ -360,7 +373,7 @@ def tile_cross_impact_hedge_s8_kernel(
             if b == 0:
                 return weighted_stage(1)
             if ("sched", b // 2) not in tiles:
-                grouped = work.tile([P, 2 * STAGE], BF16, name=f"sg_{b}", tag=f"grouped_{b // 2}", bufs=1, align_bytes=64)
+                grouped = tile([P, 2 * STAGE], BF16, name=f"sg_{b}", tag=f"grouped_{b // 2}", bufs=1)
                 tiles["sched", b // 2] = grouped
             return tiles["sched", b // 2][:, STAGE * (b % 2) : STAGE * (b % 2 + 1)]
 
@@ -396,7 +409,7 @@ def tile_cross_impact_hedge_s8_kernel(
             bank = leave_bank(("cost", qt, half))
             width = BANK // pieces
             for lo in range(0, BANK, width):
-                result = work.tile([P, width], F32, name=f"cr_{qt}_{half}_{lo}", tag="raw", bufs=6, align_bytes=64)
+                result = tile([P, width], F32, name=f"cr_{qt}_{half}_{lo}", tag="raw", bufs=6)
                 sums = bank[:].rearrange("p (t m) -> p m t", t=PACK)[:, lo // PACK : (lo + width) // PACK, :]
                 move(engine, result[:].rearrange("p (m t) -> p m t", t=PACK), sums)
                 col = half * BANK + lo
@@ -471,7 +484,7 @@ def tile_cross_impact_hedge_s8_kernel(
         flow_quantize(3)
         for c in range(A_PASSES):
             impact_quantize(c, 1)
-        words = work.tile([P, 2, 2, P], F32, name="words_5", tag="grouped_2", bufs=1, align_bytes=64)
+        words = tile([P, 2, 2, P], F32, name="words_5", tag="grouped_2", bufs=1)
         for c in range(2):
             tiles["flow_words", 5, c] = words[:, c, :, :]
             nc.gpsimd.tensor_scalar(
@@ -576,7 +589,7 @@ def tile_cross_impact_hedge_s8_kernel(
             if s == 2:
                 widen(7)
             if s == 11:
-                words = work.tile([P, T_PASSES, 2, P], F32, name="sched_words", tag="raw", bufs=6, align_bytes=64)
+                words = tile([P, T_PASSES, 2, P], F32, name="sched_words", tag="raw", bufs=6)
                 for c in range(T_PASSES):
                     tiles["sched_words", 1, c] = words[:, c, :, :]
                 sort_words(words[:], sched_sb[1][:])

@@ -34,7 +34,6 @@ BANK = 512
 CHUNK = 256
 SIZES = {F32: 4, U32: 4, BF16: 2, U8: 1}
 LINE_ROUND = 256
-SKEW = {"ident": 128, "imp_scales": 128, "wm_scales": 128, "w_words": 64, "w_scales": 192, "flow_codes": 64, "flow_scales": 192, "sch_codes": 64, "sch_scales": 192}
 SCALAR, VECTOR, GPSIMD = "scalar", "vector", "gpsimd"
 
 SHARED_STEPS = (4, 6, 8, 10)
@@ -56,10 +55,10 @@ def tile_cross_impact_hedge_s8_kernel(
         def tile(shape, dtype, name, tag=None, bufs=1, room=None):
             tag = tag or name
             if tag not in places:
-                size = room or math.prod(shape[1:]) * SIZES[dtype]
-                places[tag] = -(-places["end"] // LINE_ROUND) * LINE_ROUND + SKEW.get(tag, 0)
+                size = -(-(room or math.prod(shape[1:]) * SIZES[dtype]) // LINE_ROUND) * LINE_ROUND
+                places[tag] = -(-places["end"] // LINE_ROUND) * LINE_ROUND
                 places["end"] = places[tag] + bufs * size
-            return sbuf.tile(shape, dtype, name=name, tag=tag, bufs=bufs, align_bytes=64, offset=places[tag])
+            return sbuf.tile(shape, dtype, name=name, tag=tag, bufs=bufs, align_bytes=LINE_ROUND, offset=places[tag])
 
         w_scales = tile([P, N_PASSES, R], U8, name="w_scales")
         nc.vector.memset(w_scales[:].bitcast(I32), 0)

@@ -651,14 +651,17 @@ def tile_cross_impact_hedge_s8_kernel(
         weighted_quantize(15)
         cost_matmul(0, 0, range(last), "z_0")
         cost_matmul(1, 0, range(last), "z_1")
+        cost_matmul(0, 1, range(1))
         cost_matmul(0, 0, [last])
         cost_matmul(1, 0, [last])
         hedge_matmul(14, None)
         hedge_matmul(15)
-        cost_matmul(0, 1, range(T_PASSES))
-        cost_matmul(1, 1, range(T_PASSES))
+        cost_matmul(0, 1, range(1, last))
+        cost_matmul(1, 1, range(1))
+        cost_matmul(0, 1, [last])
+        cost_matmul(1, 1, range(1, T_PASSES))
         cost_store(0, 0, SCALAR)
-        cost_store(1, 0, VECTOR)
+        cost_store(1, 0, SCALAR)
         hedge_store(14, SCALAR)
         hedge_store(15, VECTOR)
         cost_store(0, 1, SCALAR)

@@ -424,8 +424,8 @@ def tile_cross_impact_hedge_s8_kernel(
         load_flow(3, 1)
         load_impact(0, 1)
         load_impact(1, 1)
-        load_sched(0)
         load_impact(2, 1)
+        load_sched(0)
         load_flow(4, 2)
         nc.sync.dma_start(out=vol_bf[:], in_=vol.rearrange("(g p j) -> p g j", p=P, j=PACK))
         load_flow(6, 2)
@@ -468,17 +468,18 @@ def tile_cross_impact_hedge_s8_kernel(
         impact_group(2, 1, SCALAR, 0, CHUNK, slot=1)
         flow_transpose(3, 0, 2)
         flow_transpose(3, 2, 3)
-        sched_transpose(0, "hedge")
         impact_matmul(1, 0, "z_1")
+        sched_transpose(0, "hedge")
         sched_transpose(1)
-        impact_group(2, 1, SCALAR, CHUNK, BANK)
         saturate(1, 0)
+        impact_group(2, 1, SCALAR, CHUNK, BANK)
         for i in (2, 3):
             flow_scale_out(i, 0, 2)
             flow_scale_out(i, 2, 3)
         widen(4)
         widen(5)
         moves_transpose(0, 0)
+        moves_transpose(1, 0)
         flow_quantize(2)
         flow_quantize(3)
         for c in range(A_PASSES):
@@ -516,8 +517,6 @@ def tile_cross_impact_hedge_s8_kernel(
                 weigh_chunk(s - 3)
             if shared:
                 moves_transpose(first, moved_half)
-            if s == 2:
-                moves_transpose(second, moved_half)
             flow_transpose(ahead, 0, 2)
             if half == 0:
                 last_transpose(q + 1)
@@ -583,6 +582,8 @@ def tile_cross_impact_hedge_s8_kernel(
                 widen(s + 6)
             if s in (5, 11):
                 flow_sort(s + 4, 0, 2)
+            if s == 9:
+                flow_sort(13, 0, 1)
             if s == 10:
                 flow_sort(15, 2, 3)
             if s == 2:

import math
from contextlib import ExitStack

import concourse.mybir as mybir
from concourse.masks import make_identity

T, A, N, R, Q = 2048, 1536, 1024, 512, 256

F32 = mybir.dt.float32
BF16 = mybir.dt.bfloat16
U8 = mybir.dt.uint8
U32 = mybir.dt.uint32
I32 = mybir.dt.int32
FP8 = mybir.dt.float8_e4m3fn
FP8X4 = mybir.dt.float8_e4m3fn_x4
FP4X4 = mybir.dt.float4_e2m1fn_x4
MULT = mybir.AluOpType.mult
ADD = mybir.AluOpType.add
TANH = mybir.ActivationFunctionType.Tanh
COPY = mybir.ActivationFunctionType.Copy

FLOPS = 2 * T * A * N + 2 * T * N * R + 2 * Q * T * N

P = 128
PACK = 4
K_PASS = P * PACK
A_PASSES = A // K_PASS
N_PASSES = N // K_PASS
T_PASSES = T // K_PASS
TILES = T // P
PAIRS = TILES // 2
STEPS = PAIRS * N_PASSES
BANK = 512
CHUNK = 256
SIZES = {F32: 4, U32: 4, BF16: 2, U8: 1}
LINE_ROUND = 256
SCALAR, VECTOR, GPSIMD = "scalar", "vector", "gpsimd"

SHARED_STEPS = (4, 6, 8, 10)
ORDER = [(0, 0), (1, 0), (0, 1), (1, 1)] + [divmod(s, 2) for s in range(4, STEPS)]
TURN_BANKS = 5


def tile_cross_impact_hedge_s8_kernel(
    tc, flow_bytes, flow_scale, impact, vol, depth, sched, sens_words, sens_scales, hedge, cost
):
    nc = tc.nc
    with ExitStack() as ctx:
        sbuf = ctx.enter_context(tc.tile_pool(name="sbuf", bufs=1))
        psum = ctx.enter_context(tc.psum_pool(name="psum", bufs=1))
        ctx.enter_context(tc.manual_schedule())

        places = {"end": 0}

        def tile(shape, dtype, name, tag=None, bufs=1, room=None):
            tag = tag or name
            if tag not in places:
                size = -(-(room or math.prod(shape[1:]) * SIZES[dtype]) // LINE_ROUND) * LINE_ROUND
                places[tag] = -(-places["end"] // LINE_ROUND) * LINE_ROUND
                places["end"] = places[tag] + bufs * size
            return sbuf.tile(shape, dtype, name=name, tag=tag, bufs=bufs, align_bytes=LINE_ROUND, offset=places[tag])

        w_scales = tile([P, N_PASSES, R], U8, name="w_scales")
        nc.vector.memset(w_scales[:].bitcast(I32), 0)
        ident = tile([P, P], F32, name="ident")
        make_identity(nc, ident[:])

        flow_view = flow_bytes.rearrange("(g p j) a -> g p j a", p=P, j=PACK)
        flow_sb = {}

        def load_flow(first, count):
            g, j = divmod(first, PACK)
            rows = tile([P, count, A], U8, name=f"flow_{first}")
            for r in range(count):
                flow_sb[first + r] = rows[:, r, :]
            nc.sync.dma_start(out=rows[:], in_=flow_view[g, :, j : j + count, :])

        imp_view = impact.rearrange("(c p t) n -> c p t n", p=P, t=PACK)
        imp_raw = {}

        def load_impact(c, half):
            rows = tile([P, PACK, BANK], BF16, name=f"imp_raw_{c}_{half}", tag="raw", bufs=6)
            imp_raw[c, half] = rows
            nc.sync.dma_start(out=rows[:], in_=imp_view[c, :, :, half * BANK : (half + 1) * BANK])

        scale_sb = tile([P, A_PASSES, PACK], F32, name="scale_sb")
        vol_f32 = tile([P, N_PASSES, PACK], F32, name="vol_f32")
        vol_bf = tile([P, N_PASSES, PACK], BF16, name="vol_bf")
        depth_bf = tile([P, T_PASSES, PACK], BF16, name="depth_bf")
        depth_f32 = tile([P, T_PASSES, PACK], F32, name="depth_f32")
        w_words = tile([P, N_PASSES, 2 * R], U8, name="w_words")
        sched_sb = {}

        def load_sens():
            for quad in range(4):
                nc.sync.dma_start(
                    out=w_scales[32 * quad : 32 * quad + 4, :, :].bitcast(I32),
                    in_=sens_scales[:, 4 * quad : 4 * quad + 4, :].rearrange("g r n -> r g n").bitcast(I32),
                )
            nc.sync.dma_start(out=w_words[:].bitcast(I32), in_=sens_words.rearrange("g p b -> p g b").bitcast(I32))

        def load_sched(qt):
            rows = tile([P, T], BF16, name=f"sched_{qt}")
            sched_sb[qt] = rows
            nc.sync.dma_start(out=rows[:], in_=sched[qt * P : (qt + 1) * P, :])

        imp_codes = tile([P, A_PASSES * N], U32, name="imp_codes")
        imp_scales = tile([P, A_PASSES * N], U8, name="imp_scales")
        sch_codes = tile([P, (Q // P) * T_PASSES * P], U32, name="sch_codes")
        sch_scales = tile([P, (Q // P) * T_PASSES * P], U8, name="sch_scales")
        wm_codes = tile([P, STEPS * 2 * CHUNK], U32, name="wm_codes")
        wm_scales = tile([P, STEPS * 2 * CHUNK], U8, name="wm_scales")
        stage = tile([P, 6 * CHUNK * PACK], BF16, name="stage")
        tiles = {}
        free_banks = [f"turn_{b}" for b in range(TURN_BANKS)]

        def take_bank(key, shape, name, tag=None, dtype=F32):
            tag = tag or free_banks.pop(0)
            bank = psum.tile(shape, dtype, name=name, tag=tag, bufs=1)
            tiles[key] = (bank, tag)
            return bank

        def leave_bank(key):
            bank, tag = tiles.pop(key)
            if tag.startswith("turn"):
                free_banks.append(tag)
            return bank

        def move(engine, out, in_):
            if engine == SCALAR:
                nc.scalar.copy(out=out, in_=in_)
            else:
                nc.vector.tensor_copy(out=out, in_=in_)

        def interleave(engine, grouped, planes):
            if engine == GPSIMD:
                nc.gpsimd.tensor_scalar(
                    out=grouped, in0=planes.rearrange("p t n -> p n t"), scalar1=1.0, scalar2=0.0, op0=MULT, op1=ADD
                )
            else:
                move(engine, grouped.rearrange("p (n i) t -> p n t i", i=4), planes.rearrange("p t (n i) -> p n t i", i=4))

        def quantize(codes, scales, grouped):
            nc.vector.quantize_mx(out=codes.bitcast(FP8X4), scales=scales, in_=grouped)

        def multiply(out, stationary, moving, first, final, moving_dtype=FP8X4):
            nc.tensor.matmul_mx(
                out=out,
                lhsT=stationary[0].bitcast(FP8X4),
                lhsT_scale=stationary[1],
                rhs=moving[0].bitcast(moving_dtype),
                rhs_scale=moving[1],
                start=first,
                stop=final,
            )

        def impact_group(c, half, engine, lo=0, hi=BANK, slot=None):
            if ("impact", c, half) not in tiles:
                tag = f"grouped_{c if slot is None else slot}"
                grouped = tile([P, BANK * PACK], BF16, name=f"ig_{c}_{half}", tag=tag, bufs=1)
                tiles["impact", c, half] = grouped
            grouped = tiles["impact", c, half][:, lo * PACK : hi * PACK].rearrange("p (n t) -> p n t", t=PACK)
            interleave(engine, grouped, imp_raw[c, half][:, :, lo:hi])

        def impact_quantize(c, half, lo=0, hi=BANK):
            cols = slice(c * N + half * BANK + lo, c * N + half * BANK + hi)
            quantize(imp_codes[:, cols], imp_scales[:, cols], tiles["impact", c, half][:, lo * PACK : hi * PACK])

        def widen(i, engine=SCALAR, lo=0, hi=A, table=False):
            if ("wide", i) not in tiles:
                wide = tile([P, A], BF16, name=f"wide_{i}", tag="wide", bufs=4)
                tiles["wide", i] = wide
            codes = flow_sb[i][:, lo:hi].bitcast(FP8)
            if table:
                nc.scalar.activation(out=tiles["wide", i][:, lo:hi], in_=codes, func=COPY)
            else:
                move(engine, tiles["wide", i][:, lo:hi], codes)

        def sort_words(out, rows):
            nc.scalar.copy(out=out, in_=rows.bitcast(F32).rearrange("p (c m u) -> p c u m", m=P, u=2))

        def words_of(key, rows, c, u):
            if key + (c,) in tiles:
                return tiles[key + (c,)][:, u, :]
            return rows.bitcast(F32)[:, 2 * P * c + u : 2 * P * (c + 1) : 2]

        def flow_sort(i, lo, hi):
            words = tile([P, hi - lo, 2, P], F32, name=f"words_{i}_{lo}", tag="words", bufs=3, room=A * 2)
            for c in range(lo, hi):
                tiles["flow_words", i, c] = words[:, c - lo, :, :]
            sort_words(words[:], tiles["wide", i][:, lo * K_PASS : hi * K_PASS])

        def flow_transpose(i, lo, hi, tag=None):
            bank = take_bank(("turned_flow", i, lo), [P, 2, hi - lo, P], f"xt_{i}_{lo}", tag)
            for c in range(lo, hi):
                for u in range(2):
                    nc.tensor.transpose(bank[:, u, c - lo, :], words_of(("flow_words", i), tiles["wide", i][:], c, u), ident[:])

        def flow_scale_out(i, lo, hi):
            if ("flow", i) not in tiles:
                grouped = tile([P, A], BF16, name=f"fg_{i}", tag="flow", bufs=3)
                tiles["flow", i] = grouped
            n = hi - lo
            values = leave_bank(("turned_flow", i, lo))[:].rearrange("p u c m -> p (u c m)").bitcast(BF16)
            scales = scale_sb[:, lo:hi, :].rearrange("p c (u e) -> p c u e", u=2)
            nc.vector.tensor_tensor(
                out=tiles["flow", i][:, lo * K_PASS : hi * K_PASS].rearrange("p (c m u e) -> p c m u e", c=n, u=2, e=2),
                in0=values.rearrange("p (u c m e) -> p c m u e", u=2, c=n, e=2),
                in1=scales.unsqueeze(2).to_broadcast([P, n, P, 2, 2]),
                op=MULT,
            )

        def last_transpose(q):
            bank = take_bank(("turned_last", q), [P, 2, 2, P], f"xl_{q}")
            for r in range(2):
                i = 2 * q + r
                for u in range(2):
                    nc.tensor.transpose(bank[:, u, r, :], words_of(("flow_words", i), tiles["wide", i][:], 2, u), ident[:])

        def last_scale_out(i, lo=0, hi=P):
            q, r = divmod(i, 2)
            if ("flow", i) not in tiles:
                grouped = tile([P, A], BF16, name=f"fg_{i}", tag="flow", bufs=3)
                tiles["flow", i] = grouped
            bank = leave_bank(("turned_last", q)) if (r, hi) == (1, P) else tiles["turned_last", q][0]
            values = bank[:].rearrange("p u r m -> p (u r m)").bitcast(BF16).rearrange("p (u m e) -> p m u e", u=2, e=2)
            scales = scale_sb[:, 2, :].rearrange("p (u e) -> p u e", u=2)
            out = tiles["flow", i][:, 2 * K_PASS + lo * PACK : 2 * K_PASS + hi * PACK]
            nc.vector.tensor_tensor(
                out=out.rearrange("p (m u e) -> p m u e", u=2, e=2),
                in0=values[:, r * P + lo : r * P + hi, :, :],
                in1=scales.unsqueeze(1).to_broadcast([P, hi - lo, 2, 2]),
                op=MULT,
            )

        def flow_quantize(i):
            codes = tile([P, A_PASSES * P], U32, name=f"fc_{i}", tag="flow_codes", bufs=5)
            scales = tile([P, A_PASSES * P], U8, name=f"fs_{i}", tag="flow_scales", bufs=5)
            tiles["flow_codes", i] = (codes, scales)
            quantize(codes[:], scales[:], tiles.pop(("flow", i))[:])

        def impact_matmul(i, half, tag):
            z = take_bank(("z", i, half), [P, BANK], f"z_{i}_{half}", tag)
            codes, scales = tiles["flow_codes", i]
            for c in range(A_PASSES):
                rows = slice(c * P, (c + 1) * P)
                cols = slice(c * N + half * BANK, c * N + (half + 1) * BANK)
                moving = (imp_codes[:, cols], imp_scales[:, cols])
                multiply(z[:], (codes[:, rows], scales[:, rows]), moving, c == 0, c == A_PASSES - 1)

        def saturate(i, half):
            g, j = divmod(i, PACK)
            if j == 0:
                h = tile([P, PACK, BANK], F32, name=f"h_{g}_{half}", tag="h", bufs=4)
                tiles["h", g, half] = h
            nc.scalar.activation(
                out=tiles["h", g, half][:, j, :].rearrange("p (t m) -> p t m", t=PACK),
                in_=leave_bank(("z", i, half))[:].rearrange("p (m t) -> p t m", t=PACK),
                func=TANH,
            )

        STAGE = CHUNK * PACK

        def weigh_chunk(k):
            g, chunk = divmod(k, PACK)
            half, lo = chunk // 2, (0, 1, 1, 0)[chunk] * CHUNK
            nc.gpsimd.tensor_tensor(
                out=weighted_stage(k).rearrange("p (n j) -> p n j", j=PACK),
                in0=tiles["h", g, half][:, :, lo : lo + CHUNK].rearrange("p j n -> p n j"),
                in1=depth_f32[:, g, :].unsqueeze(1).to_broadcast([P, CHUNK, PACK]),
                op=MULT,
            )

        def weigh_plane(g, half, j, lo=0, hi=BANK, engine=SCALAR):
            if ("planes", g, half) not in tiles:
                planes = tile([P, PACK, BANK], BF16, name=f"planes_{g}_{half}", tag="raw", bufs=6)
                tiles["planes", g, half] = planes
            out, in_ = tiles["planes", g, half][:, j, lo:hi], tiles["h", g, half][:, j, lo:hi]
            if engine == SCALAR:
                nc.scalar.activation(out=out, in_=in_, func=COPY, scale=depth_f32[:, g, j : j + 1])
            else:
                nc.vector.tensor_scalar(out=out, in0=in_, scalar1=depth_f32[:, g, j : j + 1], scalar2=None, op0=MULT)

        def weighted_group(k, engine):
            g, chunk = divmod(k, PACK)
            half, lo = chunk // 2, (0, 1, 1, 0)[chunk] * CHUNK
            grouped = tile([P, STAGE], BF16, name=f"wp_{k}", tag="late", bufs=3)
            tiles["weighted", k] = grouped
            interleave(engine, grouped[:].rearrange("p (n t) -> p n t", t=PACK), tiles["planes", g, half][:, :, lo : lo + CHUNK])

        def slot(k):
            return 2 * CHUNK * (k - k % 4 + (0, 1, 3, 2)[k % 4]), k % 4 in (0, 3)

        def weighted_cols(k):
            lo, moves_first = slot(k)
            lo = lo + CHUNK * moves_first
            return slice(lo, lo + CHUNK)

        def moves_cols(step):
            lo, moves_first = slot((step - 1) % STEPS)
            lo = lo + CHUNK * (not moves_first)
            return slice(lo, lo + CHUNK)

        def weighted_stage(k):
            lo = (1 + 3 * (k % 2 if k < 12 else 1)) * STAGE
            return stage[:, lo : lo + STAGE]

        def moves_stage(step):
            if step == 0:
                return weighted_stage(0)
            lo = (0, 5, 2, 3)[(step - 1) % 4] * STAGE
            return stage[:, lo : lo + STAGE]

        def weighted_quantize(k):
            grouped = tiles.pop(("weighted", k))[:] if ("weighted", k) in tiles else weighted_stage(k)
            quantize(wm_codes[:, weighted_cols(k)], wm_scales[:, weighted_cols(k)], grouped)

        def moves_quantize(step):
            quantize(wm_codes[:, moves_cols(step)], wm_scales[:, moves_cols(step)], moves_stage(step))

        def both_quantize(k):
            cols = slice(slot(k)[0], slot(k)[0] + 2 * CHUNK)
            lo = (0, 4, 1, 3)[k % 4] * STAGE
            quantize(wm_codes[:, cols], wm_scales[:, cols], stage[:, lo : lo + 2 * STAGE])

        def moves_transpose(i, half, tag=None):
            g, j = divmod(i, PACK)
            bank = take_bank(("turned_h", i, half), [P, PACK, P], f"ht_{i}_{half}", tag)
            for t in range(PACK):
                nc.tensor.transpose(bank[:, t, :], tiles["h", g, half][:, j, t * P : (t + 1) * P], ident[:])

        def moves_scale(i, half):
            q, r = divmod(i, 2)
            nc.vector.tensor_tensor(
                out=moves_stage(ORDER.index((q, half)))[:, r * K_PASS : (r + 1) * K_PASS].rearrange("p (m t) -> p m t", t=PACK),
                in0=leave_bank(("turned_h", i, half))[:].rearrange("p t m -> p m t"),
                in1=vol_bf[:, half, :].unsqueeze(1).to_broadcast([P, P, PACK]),
                op=MULT,
            )

        def moves_planes(i, half):
            planes = tile([P, PACK, P], BF16, name=f"mp_{i}_{half}", tag="moves_planes", bufs=2)
            tiles["moves_planes", i, half] = planes
            bank = leave_bank(("turned_h", i, half))
            for t in range(PACK):
                nc.scalar.activation(out=planes[:, t, :], in_=bank[:, t, :], func=COPY, scale=vol_f32[:, half, t : t + 1])

        def moves_group(i, half):
            q, r = divmod(i, 2)
            grouped = moves_stage(ORDER.index((q, half)))[:, r * K_PASS : (r + 1) * K_PASS].rearrange("p (m t) -> p m t", t=PACK)
            interleave(SCALAR, grouped, tiles.pop(("moves_planes", i, half))[:])

        def hedge_matmul(i, tag="hedge"):
            q, r = divmod(i, 2)
            bank = take_bank(("hedge", i), [P, R], f"hg_{i}", tag)
            for half in range(N_PASSES):
                lo = moves_cols(ORDER.index((q, half))).start + r * P
                rows = slice(lo, lo + P)
                moving = (w_words[:, half, :], w_scales[:, half, :])
                multiply(bank[:], (wm_codes[:, rows], wm_scales[:, rows]), moving, half == 0, half == N_PASSES - 1, FP4X4)

        hedge_view = hedge.rearrange("(g p j) r -> g j p r", p=P, j=PACK)

        def hedge_store(i, engine=SCALAR):
            g, j = divmod(i, PACK)
            result = tile([P, R], F32, name=f"hr_{i}", tag="hedge_out", bufs=5)
            move(engine, result[:], leave_bank(("hedge", i))[:])
            nc.sync.dma_start(out=hedge_view[g, j], in_=result[:])


        def sched_stage(b):
            if b == 0:
                return weighted_stage(1)
            if ("sched", b // 2) not in tiles:
                grouped = tile([P, 2 * STAGE], BF16, name=f"sg_{b}", tag=f"grouped_{b // 2}", bufs=1)
                tiles["sched", b // 2] = grouped
            return tiles["sched", b // 2][:, STAGE * (b % 2) : STAGE * (b % 2 + 1)]

        def sched_transpose(b, tag=None):
            qt, two = divmod(b, 2)
            bank = take_bank(("turned_sched", b), [P, 2, 2, P], f"st_{b}", tag)
            for s in range(2):
                for u in range(2):
                    words = words_of(("sched_words", qt), sched_sb[qt][:], 2 * two + s, u)
                    nc.tensor.transpose(bank[:, s, u, :], words, ident[:])

        def sched_group(b, engine=SCALAR):
            words = sched_stage(b).bitcast(F32)
            bank = leave_bank(("turned_sched", b))
            move(engine, words.rearrange("p (s q u) -> p s q u", s=2, u=2), bank[:].rearrange("p s u q -> p s q u"))

        def sched_quantize(b, parts=1):
            cols = slice(b * 2 * P, (b + parts) * 2 * P)
            grouped = sched_stage(b) if parts == 1 else tiles["sched", b // 2][:]
            quantize(sch_codes[:, cols], sch_scales[:, cols], grouped)

        def cost_matmul(qt, half, passes, tag=None):
            if passes[0] == 0:
                take_bank(("cost", qt, half), [P, BANK], f"cost_{qt}_{half}", tag)
            bank = tiles["cost", qt, half][0]
            for g in passes:
                rows = slice((qt * T_PASSES + g) * P, (qt * T_PASSES + g + 1) * P)
                lo = weighted_cols(PACK * g + 3 * half).start
                moving = (wm_codes[:, lo : lo + BANK], wm_scales[:, lo : lo + BANK])
                multiply(bank[:], (sch_codes[:, rows], sch_scales[:, rows]), moving, g == 0, g == T_PASSES - 1)

        def cost_store(qt, half, engine, pieces=1):
            bank = leave_bank(("cost", qt, half))
            width = BANK // pieces
            for lo in range(0, BANK, width):
                result = tile([P, width], F32, name=f"cr_{qt}_{half}_{lo}", tag="raw", bufs=6)
                sums = bank[:].rearrange("p (t m) -> p m t", t=PACK)[:, lo // PACK : (lo + width) // PACK, :]
                move(engine, result[:].rearrange("p (m t) -> p m t", t=PACK), sums)
                col = half * BANK + lo
                nc.sync.dma_start(out=cost[qt * P : (qt + 1) * P, col : col + width], in_=result[:])

        nc.scalar.dma_start(out=scale_sb[:], in_=flow_scale.rearrange("o (c p t) -> p (o c) t", p=P, t=PACK))
        load_flow(0, 1)
        load_flow(1, 1)
        load_impact(0, 0)
        load_impact(1, 0)
        load_flow(2, 1)
        load_impact(2, 0)
        load_flow(3, 1)
        load_impact(0, 1)
        load_impact(1, 1)
        load_impact(2, 1)
        load_sched(0)
        load_flow(4, 2)
        nc.sync.dma_start(out=vol_bf[:], in_=vol.rearrange("(g p j) -> p g j", p=P, j=PACK))
        load_flow(6, 2)
        nc.sync.dma_start(out=depth_bf[:], in_=depth.rearrange("(g p j) -> p g j", p=P, j=PACK))
        load_sens()
        for first in range(8, TILES, 2):
            load_flow(first, 2)
        load_sched(1)

        widen(0, VECTOR, 0, K_PASS)
        widen(0, SCALAR, K_PASS, 2 * K_PASS, table=True)
        widen(0, SCALAR, 2 * K_PASS, A)
        widen(1, VECTOR, 0, 2 * K_PASS)
        widen(1, SCALAR, 2 * K_PASS, A)
        for c in range(A_PASSES):
            flow_transpose(0, c, c + 1)
        flow_transpose(1, 0, 2)
        flow_transpose(1, 2, 3)
        for c in range(A_PASSES - 1):
            impact_group(c, 0, SCALAR, 0, CHUNK)
            impact_group(c, 0, GPSIMD, CHUNK, BANK)
        for c in range(A_PASSES):
            flow_scale_out(0, c, c + 1)
        flow_scale_out(1, 0, 2)
        flow_scale_out(1, 2, 3)
        widen(2)
        impact_group(2, 0, SCALAR, 0, CHUNK)
        impact_group(2, 0, VECTOR, CHUNK, BANK)
        widen(3)
        flow_transpose(2, 0, 2)
        flow_transpose(2, 2, 3)
        flow_quantize(0)
        for c in range(A_PASSES):
            impact_quantize(c, 0)
        flow_quantize(1)
        impact_group(0, 1, SCALAR, slot=0)
        impact_group(1, 1, GPSIMD, slot=2)
        impact_matmul(0, 0, "z_0")
        saturate(0, 0)
        impact_group(2, 1, SCALAR, 0, CHUNK, slot=1)
        flow_transpose(3, 0, 2)
        flow_transpose(3, 2, 3)
        impact_matmul(1, 0, "z_1")
        sched_transpose(0, "hedge")
        sched_transpose(1)
        saturate(1, 0)
        impact_group(2, 1, SCALAR, CHUNK, BANK)
        for i in (2, 3):
            flow_scale_out(i, 0, 2)
            flow_scale_out(i, 2, 3)
        widen(4)
        widen(5)
        moves_transpose(0, 0)
        moves_transpose(1, 0)
        flow_quantize(2)
        flow_quantize(3)
        for c in range(A_PASSES):
            impact_quantize(c, 1)
        words = tile([P, 2, 2, P], F32, name="words_5", tag="grouped_2", bufs=1)
        for c in range(2):
            tiles["flow_words", 5, c] = words[:, c, :, :]
            nc.gpsimd.tensor_scalar(
                out=words[:, c, :, :].rearrange("p u m -> p (u m)").bitcast(BF16).rearrange("p (u m e) -> p u m e", u=2, e=2),
                in0=tiles["wide", 5][:, c * K_PASS : (c + 1) * K_PASS].rearrange("p (m u e) -> p u m e", u=2, e=2),
                scalar1=1.0,
                scalar2=0.0,
                op0=MULT,
                op1=ADD,
            )
        for i in (2, 3):
            impact_matmul(i, 0, f"z_{i % 2}")
            saturate(i, 0)
        widen(6)
        nc.scalar.copy(out=depth_f32[:], in_=depth_bf[:])
        nc.scalar.copy(out=vol_f32[:], in_=vol_bf[:])
        sched_group(0)

        last = T_PASSES - 1
        for s in range(2, STEPS - 2):
            pair, part = ORDER[s]
            q, half = divmod(s, 2)
            ahead = s + 2
            moved_pair, moved_half = ORDER[s - 2]
            first, second = 2 * moved_pair, 2 * moved_pair + 1
            shared = s in SHARED_STEPS
            cut = P // 2 if s - half in SHARED_STEPS else 0

            if s >= 3:
                weigh_chunk(s - 3)
            if shared:
                moves_transpose(first, moved_half)
            flow_transpose(ahead, 0, 2)
            if half == 0:
                last_transpose(q + 1)
            if s == 13:
                sched_transpose(2)
            if s > 2:
                if not shared:
                    moves_transpose(first, moved_half)
                moves_transpose(second, moved_half, "hedge" if s == 6 else None)

            if shared:
                moves_planes(first, moved_half)
            if s == 3:
                flow_scale_out(ahead, 0, 2)
            if s == 2:
                moves_scale(first, moved_half)
            moves_scale(second, moved_half)
            if not shared and s > 2:
                moves_scale(first, moved_half)
            if s != 3:
                flow_scale_out(ahead, 0, 2)
            if half == 0:
                last_scale_out(ahead)
                if cut:
                    last_scale_out(ahead + 1, 0, cut)
            else:
                last_scale_out(ahead, cut, P)
            if s > 3:
                both_quantize(s - 4)
            elif s == 3:
                sched_quantize(0)
            else:
                moves_quantize(0)
            flow_quantize(ahead)

            if s == 2:
                sched_group(1, VECTOR)
            if s == 13:
                sched_group(2)
            impact_matmul(2 * pair, part, "z_0")
            saturate(2 * pair, part)
            if s == 6:
                hedge_matmul(0, None)
            if s > 6:
                hedge_matmul(s - 5)
            if s >= 6:
                hedge_store(s - 5 if s > 6 else 0)
            impact_matmul(2 * pair + 1, part, "z_1")
            if s == 6:
                hedge_matmul(1)
            if half == 1 and s + 5 < TILES and s < 6:
                widen(s + 5)
            saturate(2 * pair + 1, part)
            if s == 6:
                hedge_store(1)
            if half == 1 and s + 5 < TILES and s >= 6:
                widen(s + 5)
            if half == 0 and s + 4 < TILES:
                flow_sort(s + 4, 0, A_PASSES if s >= 10 else 2)
            if shared:
                moves_group(first, moved_half)
            if half == 1 and s + 6 < TILES:
                widen(s + 6)
            if s in (5, 11):
                flow_sort(s + 4, 0, 2)
            if s == 9:
                flow_sort(13, 0, 1)
            if s == 10:
                flow_sort(15, 2, 3)
            if s == 2:
                widen(7)
            if s == 11:
                words = tile([P, T_PASSES, 2, P], F32, name="sched_words", tag="raw", bufs=6)
                for c in range(T_PASSES):
                    tiles["sched_words", 1, c] = words[:, c, :, :]
                sort_words(words[:], sched_sb[1][:])
            if 2 * q >= PACK * last:
                for j in range(2):
                    weigh_plane(last, half, j, 0 if half else CHUNK)

        final = (TILES - 2, TILES - 1)
        weigh_chunk(11)
        impact_matmul(14, 0, "z_0")
        for half in range(N_PASSES):
            for i in (12, 13):
                moves_transpose(i, half)
        for half in range(N_PASSES):
            for i in (12, 13):
                moves_scale(i, half)
        impact_matmul(14, 1, "z_1")
        impact_matmul(15, 0, None)
        impact_matmul(15, 1, None)
        hedge_matmul(9)
        saturate(14, 0)
        saturate(14, 1)
        weigh_plane(last, 0, 2, CHUNK)
        saturate(15, 0)
        saturate(15, 1)
        both_quantize(10)
        moves_quantize(13)
        sched_quantize(2)
        both_quantize(11)
        weigh_chunk(12)
        sched_quantize(1)
        sched_transpose(3)
        moves_transpose(14, 0, "z_0")
        moves_transpose(14, 1, "z_1")
        moves_transpose(15, 0)
        moves_transpose(15, 1)
        hedge_store(9)
        weigh_plane(last, 0, 3, CHUNK)
        sched_group(3)
        for i in final:
            for half in range(N_PASSES):
                moves_scale(i, half)
        hedge_matmul(10, None)
        hedge_matmul(11, None)
        hedge_matmul(12)
        hedge_matmul(13, None)
        weighted_group(13, SCALAR)
        weigh_plane(last, 1, 2)
        weigh_plane(last, 1, 3)
        for i in (10, 11, 12, 13):
            hedge_store(i)
        sched_quantize(3)
        moves_quantize(14)
        weighted_quantize(12)
        weighted_quantize(13)
        moves_quantize(15)
        weighted_group(14, VECTOR)
        weighted_group(15, VECTOR)
        weighted_quantize(14)
        weighted_quantize(15)
        cost_matmul(0, 0, range(last), "z_0")
        cost_matmul(1, 0, range(last), "z_1")
        cost_matmul(0, 1, range(1))
        cost_matmul(0, 0, [last])
        cost_matmul(1, 0, [last])
        hedge_matmul(14, None)
        hedge_matmul(15)
        cost_matmul(0, 1, range(1, last))
        cost_matmul(1, 1, range(1))
        cost_matmul(0, 1, [last])
        cost_matmul(1, 1, range(1, T_PASSES))
        cost_store(0, 0, SCALAR)
        cost_store(1, 0, SCALAR)
        hedge_store(14, SCALAR)
        hedge_store(15, VECTOR)
        cost_store(0, 1, SCALAR)
        cost_store(1, 1, VECTOR, pieces=2)
